import numpy as np
import ml_dtypes


def mxq(x, axis, fmt="e4m3"):
    dtype, down = {"e4m3": (ml_dtypes.float8_e4m3fn, 7), "e5m2": (ml_dtypes.float8_e5m2, 14)}[fmt]
    v = np.moveaxis(np.asarray(x, np.float32).astype(ml_dtypes.bfloat16).astype(np.float64), axis, -1)
    blocks = v.reshape(v.shape[:-1] + (-1, 32))
    amax = np.abs(blocks).max(-1, keepdims=True)
    byte = np.maximum(np.where(amax > 0, np.frexp(amax)[1] - 1 + 127, 0) - down, 1)
    scale = np.exp2(byte - 127.0)
    codes = (blocks / scale).astype(np.float32).astype(dtype).astype(np.float64)
    return np.moveaxis((codes * scale).reshape(v.shape), -1, axis)


WIDE = False


def mx_kscale(k):
    if not WIDE:
        return np.ones(k)
    levels = np.array([30, -30])
    if k % 512:
        return np.exp2(np.random.permutation(np.resize(levels, k // 32))).repeat(32)
    a = np.empty((k // 512, 16))
    for p in range(k // 512):
        a[p, :8] = np.random.permutation(np.resize(levels, 8))
        for g in range(8):
            far = levels[np.abs(levels - a[p, g]) >= 10]
            a[p, g + 8] = far[np.random.randint(len(far))]
    return np.exp2(a.ravel()).repeat(32)


def f64(x):
    return np.asarray(x).astype(np.float64)


def striped(idx):
    return np.tile(idx.reshape(-1, 16).T, (8, 1)).astype(np.uint16)


def unstriped(offs):
    return offs[:16].T.reshape(-1).astype(np.int64)


def d_relu2(v):
    return 2.0 * np.maximum(v, 0.0)


K, T, E, C, H, N = 384, 2048, 4, 512, 1024, 512


def by_expert(wq, xq):
    return np.concatenate([wq[e].T @ xq[:, e * C:(e + 1) * C] for e in range(E)], axis=1)


def setup_inputs():
    n = np.random.standard_normal
    s = mx_kscale(N)[:, None]
    u = mx_kscale(H)
    return {
        "dyT": (n((N, T)) * s).astype(np.float32),
        "a": n((H, E * C)).astype(np.float32),
        "w2": (n((E, N, H)) / np.sqrt(N) / s[None] * u[None, None, :]).astype(np.float32),
        "w1": (n((E, H, K)) / np.sqrt(H) / u[None, :, None]).astype(np.float32),
        "gate": np.tile(np.random.uniform(0.2, 1.0, E * C), (N, 1)).astype(np.float32),
        "offs": striped(np.random.permutation(T)[:E * C]),
    }


def reference(dyT, a, w2, w1, gate, offs):
    idx = unstriped(offs)
    gq = mxq(f64(gate) * f64(dyT)[:, idx], 0, "e5m2")
    dh = by_expert(mxq(f64(w2), 1, "e4m3"), gq)
    da = dh * d_relu2(f64(a))
    dx = by_expert(mxq(f64(w1), 1, "e4m3"), mxq(da, 0, "e5m2"))
    out = np.zeros((K, T))
    out[:, idx] = dx
    return out

@@ -1,0 +1,247 @@
+from contextlib import ExitStack
+
+import concourse.mybir as mybir
+
+K, T, E, C, H, N = 384, 2048, 4, 512, 1024, 512
+P = 128
+J = 4
+HALVES = H // (P * J)
+K_TILES = K // P
+FLOPS = 2 * E * C * (N * H + H * K)
+BYTES = 4 * (N * T + H * E * C + E * N * H + E * H * K + E * C + K * T) + 2 * P * (E * C // 16)
+
+F32 = mybir.dt.float32
+BF16 = mybir.dt.bfloat16
+U32 = mybir.dt.uint32
+U16 = mybir.dt.uint16
+U8 = mybir.dt.uint8
+E4M3 = mybir.dt.float8_e4m3fn_x4
+E5M2 = mybir.dt.float8_e5m2_x4
+MULT = mybir.AluOpType.mult
+MAX = mybir.AluOpType.max
+COPY = mybir.ActivationFunctionType.Copy
+
+
+def tile_moe_bdx_mlp_relu2_kernel(tc, dyT, a, w2, w1, gate, offs, out):
+    nc = tc.nc
+    with ExitStack() as ctx:
+        held = ctx.enter_context(tc.tile_pool(name="held", bufs=1))
+        work = ctx.enter_context(tc.tile_pool(name="work", bufs=2))
+        psum = ctx.enter_context(tc.psum_pool(name="psum", bufs=1))
+
+        offsets = held.tile([P, E * C // 16], U16, name="offsets")
+        nc.sync.dma_start(offsets[:], offs)
+        gates = [held.tile([P, C], F32, name=f"gate{e}") for e in range(E)]
+        tokens = [held.tile([P, T], F32, name=f"tokens{t}") for t in range(J)]
+        windows = [held.tile([P, T], F32, name=f"window{k}") for k in range(K_TILES)]
+
+        dy_rows = dyT.rearrange("(p t) s -> p t s", t=J)
+        a_rows = a.rearrange("(h p t) s -> h p t s", p=P, t=J)
+        w2_raw, a_raw, w1_raw, gathered, g_mx, w2_mx, w1_mx, da_mx, dx_banks, results = {}, {}, {}, {}, {}, {}, {}, {}, {}, {}
+
+        def listed(e):
+            return offsets[:, e * C // 16 : (e + 1) * C // 16]
+
+        def load_tokens(t):
+            nc.sync.dma_start(tokens[t][:], dy_rows[:, t, :])
+
+        def load_gate(e):
+            nc.sync.dma_start(gates[e][:], gate[0:P, e * C : (e + 1) * C])
+
+        def load_w2(e, h):
+            w2_raw[e, h] = work.tile([P, J, P * J], F32, name="w2_raw", bufs=3)
+            rows = w2[e].rearrange("(p j) i -> p j i", j=J)
+            nc.sync.dma_start(w2_raw[e, h][:], rows[:, :, h * P * J : (h + 1) * P * J])
+
+        def load_a(e, h):
+            a_raw[e, h] = work.tile([P, J, C], F32, name="a_raw", bufs=4)
+            nc.sync.dma_start(a_raw[e, h][:], a_rows[h][:, :, e * C : (e + 1) * C])
+
+        def load_w1(e, h):
+            w1_raw[e, h] = work.tile([P, J, K], F32, name="w1_raw", bufs=3)
+            nc.sync.dma_start(w1_raw[e, h][:], w1[e].rearrange("(h p j) k -> h p j k", p=P, j=J)[h])
+
+
+        def gather(e):
+            gathered[e] = work.tile([P, J, C], F32, name="gathered", bufs=2)
+            for t in range(J):
+                nc.vector.tensor_tensor(gathered[e][:, t, :], tokens[t][:].indirect(listed(e)), gates[e][:], MULT)
+
+        def quantize_g(e):
+            mixed = work.tile([P, C, J], BF16, name="g_mixed", align_bytes=64)
+            nc.scalar.activation(
+                mixed[:].rearrange("p (c i) t -> p c t i", i=4), gathered[e][:].rearrange("p t (c i) -> p c t i", i=4), COPY
+            )
+            codes = work.tile([P, C], U32, name="g_codes", bufs=3, align_bytes=64)
+            scales = work.tile([P, C], U8, name="g_scales", bufs=3, align_bytes=64)
+            nc.vector.quantize_mx(out=codes[:].bitcast(E5M2), scales=scales[:], in_=mixed[:].rearrange("p c t -> p (c t)"))
+            g_mx[e] = codes, scales
+
+        def quantize_w2(e):
+            codes = work.tile([P, H], U32, name="w2_codes", align_bytes=64)
+            scales = work.tile([P, H], U8, name="w2_scales", align_bytes=64)
+            for h in range(HALVES):
+                mixed = work.tile([P, J, P, J], BF16, name="w2_mixed", bufs=2, align_bytes=64)
+                nc.scalar.activation(
+                    mixed[:].rearrange("p t m j -> p m j t"), w2_raw[e, h][:].rearrange("p j (m t) -> p m j t", t=J), COPY
+                )
+                cols = slice(h * P * J, (h + 1) * P * J)
+                nc.vector.quantize_mx(
+                    out=codes[:, cols].bitcast(E4M3), scales=scales[:, cols], in_=mixed[:].rearrange("p t m j -> p (t m j)")
+                )
+            w2_mx[e] = codes, scales
+
+        def quantize_w1(e):
+            mixed = work.tile([P, HALVES * K, J], BF16, name="w1_mixed", bufs=2, align_bytes=64)
+            codes = work.tile([P, HALVES * K], U32, name="w1_codes", align_bytes=64)
+            scales = work.tile([P, HALVES * K], U8, name="w1_scales", align_bytes=64)
+            for h in range(HALVES):
+                nc.scalar.activation(
+                    mixed[:, h * K : (h + 1) * K, :].rearrange("p (c i) j -> p c j i", i=4),
+                    w1_raw[e, h][:].rearrange("p j (c i) -> p c j i", i=4),
+                    COPY,
+                )
+            for lo, hi in ((0, 512), (512, HALVES * K)):
+                nc.vector.quantize_mx(
+                    out=codes[:, lo:hi].bitcast(E4M3),
+                    scales=scales[:, lo:hi],
+                    in_=mixed[:, lo:hi, :].rearrange("p c j -> p (c j)"),
+                )
+            w1_mx[e] = codes, scales
+
+        def hidden_gradient(e, h):
+            w2_codes, w2_scales = w2_mx[e]
+            g_codes, g_scales = g_mx[e]
+            da = work.tile([P, J, C], BF16, name="da")
+            for t in range(J):
+                dh = psum.tile([P, C], F32, name="dh", bufs=5)
+                col = (h * J + t) * P
+                nc.tensor.matmul_mx(
+                    out=dh[:],
+                    lhsT=w2_codes[:, col : col + P].bitcast(E4M3),
+                    lhsT_scale=w2_scales[:, col : col + P],
+                    rhs=g_codes[:].bitcast(E5M2),
+                    rhs_scale=g_scales[:],
+                    start=True,
+                    stop=True,
+                )
+                nc.vector.scalar_tensor_tensor(da[:, t, :], a_raw[e, h][:, t, :], 0.0, dh[:], MAX, MULT)
+            mixed = work.tile([P, C, J], BF16, name="da_mixed", align_bytes=64)
+            nc.scalar.activation(mixed[:].rearrange("p (c i) t -> p c t i", i=8), da[:].rearrange("p t (c i) -> p c t i", i=8), COPY)
+            codes = work.tile([P, C], U32, name="da_codes", bufs=3, align_bytes=64)
+            scales = work.tile([P, C], U8, name="da_scales", bufs=3, align_bytes=64)
+            nc.vector.quantize_mx(out=codes[:].bitcast(E5M2), scales=scales[:], in_=mixed[:].rearrange("p c t -> p (c t)"))
+            da_mx[e, h] = codes, scales
+
+        def input_gradient(e):
+            w1_codes, w1_scales = w1_mx[e]
+            for k in range(K_TILES):
+                dx = psum.tile([P, C], F32, name="dx", bufs=3)
+                for h in range(HALVES):
+                    col = h * K + k * P
+                    da_codes, da_scales = da_mx[e, h]
+                    nc.tensor.matmul_mx(
+                        out=dx[:],
+                        lhsT=w1_codes[:, col : col + P].bitcast(E4M3),
+                        lhsT_scale=w1_scales[:, col : col + P],
+                        rhs=da_codes[:].bitcast(E5M2),
+                        rhs_scale=da_scales[:],
+                        start=(h == 0),
+                        stop=(h == HALVES - 1),
+                    )
+                dx_banks[e, k] = dx
+
+        def copy_out(e, k, h):
+            plane = a_raw[min(e + 1, E - 1), h][:, k, :]
+            nc.scalar.activation(plane, dx_banks[e, k][:], COPY, scale=2.0)
+            results[e, k] = plane
+
+        def scatter(e, k):
+            nc.vector.tensor_copy(windows[k][:].indirect(listed(e)), results[e, k])
+            if e == E - 1:
+                nc.sync.dma_start(out[k * P : (k + 1) * P, :], windows[k][:])
+
+        load_gate(0)
+        load_tokens(0)
+        load_gate(1)
+        load_tokens(1)
+        load_tokens(2)
+        load_tokens(3)
+        load_w2(0, 0)
+        load_w2(0, 1)
+        load_gate(2)
+        load_gate(3)
+        load_a(0, 0)
+        load_a(0, 1)
+        load_w1(0, 0)
+        load_w1(0, 1)
+        load_w2(1, 0)
+        load_w2(1, 1)
+        load_a(1, 0)
+        load_a(1, 1)
+        load_w1(1, 0)
+        load_w1(1, 1)
+        load_w2(2, 0)
+        load_w2(2, 1)
+        load_a(2, 0)
+        load_a(2, 1)
+        load_w1(2, 0)
+        load_w1(2, 1)
+        load_w2(3, 0)
+        load_w2(3, 1)
+        load_a(3, 0)
+        load_a(3, 1)
+        load_w1(3, 0)
+        load_w1(3, 1)
+        gather(0)
+        quantize_g(0)
+        gather(1)
+        quantize_w2(0)
+        hidden_gradient(0, 0)
+        quantize_w1(0)
+        quantize_g(1)
+        quantize_w2(1)
+        hidden_gradient(0, 1)
+        input_gradient(0)
+        gather(2)
+        hidden_gradient(1, 0)
+        copy_out(0, 2, 0)
+        copy_out(0, 0, 0)
+        quantize_w1(1)
+        quantize_g(2)
+        quantize_w2(2)
+        scatter(0, 0)
+        hidden_gradient(1, 1)
+        copy_out(0, 1, 0)
+        input_gradient(1)
+        gather(3)
+        hidden_gradient(2, 0)
+        copy_out(1, 2, 0)
+        copy_out(1, 0, 0)
+        quantize_w1(2)
+        quantize_g(3)
+        scatter(0, 1)
+        quantize_w2(3)
+        scatter(1, 0)
+        hidden_gradient(2, 1)
+        scatter(0, 2)
+        copy_out(1, 1, 0)
+        input_gradient(2)
+        hidden_gradient(3, 0)
+        copy_out(2, 2, 0)
+        copy_out(2, 0, 0)
+        quantize_w1(3)
+        scatter(1, 1)
+        scatter(2, 0)
+        hidden_gradient(3, 1)
+        scatter(1, 2)
+        copy_out(2, 1, 0)
+        input_gradient(3)
+        copy_out(3, 0, 1)
+        copy_out(3, 1, 1)
+        copy_out(3, 2, 1)
+        scatter(2, 1)
+        scatter(2, 2)
+        scatter(3, 0)
+        scatter(3, 1)
+        scatter(3, 2)

@@ -19,6 +19,8 @@ E4M3 = mybir.dt.float8_e4m3fn_x4
 E5M2 = mybir.dt.float8_e5m2_x4
 MULT = mybir.AluOpType.mult
 MAX = mybir.AluOpType.max
+MIN = mybir.AluOpType.min
+F32_MAX = 3.4028234663852886e38
 COPY = mybir.ActivationFunctionType.Copy
 
 
@@ -27,6 +29,7 @@ def tile_moe_bdx_mlp_relu2_kernel(tc, dyT, a, w2, w1, gate, offs, out):
     with ExitStack() as ctx:
         held = ctx.enter_context(tc.tile_pool(name="held", bufs=1))
         work = ctx.enter_context(tc.tile_pool(name="work", bufs=2))
+        shared = ctx.enter_context(tc.tile_pool(name="shared", bufs=1))
         psum = ctx.enter_context(tc.psum_pool(name="psum", bufs=1))
 
         offsets = held.tile([P, E * C // 16], U16, name="offsets")
@@ -38,6 +41,7 @@ def tile_moe_bdx_mlp_relu2_kernel(tc, dyT, a, w2, w1, gate, offs, out):
         dy_rows = dyT.rearrange("(p t) s -> p t s", t=J)
         a_rows = a.rearrange("(h p t) s -> h p t s", p=P, t=J)
         w2_raw, a_raw, w1_raw, gathered, g_mx, w2_mx, w1_mx, da_mx, dx_banks, results = {}, {}, {}, {}, {}, {}, {}, {}, {}, {}
+        da_planes, da_mixed, relu_a, dh_planes = {}, {}, {}, {}
 
         def listed(e):
             return offsets[:, e * C // 16 : (e + 1) * C // 16]
@@ -77,22 +81,25 @@ def tile_moe_bdx_mlp_relu2_kernel(tc, dyT, a, w2, w1, gate, offs, out):
             nc.vector.quantize_mx(out=codes[:].bitcast(E5M2), scales=scales[:], in_=mixed[:].rearrange("p c t -> p (c t)"))
             g_mx[e] = codes, scales
 
-        def quantize_w2(e):
-            codes = work.tile([P, H], U32, name="w2_codes", align_bytes=64)
-            scales = work.tile([P, H], U8, name="w2_scales", align_bytes=64)
-            for h in range(HALVES):
-                mixed = work.tile([P, J, P, J], BF16, name="w2_mixed", bufs=2, align_bytes=64)
-                nc.scalar.activation(
-                    mixed[:].rearrange("p t m j -> p m j t"), w2_raw[e, h][:].rearrange("p j (m t) -> p m j t", t=J), COPY
-                )
-                cols = slice(h * P * J, (h + 1) * P * J)
-                nc.vector.quantize_mx(
-                    out=codes[:, cols].bitcast(E4M3), scales=scales[:, cols], in_=mixed[:].rearrange("p t m j -> p (t m j)")
-                )
-            w2_mx[e] = codes, scales
+        def quantize_w2(e, h):
+            if h == 0:
+                codes = work.tile([P, H], U32, name="w2_codes", align_bytes=64)
+                scales = work.tile([P, H], U8, name="w2_scales", align_bytes=64)
+                w2_mx[e] = codes, scales
+                mixed = work.tile([P, J, P, J], BF16, name="w2_mixed", bufs=1, align_bytes=64)
+            else:
+                mixed = shared.tile([P, J, P, J], BF16, name="w2_mixed_late", align_bytes=64, offset=7680)
+            codes, scales = w2_mx[e]
+            nc.scalar.activation(
+                mixed[:].rearrange("p t m j -> p m j t"), w2_raw[e, h][:].rearrange("p j (m t) -> p m j t", t=J), COPY
+            )
+            cols = slice(h * P * J, (h + 1) * P * J)
+            nc.vector.quantize_mx(
+                out=codes[:, cols].bitcast(E4M3), scales=scales[:, cols], in_=mixed[:].rearrange("p t m j -> p (t m j)")
+            )
 
         def quantize_w1(e):
-            mixed = work.tile([P, HALVES * K, J], BF16, name="w1_mixed", bufs=2, align_bytes=64)
+            mixed = work.tile([P, HALVES * K, J], BF16, name="w1_mixed", bufs=1, align_bytes=64)
             codes = work.tile([P, HALVES * K], U32, name="w1_codes", align_bytes=64)
             scales = work.tile([P, HALVES * K], U8, name="w1_scales", align_bytes=64)
             for h in range(HALVES):
@@ -109,28 +116,58 @@ def tile_moe_bdx_mlp_relu2_kernel(tc, dyT, a, w2, w1, gate, offs, out):
                 )
             w1_mx[e] = codes, scales
 
-        def hidden_gradient(e, h):
+        def hidden_sums(e, h, t):
             w2_codes, w2_scales = w2_mx[e]
             g_codes, g_scales = g_mx[e]
-            da = work.tile([P, J, C], BF16, name="da")
+            dh = psum.tile([P, C], F32, name="dh", bufs=5)
+            col = (h * J + t) * P
+            nc.tensor.matmul_mx(
+                out=dh[:],
+                lhsT=w2_codes[:, col : col + P].bitcast(E4M3),
+                lhsT_scale=w2_scales[:, col : col + P],
+                rhs=g_codes[:].bitcast(E5M2),
+                rhs_scale=g_scales[:],
+                start=True,
+                stop=True,
+            )
+            return dh
+
+        def product_on_vector(e, h):
+            if h == 0:
+                da = shared.tile([P, J, C], BF16, name="da_planes", align_bytes=64, offset=8192)
+            else:
+                da = shared.tile([P, J, C], BF16, name="da_planes_first", align_bytes=64, offset=0)
             for t in range(J):
-                dh = psum.tile([P, C], F32, name="dh", bufs=5)
-                col = (h * J + t) * P
-                nc.tensor.matmul_mx(
-                    out=dh[:],
-                    lhsT=w2_codes[:, col : col + P].bitcast(E4M3),
-                    lhsT_scale=w2_scales[:, col : col + P],
-                    rhs=g_codes[:].bitcast(E5M2),
-                    rhs_scale=g_scales[:],
-                    start=True,
-                    stop=True,
-                )
-                nc.vector.scalar_tensor_tensor(da[:, t, :], a_raw[e, h][:, t, :], 0.0, dh[:], MAX, MULT)
-            mixed = work.tile([P, C, J], BF16, name="da_mixed", align_bytes=64)
-            nc.scalar.activation(mixed[:].rearrange("p (c i) t -> p c t i", i=8), da[:].rearrange("p t (c i) -> p c t i", i=8), COPY)
+                nc.vector.scalar_tensor_tensor(da[:, t, :], a_raw[e, h][:, t, :], 0.0, hidden_sums(e, h, t)[:], MAX, MULT)
+            da_planes[e, h] = da
+
+        def interleave_da(e, h):
+            da_mixed[e, h] = work.tile([P, C, J], BF16, name="da_mixed", tag=f"da_mixed{h}", bufs=1, align_bytes=64)
+            nc.scalar.activation(
+                da_mixed[e, h][:].rearrange("p (c i) t -> p c t i", i=8),
+                da_planes[e, h][:].rearrange("p t (c i) -> p c t i", i=8),
+                COPY,
+            )
+
+        def relu_on_gpsimd(e):
+            relu_a[e] = shared.tile([P, C, J], F32, name="relu_a", align_bytes=64, offset=0)
+            nc.gpsimd.tensor_scalar(relu_a[e][:], a_raw[e, 1][:].rearrange("p t c -> p c t"), F32_MAX, 0.0, MIN, MAX)
+
+        def sums_to_sbuf(e):
+            dh_planes[e] = work.tile([P, J, C], F32, name="dh_planes", bufs=1)
+            for t in range(J):
+                nc.scalar.activation(dh_planes[e][:, t, :], hidden_sums(e, 1, t)[:], COPY)
+
+        def product_on_gpsimd(e):
+            da_mixed[e, 1] = work.tile([P, C, J], BF16, name="da_mixed", tag="da_mixed1", bufs=1, align_bytes=64)
+            nc.gpsimd.tensor_tensor(da_mixed[e, 1][:], dh_planes[e][:].rearrange("p t c -> p c t"), relu_a[e][:], MULT)
+
+        def quantize_da(e, h):
             codes = work.tile([P, C], U32, name="da_codes", bufs=3, align_bytes=64)
             scales = work.tile([P, C], U8, name="da_scales", bufs=3, align_bytes=64)
-            nc.vector.quantize_mx(out=codes[:].bitcast(E5M2), scales=scales[:], in_=mixed[:].rearrange("p c t -> p (c t)"))
+            nc.vector.quantize_mx(
+                out=codes[:].bitcast(E5M2), scales=scales[:], in_=da_mixed[e, h][:].rearrange("p c t -> p (c t)")
+            )
             da_mx[e, h] = codes, scales
 
         def input_gradient(e):
@@ -151,8 +188,13 @@ def tile_moe_bdx_mlp_relu2_kernel(tc, dyT, a, w2, w1, gate, offs, out):
                     )
                 dx_banks[e, k] = dx
 
-        def copy_out(e, k, h):
-            plane = a_raw[min(e + 1, E - 1), h][:, k, :]
+        def copy_out(e, k):
+            if e == E - 1:
+                plane = a_raw[e, 1][:, k, :]
+            elif e == E - 2 and k == K_TILES - 1:
+                plane = work.tile([P, C], F32, name="late_result", tag="da_mixed0", bufs=1, align_bytes=64)[:]
+            else:
+                plane = a_raw[e + 1, 0][:, k, :]
             nc.scalar.activation(plane, dx_banks[e, k][:], COPY, scale=2.0)
             results[e, k] = plane
 
@@ -164,84 +206,65 @@ def tile_moe_bdx_mlp_relu2_kernel(tc, dyT, a, w2, w1, gate, offs, out):
         load_gate(0)
         load_tokens(0)
         load_gate(1)
-        load_tokens(1)
-        load_tokens(2)
-        load_tokens(3)
-        load_w2(0, 0)
-        load_w2(0, 1)
-        load_gate(2)
-        load_gate(3)
-        load_a(0, 0)
-        load_a(0, 1)
-        load_w1(0, 0)
-        load_w1(0, 1)
-        load_w2(1, 0)
-        load_w2(1, 1)
-        load_a(1, 0)
-        load_a(1, 1)
-        load_w1(1, 0)
-        load_w1(1, 1)
-        load_w2(2, 0)
-        load_w2(2, 1)
-        load_a(2, 0)
-        load_a(2, 1)
-        load_w1(2, 0)
-        load_w1(2, 1)
-        load_w2(3, 0)
-        load_w2(3, 1)
-        load_a(3, 0)
-        load_a(3, 1)
-        load_w1(3, 0)
-        load_w1(3, 1)
+        for t in range(1, J):
+            load_tokens(t)
+        for e in range(E):
+            for h in range(HALVES):
+                load_w2(e, h)
+            if e == 0:
+                load_gate(2)
+                load_gate(3)
+            for h in range(HALVES):
+                load_a(e, h)
+            for h in range(HALVES):
+                load_w1(e, h)
+
         gather(0)
         quantize_g(0)
         gather(1)
-        quantize_w2(0)
-        hidden_gradient(0, 0)
-        quantize_w1(0)
+        quantize_w2(0, 0)
+        quantize_w2(0, 1)
+        product_on_vector(0, 0)
         quantize_g(1)
-        quantize_w2(1)
-        hidden_gradient(0, 1)
+        interleave_da(0, 0)
+        quantize_da(0, 0)
+        product_on_vector(0, 1)
+        quantize_w1(0)
+        interleave_da(0, 1)
+        quantize_da(0, 1)
         input_gradient(0)
-        gather(2)
-        hidden_gradient(1, 0)
-        copy_out(0, 2, 0)
-        copy_out(0, 0, 0)
-        quantize_w1(1)
-        quantize_g(2)
-        quantize_w2(2)
-        scatter(0, 0)
-        hidden_gradient(1, 1)
-        copy_out(0, 1, 0)
-        input_gradient(1)
-        gather(3)
-        hidden_gradient(2, 0)
-        copy_out(1, 2, 0)
-        copy_out(1, 0, 0)
-        quantize_w1(2)
-        quantize_g(3)
-        scatter(0, 1)
-        quantize_w2(3)
-        scatter(1, 0)
-        hidden_gradient(2, 1)
-        scatter(0, 2)
-        copy_out(1, 1, 0)
-        input_gradient(2)
-        hidden_gradient(3, 0)
-        copy_out(2, 2, 0)
-        copy_out(2, 0, 0)
-        quantize_w1(3)
-        scatter(1, 1)
-        scatter(2, 0)
-        hidden_gradient(3, 1)
-        scatter(1, 2)
-        copy_out(2, 1, 0)
-        input_gradient(3)
-        copy_out(3, 0, 1)
-        copy_out(3, 1, 1)
-        copy_out(3, 2, 1)
-        scatter(2, 1)
-        scatter(2, 2)
-        scatter(3, 0)
-        scatter(3, 1)
-        scatter(3, 2)
+        quantize_w2(1, 0)
+        quantize_w2(1, 1)
+        for e in range(E - 1):
+            last = e == E - 2
+            product_on_vector(e + 1, 0)
+            relu_on_gpsimd(e + 1)
+            copy_out(e, 0)
+            sums_to_sbuf(e + 1)
+            product_on_gpsimd(e + 1)
+            copy_out(e, 1)
+            if not last:
+                copy_out(e, 2)
+            scatter(e, 0)
+            scatter(e, 1)
+            if not last:
+                scatter(e, 2)
+            interleave_da(e + 1, 0)
+            quantize_da(e + 1, 0)
+            if not last:
+                quantize_w2(e + 2, 0)
+            quantize_da(e + 1, 1)
+            if not last:
+                gather(e + 2)
+                quantize_g(e + 2)
+            quantize_w1(e + 1)
+            if not last:
+                quantize_w2(e + 2, 1)
+            else:
+                copy_out(e, 2)
+                scatter(e, 2)
+            input_gradient(e + 1)
+        for k in range(K_TILES):
+            copy_out(E - 1, k)
+        for k in range(K_TILES):
+            scatter(E - 1, k)

@@ -23,6 +23,22 @@ MIN = mybir.AluOpType.min
 F32_MAX = 3.4028234663852886e38
 COPY = mybir.ActivationFunctionType.Copy
 
+W2_MIXED_AT = (0, 18240)
+RELU_AT = 4032
+G_MIXED_AT = (4096, 8192, 4032, 8192)
+W1_TAIL_AT = 12160
+DA_AT = 14144
+GATHERED_AT = (22336, 30528, 53824, 30592)
+FIRST_A_AT = 38720
+DH_AT = FIRST_A_AT + 4096
+DH_SHIFT = 2816
+W1_HEAD_AT = FIRST_A_AT + 8192
+FIRST_GATE_AT = GATHERED_AT[2] + 8128
+SECOND_GATE_AT = FIRST_GATE_AT + 2048
+DA_MIXED_AT = SECOND_GATE_AT + 2048
+W1_HEAD = 512
+BANK = 2048
+
 
 def tile_moe_bdx_mlp_relu2_kernel(tc, dyT, a, w2, w1, gate, offs, out):
     nc = tc.nc
@@ -34,14 +50,17 @@ def tile_moe_bdx_mlp_relu2_kernel(tc, dyT, a, w2, w1, gate, offs, out):
 
         offsets = held.tile([P, E * C // 16], U16, name="offsets")
         nc.sync.dma_start(offsets[:], offs)
-        gates = [held.tile([P, C], F32, name=f"gate{e}") for e in range(E)]
-        tokens = [held.tile([P, T], F32, name=f"tokens{t}") for t in range(J)]
-        windows = [held.tile([P, T], F32, name=f"window{k}") for k in range(K_TILES)]
+        gates = [
+            shared.tile([P, C], F32, name=f"gate{e}", align_bytes=64, offset=at) for e, at in enumerate((FIRST_GATE_AT, SECOND_GATE_AT))
+        ]
+        gates.extend(held.tile([P, C], F32, name=f"gate{e}") for e in range(2, E))
+        tokens = [held.tile([P, T], F32, name=f"tokens{t}", tag=f"columns{t}") for t in range(J)]
+        windows = [held.tile([P, T], F32, name=f"window{k}", tag=f"columns{k}") for k in range(K_TILES)]
 
         dy_rows = dyT.rearrange("(p t) s -> p t s", t=J)
         a_rows = a.rearrange("(h p t) s -> h p t s", p=P, t=J)
         w2_raw, a_raw, w1_raw, gathered, g_mx, w2_mx, w1_mx, da_mx, dx_banks, results = {}, {}, {}, {}, {}, {}, {}, {}, {}, {}
-        da_planes, da_mixed, relu_a, dh_planes = {}, {}, {}, {}
+        da_planes, da_mixed, relu_a, dh_planes, g_mixed = {}, {}, {}, {}, {}
 
         def listed(e):
             return offsets[:, e * C // 16 : (e + 1) * C // 16]
@@ -53,74 +72,103 @@ def tile_moe_bdx_mlp_relu2_kernel(tc, dyT, a, w2, w1, gate, offs, out):
             nc.sync.dma_start(gates[e][:], gate[0:P, e * C : (e + 1) * C])
 
         def load_w2(e, h):
-            w2_raw[e, h] = work.tile([P, J, P * J], F32, name="w2_raw", bufs=3)
+            w2_raw[e, h] = work.tile([P, J, P * J], F32, name="w2_raw", bufs=4)
             rows = w2[e].rearrange("(p j) i -> p j i", j=J)
             nc.sync.dma_start(w2_raw[e, h][:], rows[:, :, h * P * J : (h + 1) * P * J])
 
         def load_a(e, h):
-            a_raw[e, h] = work.tile([P, J, C], F32, name="a_raw", bufs=4)
+            if (e, h) == (0, 1):
+                a_raw[e, h] = placed("a_first", [P, J, C], F32, FIRST_A_AT)
+            else:
+                a_raw[e, h] = work.tile([P, J, C], F32, name="a_raw", bufs=4)
             nc.sync.dma_start(a_raw[e, h][:], a_rows[h][:, :, e * C : (e + 1) * C])
 
         def load_w1(e, h):
-            w1_raw[e, h] = work.tile([P, J, K], F32, name="w1_raw", bufs=3)
+            w1_raw[e, h] = work.tile([P, J, K], F32, name="w1_raw", bufs=4)
             nc.sync.dma_start(w1_raw[e, h][:], w1[e].rearrange("(h p j) k -> h p j k", p=P, j=J)[h])
 
 
-        def gather(e):
-            gathered[e] = work.tile([P, J, C], F32, name="gathered", bufs=2)
-            for t in range(J):
-                nc.vector.tensor_tensor(gathered[e][:, t, :], tokens[t][:].indirect(listed(e)), gates[e][:], MULT)
+        def placed(name, shape, dtype, at):
+            return shared.tile(shape, dtype, name=f"{name}_at{at}", align_bytes=64, offset=at)
 
-        def quantize_g(e):
-            mixed = work.tile([P, C, J], BF16, name="g_mixed", align_bytes=64)
+        def bank(b):
+            return psum.tile([P, C], F32, name=f"bank{b}", offset=b * BANK)
+
+        def scale_plane(name, width, bufs, at):
+            if at is None:
+                return work.tile([P, width], U8, name=name, bufs=bufs, align_bytes=64)
+            return placed(name, [P, width], U8, at)
+
+        def batch_at(e):
+            if e == 0:
+                return FIRST_A_AT + 64
+            return DH_AT if e % 2 else DH_AT + 8192
+
+        def gather(e):
+            gathered[e] = placed("gathered", [P, J, C], F32, GATHERED_AT[e])
+            for t in range(J):
+                if e == 0:
+                    nc.vector.tensor_tensor(gathered[e][:, t, :], tokens[t][:].indirect(listed(e)), gates[e][:], MULT)
+                else:
+                    nc.vector.tensor_copy(gathered[e][:, t, :], tokens[t][:].indirect(listed(e)))
+
+        def interleave_g(e):
+            g_mixed[e, 0] = placed("g_mixed", [P, C, J], BF16, G_MIXED_AT[e])
             nc.scalar.activation(
-                mixed[:].rearrange("p (c i) t -> p c t i", i=4), gathered[e][:].rearrange("p t (c i) -> p c t i", i=4), COPY
+                g_mixed[e, 0][:].rearrange("p (c i) t -> p c t i", i=4), gathered[e][:].rearrange("p t (c i) -> p c t i", i=4), COPY
             )
-            codes = work.tile([P, C], U32, name="g_codes", bufs=3, align_bytes=64)
-            scales = work.tile([P, C], U8, name="g_scales", bufs=3, align_bytes=64)
-            nc.vector.quantize_mx(out=codes[:].bitcast(E5M2), scales=scales[:], in_=mixed[:].rearrange("p c t -> p (c t)"))
-            g_mx[e] = codes, scales
+
+        def gate_on_gpsimd(e, lo=0, hi=C):
+            g_mixed[e, lo] = placed(f"g_mixed{hi - lo}", [P, hi - lo, J], BF16, G_MIXED_AT[e])
+            nc.gpsimd.tensor_tensor(
+                g_mixed[e, lo][:],
+                gathered[e][:, :, lo:hi].rearrange("p t c -> p c t"),
+                gates[e][:, lo:hi].unsqueeze(2).to_broadcast([P, hi - lo, J]),
+                MULT,
+            )
+
+        def quantize_g(e, lo=0, hi=C):
+            if lo == 0:
+                codes = work.tile([P, C], U32, name="g_codes", bufs=3, align_bytes=64)
+                g_mx[e] = codes, scale_plane("g_scales", C, 2, {0: SECOND_GATE_AT + 1024, 2: FIRST_A_AT + 2880}.get(e))
+            codes, scales = g_mx[e]
+            nc.vector.quantize_mx(
+                out=codes[:, lo:hi].bitcast(E5M2), scales=scales[:, lo:hi], in_=g_mixed[e, lo][:].rearrange("p c t -> p (c t)")
+            )
 
         def quantize_w2(e, h):
-            if h == 0:
-                codes = work.tile([P, H], U32, name="w2_codes", align_bytes=64)
-                scales = work.tile([P, H], U8, name="w2_scales", align_bytes=64)
-                w2_mx[e] = codes, scales
-                mixed = work.tile([P, J, P, J], BF16, name="w2_mixed", bufs=1, align_bytes=64)
-            else:
-                mixed = shared.tile([P, J, P, J], BF16, name="w2_mixed_late", align_bytes=64, offset=7680)
-            codes, scales = w2_mx[e]
+            codes = work.tile([P, P * J], U32, name="w2_codes", bufs=4, align_bytes=64)
+            scales = scale_plane("w2_scales", P * J, 2, (batch_at(e - 1) if e else SECOND_GATE_AT) + 512 * h)
+            w2_mx[e, h] = codes, scales
+            mixed = placed("w2_mixed", [P, J, P, J], BF16, W2_MIXED_AT[h if e else 1 - h])
             nc.scalar.activation(
                 mixed[:].rearrange("p t m j -> p m j t"), w2_raw[e, h][:].rearrange("p j (m t) -> p m j t", t=J), COPY
             )
-            cols = slice(h * P * J, (h + 1) * P * J)
-            nc.vector.quantize_mx(
-                out=codes[:, cols].bitcast(E4M3), scales=scales[:, cols], in_=mixed[:].rearrange("p t m j -> p (t m j)")
-            )
+            nc.vector.quantize_mx(out=codes[:].bitcast(E4M3), scales=scales[:], in_=mixed[:].rearrange("p t m j -> p (t m j)"))
 
         def quantize_w1(e):
-            mixed = work.tile([P, HALVES * K, J], BF16, name="w1_mixed", bufs=1, align_bytes=64)
+            head = placed("w1_head", [P, W1_HEAD, J], BF16, W1_HEAD_AT if e < E - 1 else W2_MIXED_AT[1])
+            tail = placed("w1_tail", [P, HALVES * K - W1_HEAD, J], BF16, W1_TAIL_AT if e < E - 1 else W2_MIXED_AT[0] + 1024)
             codes = work.tile([P, HALVES * K], U32, name="w1_codes", align_bytes=64)
-            scales = work.tile([P, HALVES * K], U8, name="w1_scales", align_bytes=64)
-            for h in range(HALVES):
-                nc.scalar.activation(
-                    mixed[:, h * K : (h + 1) * K, :].rearrange("p (c i) j -> p c j i", i=4),
-                    w1_raw[e, h][:].rearrange("p j (c i) -> p c j i", i=4),
-                    COPY,
-                )
-            for lo, hi in ((0, 512), (512, HALVES * K)):
+            scales = scale_plane("w1_scales", HALVES * K, 2, batch_at(e) + 1536)
+            cut = W1_HEAD - K
+            for to, source in (
+                (head[:, 0:K, :], w1_raw[e, 0][:]),
+                (head[:, K:W1_HEAD, :], w1_raw[e, 1][:, :, 0:cut]),
+                (tail[:], w1_raw[e, 1][:, :, cut:K]),
+            ):
+                nc.scalar.activation(to.rearrange("p (c i) j -> p c j i", i=4), source.rearrange("p j (c i) -> p c j i", i=4), COPY)
+            for mixed, cols in ((head, slice(0, W1_HEAD)), (tail, slice(W1_HEAD, HALVES * K))):
                 nc.vector.quantize_mx(
-                    out=codes[:, lo:hi].bitcast(E4M3),
-                    scales=scales[:, lo:hi],
-                    in_=mixed[:, lo:hi, :].rearrange("p c j -> p (c j)"),
+                    out=codes[:, cols].bitcast(E4M3), scales=scales[:, cols], in_=mixed[:].rearrange("p c j -> p (c j)")
                 )
             w1_mx[e] = codes, scales
 
         def hidden_sums(e, h, t):
-            w2_codes, w2_scales = w2_mx[e]
+            w2_codes, w2_scales = w2_mx[e, h]
             g_codes, g_scales = g_mx[e]
-            dh = psum.tile([P, C], F32, name="dh", bufs=5)
-            col = (h * J + t) * P
+            dh = bank(h * J + t)
+            col = t * P
             nc.tensor.matmul_mx(
                 out=dh[:],
                 lhsT=w2_codes[:, col : col + P].bitcast(E4M3),
@@ -133,16 +181,13 @@ def tile_moe_bdx_mlp_relu2_kernel(tc, dyT, a, w2, w1, gate, offs, out):
             return dh
 
         def product_on_vector(e, h):
-            if h == 0:
-                da = shared.tile([P, J, C], BF16, name="da_planes", align_bytes=64, offset=8192)
-            else:
-                da = shared.tile([P, J, C], BF16, name="da_planes_first", align_bytes=64, offset=0)
+            da = placed("da_planes", [P, J, C], BF16, DA_AT if e else GATHERED_AT[0] + 4096 * h)
             for t in range(J):
                 nc.vector.scalar_tensor_tensor(da[:, t, :], a_raw[e, h][:, t, :], 0.0, hidden_sums(e, h, t)[:], MAX, MULT)
             da_planes[e, h] = da
 
         def interleave_da(e, h):
-            da_mixed[e, h] = work.tile([P, C, J], BF16, name="da_mixed", tag=f"da_mixed{h}", bufs=1, align_bytes=64)
+            da_mixed[e, h] = placed("da_mixed", [P, C, J], BF16, DA_MIXED_AT + 4096 * h)
             nc.scalar.activation(
                 da_mixed[e, h][:].rearrange("p (c i) t -> p c t i", i=8),
                 da_planes[e, h][:].rearrange("p t (c i) -> p c t i", i=8),
@@ -150,30 +195,37 @@ def tile_moe_bdx_mlp_relu2_kernel(tc, dyT, a, w2, w1, gate, offs, out):
             )
 
         def relu_on_gpsimd(e):
-            relu_a[e] = shared.tile([P, C, J], F32, name="relu_a", align_bytes=64, offset=0)
+            relu_a[e] = shared.tile([P, C, J], F32, name="relu_a", align_bytes=64, offset=RELU_AT)
             nc.gpsimd.tensor_scalar(relu_a[e][:], a_raw[e, 1][:].rearrange("p t c -> p c t"), F32_MAX, 0.0, MIN, MAX)
 
-        def sums_to_sbuf(e):
-            dh_planes[e] = work.tile([P, J, C], F32, name="dh_planes", bufs=1)
-            for t in range(J):
+        def sums_to_sbuf(e, planes):
+            if e not in dh_planes:
+                dh_planes[e] = placed("dh_planes", [P, J, C], F32, DH_AT if e % 2 else DH_AT + DH_SHIFT)
+            for t in planes:
                 nc.scalar.activation(dh_planes[e][:, t, :], hidden_sums(e, 1, t)[:], COPY)
 
         def product_on_gpsimd(e):
-            da_mixed[e, 1] = work.tile([P, C, J], BF16, name="da_mixed", tag="da_mixed1", bufs=1, align_bytes=64)
+            da_mixed[e, 1] = placed("da_mixed", [P, C, J], BF16, DA_MIXED_AT + 4096)
             nc.gpsimd.tensor_tensor(da_mixed[e, 1][:], dh_planes[e][:].rearrange("p t c -> p c t"), relu_a[e][:], MULT)
 
         def quantize_da(e, h):
             codes = work.tile([P, C], U32, name="da_codes", bufs=3, align_bytes=64)
-            scales = work.tile([P, C], U8, name="da_scales", bufs=3, align_bytes=64)
+            if e == 0:
+                at = batch_at(0) + (2304 if h else 1024)
+            elif e < E - 1:
+                at = W2_MIXED_AT[0] + 512 * h
+            else:
+                at = None if h else batch_at(e) + 1024
+            scales = scale_plane("da_scales", C, 2, at)
             nc.vector.quantize_mx(
                 out=codes[:].bitcast(E5M2), scales=scales[:], in_=da_mixed[e, h][:].rearrange("p c t -> p (c t)")
             )
             da_mx[e, h] = codes, scales
 
-        def input_gradient(e):
+        def input_gradient(e, tiles):
             w1_codes, w1_scales = w1_mx[e]
-            for k in range(K_TILES):
-                dx = psum.tile([P, C], F32, name="dx", bufs=3)
+            for k in tiles:
+                dx = bank(J + k if e < E - 1 else k)
                 for h in range(HALVES):
                     col = h * K + k * P
                     da_codes, da_scales = da_mx[e, h]
@@ -189,12 +241,10 @@ def tile_moe_bdx_mlp_relu2_kernel(tc, dyT, a, w2, w1, gate, offs, out):
                 dx_banks[e, k] = dx
 
         def copy_out(e, k):
-            if e == E - 1:
-                plane = a_raw[e, 1][:, k, :]
-            elif e == E - 2 and k == K_TILES - 1:
-                plane = work.tile([P, C], F32, name="late_result", tag="da_mixed0", bufs=1, align_bytes=64)[:]
+            if e == E - 2 and k == K_TILES - 1:
+                plane = placed("late_result", [P, C], F32, DA_MIXED_AT)[:]
             else:
-                plane = a_raw[e + 1, 0][:, k, :]
+                plane = work.tile([P, C], F32, name="result", bufs=3)[:]
             nc.scalar.activation(plane, dx_banks[e, k][:], COPY, scale=2.0)
             results[e, k] = plane
 
@@ -204,44 +254,62 @@ def tile_moe_bdx_mlp_relu2_kernel(tc, dyT, a, w2, w1, gate, offs, out):
                 nc.sync.dma_start(out[k * P : (k + 1) * P, :], windows[k][:])
 
         load_gate(0)
-        load_tokens(0)
-        load_gate(1)
-        for t in range(1, J):
+        for t in range(J):
             load_tokens(t)
-        for e in range(E):
-            for h in range(HALVES):
-                load_w2(e, h)
-            if e == 0:
-                load_gate(2)
+        load_gate(1)
+        load_w2(0, 0)
+        load_w2(0, 1)
+        load_w1(0, 0)
+        load_a(0, 0)
+        load_w1(0, 1)
+        load_gate(2)
+        load_a(0, 1)
+        for e in range(1, E):
+            load_w2(e, 1)
+            load_w2(e, 0)
+            if e > 1:
+                load_w1(e - 1, 0)
+                load_w1(e - 1, 1)
+            load_a(e, 0)
+            load_a(e, 1)
+            if e == 1:
                 load_gate(3)
-            for h in range(HALVES):
-                load_a(e, h)
-            for h in range(HALVES):
-                load_w1(e, h)
+        load_w1(E - 1, 0)
+        load_w1(E - 1, 1)
 
         gather(0)
-        quantize_g(0)
+        interleave_g(0)
         gather(1)
+        gate_on_gpsimd(1)
+        gather(2)
+        quantize_g(0)
         quantize_w2(0, 0)
-        quantize_w2(0, 1)
-        product_on_vector(0, 0)
         quantize_g(1)
+        quantize_w2(0, 1)
+        gate_on_gpsimd(2)
+        product_on_vector(0, 0)
+        product_on_vector(0, 1)
+        gather(3)
         interleave_da(0, 0)
         quantize_da(0, 0)
-        product_on_vector(0, 1)
-        quantize_w1(0)
+        quantize_g(2)
+        quantize_w2(1, 1)
         interleave_da(0, 1)
         quantize_da(0, 1)
-        input_gradient(0)
         quantize_w2(1, 0)
-        quantize_w2(1, 1)
+        quantize_w1(0)
         for e in range(E - 1):
             last = e == E - 2
+            sums_to_sbuf(e + 1, [0])
+            input_gradient(e, [0])
             product_on_vector(e + 1, 0)
             relu_on_gpsimd(e + 1)
             copy_out(e, 0)
-            sums_to_sbuf(e + 1)
+            sums_to_sbuf(e + 1, [1, 2, 3])
             product_on_gpsimd(e + 1)
+            if not last:
+                gate_on_gpsimd(E - 1, e * C // 2, (e + 1) * C // 2)
+            input_gradient(e, [1, 2])
             copy_out(e, 1)
             if not last:
                 copy_out(e, 2)
@@ -250,20 +318,17 @@ def tile_moe_bdx_mlp_relu2_kernel(tc, dyT, a, w2, w1, gate, offs, out):
             if not last:
                 scatter(e, 2)
             interleave_da(e + 1, 0)
-            quantize_da(e + 1, 0)
-            if not last:
-                quantize_w2(e + 2, 0)
-            quantize_da(e + 1, 1)
-            if not last:
-                gather(e + 2)
-                quantize_g(e + 2)
-            quantize_w1(e + 1)
             if not last:
                 quantize_w2(e + 2, 1)
-            else:
+                quantize_w2(e + 2, 0)
+                quantize_g(E - 1, e * C // 2, (e + 1) * C // 2)
+            quantize_da(e + 1, 1)
+            quantize_da(e + 1, 0)
+            quantize_w1(e + 1)
+            if last:
                 copy_out(e, 2)
                 scatter(e, 2)
-            input_gradient(e + 1)
+        input_gradient(E - 1, range(K_TILES))
         for k in range(K_TILES):
             copy_out(E - 1, k)
         for k in range(K_TILES):

@@ -19,15 +19,15 @@ E4M3 = mybir.dt.float8_e4m3fn_x4
 E5M2 = mybir.dt.float8_e5m2_x4
 MULT = mybir.AluOpType.mult
 MAX = mybir.AluOpType.max
+ADD = mybir.AluOpType.add
 MIN = mybir.AluOpType.min
 F32_MAX = 3.4028234663852886e38
 COPY = mybir.ActivationFunctionType.Copy
 
-W2_MIXED_AT = (0, 18240)
-RELU_AT = 4032
-G_MIXED_AT = (4096, 8192, 4032, 8192)
-W1_TAIL_AT = 12160
-DA_AT = 14144
+W2_MIXED_AT = (18240, 0)
+RELU_AT = 4096
+W1_TAIL_AT = 12224
+DA_AT = 14208
 GATHERED_AT = (22336, 30528, 53824, 30592)
 FIRST_A_AT = 38720
 DH_AT = FIRST_A_AT + 4096
@@ -36,6 +36,8 @@ W1_HEAD_AT = FIRST_A_AT + 8192
 FIRST_GATE_AT = GATHERED_AT[2] + 8128
 SECOND_GATE_AT = FIRST_GATE_AT + 2048
 DA_MIXED_AT = SECOND_GATE_AT + 2048
+G_MIXED_AT = (4032, 8128, DA_MIXED_AT + 8192, 8192)
+FIRST_W2_MIXED_AT = (W2_MIXED_AT[0], G_MIXED_AT[2] - 4032)
 W1_HEAD = 512
 BANK = 2048
 
@@ -130,7 +132,7 @@ def tile_moe_bdx_mlp_relu2_kernel(tc, dyT, a, w2, w1, gate, offs, out):
         def quantize_g(e, lo=0, hi=C):
             if lo == 0:
                 codes = work.tile([P, C], U32, name="g_codes", bufs=3, align_bytes=64)
-                g_mx[e] = codes, scale_plane("g_scales", C, 2, {0: SECOND_GATE_AT + 1024, 2: FIRST_A_AT + 2880}.get(e))
+                g_mx[e] = codes, scale_plane("g_scales", C, 2, {0: SECOND_GATE_AT + 1024, 1: FIRST_A_AT + 2368, 2: FIRST_A_AT + 2880}.get(e))
             codes, scales = g_mx[e]
             nc.vector.quantize_mx(
                 out=codes[:, lo:hi].bitcast(E5M2), scales=scales[:, lo:hi], in_=g_mixed[e, lo][:].rearrange("p c t -> p (c t)")
@@ -140,17 +142,17 @@ def tile_moe_bdx_mlp_relu2_kernel(tc, dyT, a, w2, w1, gate, offs, out):
             codes = work.tile([P, P * J], U32, name="w2_codes", bufs=4, align_bytes=64)
             scales = scale_plane("w2_scales", P * J, 2, (batch_at(e - 1) if e else SECOND_GATE_AT) + 512 * h)
             w2_mx[e, h] = codes, scales
-            mixed = placed("w2_mixed", [P, J, P, J], BF16, W2_MIXED_AT[h if e else 1 - h])
+            mixed = placed("w2_mixed", [P, J, P, J], BF16, (W2_MIXED_AT if e else FIRST_W2_MIXED_AT)[h])
             nc.scalar.activation(
                 mixed[:].rearrange("p t m j -> p m j t"), w2_raw[e, h][:].rearrange("p j (m t) -> p m j t", t=J), COPY
             )
             nc.vector.quantize_mx(out=codes[:].bitcast(E4M3), scales=scales[:], in_=mixed[:].rearrange("p t m j -> p (t m j)"))
 
         def quantize_w1(e):
-            head = placed("w1_head", [P, W1_HEAD, J], BF16, W1_HEAD_AT if e < E - 1 else W2_MIXED_AT[1])
-            tail = placed("w1_tail", [P, HALVES * K - W1_HEAD, J], BF16, W1_TAIL_AT if e < E - 1 else W2_MIXED_AT[0] + 1024)
+            head = placed("w1_head", [P, W1_HEAD, J], BF16, W1_HEAD_AT if e < E - 1 else W2_MIXED_AT[0])
+            tail = placed("w1_tail", [P, HALVES * K - W1_HEAD, J], BF16, W1_TAIL_AT if e < E - 1 else W1_TAIL_AT + 64)
             codes = work.tile([P, HALVES * K], U32, name="w1_codes", align_bytes=64)
-            scales = scale_plane("w1_scales", HALVES * K, 2, batch_at(e) + 1536)
+            scales = scale_plane("w1_scales", HALVES * K, 2, W2_MIXED_AT[0] + 576 if e < E - 1 else batch_at(e) + 1536)
             cut = W1_HEAD - K
             for to, source in (
                 (head[:, 0:K, :], w1_raw[e, 0][:]),
@@ -188,11 +190,14 @@ def tile_moe_bdx_mlp_relu2_kernel(tc, dyT, a, w2, w1, gate, offs, out):
 
         def interleave_da(e, h):
             da_mixed[e, h] = placed("da_mixed", [P, C, J], BF16, DA_MIXED_AT + 4096 * h)
-            nc.scalar.activation(
-                da_mixed[e, h][:].rearrange("p (c i) t -> p c t i", i=8),
-                da_planes[e, h][:].rearrange("p t (c i) -> p c t i", i=8),
-                COPY,
-            )
+            if h:
+                nc.gpsimd.tensor_scalar(da_mixed[e, h][:], da_planes[e, h][:].rearrange("p t c -> p c t"), 1.0, 0.0, MULT, ADD)
+            else:
+                nc.scalar.activation(
+                    da_mixed[e, h][:].rearrange("p (c i) t -> p c t i", i=8),
+                    da_planes[e, h][:].rearrange("p t (c i) -> p c t i", i=8),
+                    COPY,
+                )
 
         def relu_on_gpsimd(e):
             relu_a[e] = shared.tile([P, C, J], F32, name="relu_a", align_bytes=64, offset=RELU_AT)
@@ -210,10 +215,8 @@ def tile_moe_bdx_mlp_relu2_kernel(tc, dyT, a, w2, w1, gate, offs, out):
 
         def quantize_da(e, h):
             codes = work.tile([P, C], U32, name="da_codes", bufs=3, align_bytes=64)
-            if e == 0:
-                at = batch_at(0) + (2304 if h else 1024)
-            elif e < E - 1:
-                at = W2_MIXED_AT[0] + 512 * h
+            if e < E - 1:
+                at = W2_MIXED_AT[h] + 64
             else:
                 at = None if h else batch_at(e) + 1024
             scales = scale_plane("da_scales", C, 2, at)
@@ -253,17 +256,18 @@ def tile_moe_bdx_mlp_relu2_kernel(tc, dyT, a, w2, w1, gate, offs, out):
             if e == E - 1:
                 nc.sync.dma_start(out[k * P : (k + 1) * P, :], windows[k][:])
 
+        load_tokens(0)
         load_gate(0)
-        for t in range(J):
+        for t in range(1, J):
             load_tokens(t)
         load_gate(1)
         load_w2(0, 0)
         load_w2(0, 1)
         load_w1(0, 0)
         load_a(0, 0)
-        load_w1(0, 1)
         load_gate(2)
         load_a(0, 1)
+        load_w1(0, 1)
         for e in range(1, E):
             load_w2(e, 1)
             load_w2(e, 0)
@@ -284,19 +288,19 @@ def tile_moe_bdx_mlp_relu2_kernel(tc, dyT, a, w2, w1, gate, offs, out):
         gather(2)
         quantize_g(0)
         quantize_w2(0, 0)
-        quantize_g(1)
         quantize_w2(0, 1)
         gate_on_gpsimd(2)
         product_on_vector(0, 0)
         product_on_vector(0, 1)
         gather(3)
         interleave_da(0, 0)
-        quantize_da(0, 0)
-        quantize_g(2)
-        quantize_w2(1, 1)
         interleave_da(0, 1)
-        quantize_da(0, 1)
+        quantize_g(1)
+        quantize_w2(1, 1)
+        quantize_g(2)
         quantize_w2(1, 0)
+        quantize_da(0, 0)
+        quantize_da(0, 1)
         quantize_w1(0)
         for e in range(E - 1):
             last = e == E - 2

@@ -154,12 +154,17 @@ def tile_moe_bdx_mlp_relu2_kernel(tc, dyT, a, w2, w1, gate, offs, out):
             codes = work.tile([P, HALVES * K], U32, name="w1_codes", align_bytes=64)
             scales = scale_plane("w1_scales", HALVES * K, 2, W2_MIXED_AT[0] + 576 if e < E - 1 else batch_at(e) + 1536)
             cut = W1_HEAD - K
-            for to, source in (
+            pieces = (
                 (head[:, 0:K, :], w1_raw[e, 0][:]),
                 (head[:, K:W1_HEAD, :], w1_raw[e, 1][:, :, 0:cut]),
                 (tail[:], w1_raw[e, 1][:, :, cut:K]),
-            ):
-                nc.scalar.activation(to.rearrange("p (c i) j -> p c j i", i=4), source.rearrange("p j (c i) -> p c j i", i=4), COPY)
+            )
+            for piece, (to, source) in enumerate(pieces):
+                to, source = to.rearrange("p (c i) j -> p c j i", i=4), source.rearrange("p j (c i) -> p c j i", i=4)
+                if piece == 1 and 0 < e < E - 1:
+                    nc.vector.tensor_copy(to, source)
+                else:
+                    nc.scalar.activation(to, source, COPY)
             for mixed, cols in ((head, slice(0, W1_HEAD)), (tail, slice(W1_HEAD, HALVES * K))):
                 nc.vector.quantize_mx(
                     out=codes[:, cols].bitcast(E4M3), scales=scales[:, cols], in_=mixed[:].rearrange("p c j -> p (c j)")

@@ -123,9 +123,9 @@ def tile_moe_bdx_mlp_relu2_kernel(tc, dyT, a, w2, w1, gate, offs, out):
         def gate_on_gpsimd(e, lo=0, hi=C):
             g_mixed[e, lo] = placed(f"g_mixed{hi - lo}", [P, hi - lo, J], BF16, G_MIXED_AT[e])
             nc.gpsimd.tensor_tensor(
-                g_mixed[e, lo][:],
-                gathered[e][:, :, lo:hi].rearrange("p t c -> p c t"),
-                gates[e][:, lo:hi].unsqueeze(2).to_broadcast([P, hi - lo, J]),
+                g_mixed[e, lo][:].rearrange("p (c i) t -> p c t i", i=2),
+                gathered[e][:, :, lo:hi].rearrange("p t (c i) -> p c t i", i=2),
+                gates[e][:, lo:hi].rearrange("p (c i) -> p c i", i=2).unsqueeze(2).to_broadcast([P, (hi - lo) // 2, J, 2]),
                 MULT,
             )
 
@@ -196,7 +196,14 @@ def tile_moe_bdx_mlp_relu2_kernel(tc, dyT, a, w2, w1, gate, offs, out):
         def interleave_da(e, h):
             da_mixed[e, h] = placed("da_mixed", [P, C, J], BF16, DA_MIXED_AT + 4096 * h)
             if h:
-                nc.gpsimd.tensor_scalar(da_mixed[e, h][:], da_planes[e, h][:].rearrange("p t c -> p c t"), 1.0, 0.0, MULT, ADD)
+                nc.gpsimd.tensor_scalar(
+                    da_mixed[e, h][:].rearrange("p (c i) t -> p c t i", i=2),
+                    da_planes[e, h][:].rearrange("p t (c i) -> p c t i", i=2),
+                    1.0,
+                    0.0,
+                    MULT,
+                    ADD,
+                )
             else:
                 nc.scalar.activation(
                     da_mixed[e, h][:].rearrange("p (c i) t -> p c t i", i=8),
@@ -205,8 +212,8 @@ def tile_moe_bdx_mlp_relu2_kernel(tc, dyT, a, w2, w1, gate, offs, out):
                 )
 
         def relu_on_gpsimd(e):
-            relu_a[e] = shared.tile([P, C, J], F32, name="relu_a", align_bytes=64, offset=RELU_AT)
-            nc.gpsimd.tensor_scalar(relu_a[e][:], a_raw[e, 1][:].rearrange("p t c -> p c t"), F32_MAX, 0.0, MIN, MAX)
+            relu_a[e] = shared.tile([P, C // 2, J, 2], F32, name="relu_a", align_bytes=64, offset=RELU_AT)
+            nc.gpsimd.tensor_scalar(relu_a[e][:], a_raw[e, 1][:].rearrange("p t (c i) -> p c t i", i=2), F32_MAX, 0.0, MIN, MAX)
 
         def sums_to_sbuf(e, planes):
             if e not in dh_planes:
@@ -216,7 +223,12 @@ def tile_moe_bdx_mlp_relu2_kernel(tc, dyT, a, w2, w1, gate, offs, out):
 
         def product_on_gpsimd(e):
             da_mixed[e, 1] = placed("da_mixed", [P, C, J], BF16, DA_MIXED_AT + 4096)
-            nc.gpsimd.tensor_tensor(da_mixed[e, 1][:], dh_planes[e][:].rearrange("p t c -> p c t"), relu_a[e][:], MULT)
+            nc.gpsimd.tensor_tensor(
+                da_mixed[e, 1][:].rearrange("p (c i) t -> p c t i", i=2),
+                dh_planes[e][:].rearrange("p t (c i) -> p c t i", i=2),
+                relu_a[e][:],
+                MULT,
+            )
 
         def quantize_da(e, h):
             codes = work.tile([P, C], U32, name="da_codes", bufs=3, align_bytes=64)

@@ -5,6 +5,7 @@ import concourse.mybir as mybir
 K, T, E, C, H, N = 384, 2048, 4, 512, 1024, 512
 P = 128
 J = 4
+Q = 32
 HALVES = H // (P * J)
 K_TILES = K // P
 FLOPS = 2 * E * C * (N * H + H * K)
@@ -24,19 +25,22 @@ MIN = mybir.AluOpType.min
 F32_MAX = 3.4028234663852886e38
 COPY = mybir.ActivationFunctionType.Copy
 
-W2_MIXED_AT = (18240, 0)
-RELU_AT = 4096
-W1_TAIL_AT = 12224
-DA_AT = 14208
-GATHERED_AT = (22336, 30528, 53824, 30592)
-FIRST_A_AT = 38720
+W2_MIXED_AT = (18368, (12224, 0))
+RELU_AT = (4096, 4032)
+GATHERED_AT = (22464, 30656, 52160, 30720)
+W1_TAIL_AT = (12224, GATHERED_AT[0] + 4096)
+W1_HEAD_AT = (14272, GATHERED_AT[0])
+FIRST_A_AT = 38848
 DH_AT = FIRST_A_AT + 4096
-DH_SHIFT = 2816
-W1_HEAD_AT = FIRST_A_AT + 8192
-FIRST_GATE_AT = GATHERED_AT[2] + 8128
+DH_SHIFT = 1024
+FIRST_GATE_AT = GATHERED_AT[2] + 8192
 SECOND_GATE_AT = FIRST_GATE_AT + 2048
-DA_MIXED_AT = SECOND_GATE_AT + 2048
-G_MIXED_AT = (4032, 8128, DA_MIXED_AT + 8192, 8192)
+DA_MIXED_AT = SECOND_GATE_AT + 2048 + 192
+G_MIXED_AT = (3968, 8064, DA_MIXED_AT + 8192)
+W2_RAW_AT = ((G_MIXED_AT[2] + 4608, G_MIXED_AT[2] + 13312), (G_MIXED_AT[2] + 21504, G_MIXED_AT[2] + 33728))
+DA_AT = (W2_RAW_AT[1][0] + 8128, W2_RAW_AT[1][0] + 8192)
+A_RAW_AT = (W2_RAW_AT[1][1] + 8192, W2_RAW_AT[1][1] + 18432)
+LAST_G_AT = (A_RAW_AT[1] - 2048, A_RAW_AT[0])
 FIRST_W2_MIXED_AT = (W2_MIXED_AT[0], G_MIXED_AT[2] - 4032)
 W1_HEAD = 512
 BANK = 2048
@@ -51,44 +55,75 @@ def tile_moe_bdx_mlp_relu2_kernel(tc, dyT, a, w2, w1, gate, offs, out):
         psum = ctx.enter_context(tc.psum_pool(name="psum", bufs=1))
 
         offsets = held.tile([P, E * C // 16], U16, name="offsets")
-        nc.sync.dma_start(offsets[:], offs)
-        gates = [
-            shared.tile([P, C], F32, name=f"gate{e}", align_bytes=64, offset=at) for e, at in enumerate((FIRST_GATE_AT, SECOND_GATE_AT))
-        ]
-        gates.extend(held.tile([P, C], F32, name=f"gate{e}") for e in range(2, E))
+        gates = {}
         tokens = [held.tile([P, T], F32, name=f"tokens{t}", tag=f"columns{t}") for t in range(J)]
         windows = [held.tile([P, T], F32, name=f"window{k}", tag=f"columns{k}") for k in range(K_TILES)]
 
+        identity = held.tile([P, P], F32, name="identity")
+        ones = held.tile([P, Q], F32, name="ones")
+        column = held.tile([P, Q], F32, name="column", align_bytes=64)
+        row = held.tile([P, Q], F32, name="row", align_bytes=64)
+        nc.vector.memset(identity[:], 0.0)
+        nc.vector.memset(ones[:], 1.0)
+        nc.vector.tensor_tensor_scan(column[:], ones[:], ones[:], 0.0, MULT, ADD)
+        nc.vector.transpose(row[:], column[:])
+        for first in range(0, P, Q):
+            rows = slice(first, first + Q)
+            nc.vector.tensor_tensor(identity[rows, rows], column[rows, :], row[rows, :], mybir.AluOpType.is_equal)
+        gate_rows, w1_mixed = {}, {}
+        twos = [shared.tile([P, 1], F32, name=f"two{e}", align_bytes=64, offset=DA_MIXED_AT - 64 * (e + 1)) for e in range(E - 1)]
+        for two in twos:
+            nc.vector.memset(two[:], 2.0)
         dy_rows = dyT.rearrange("(p t) s -> p t s", t=J)
         a_rows = a.rearrange("(h p t) s -> h p t s", p=P, t=J)
         w2_raw, a_raw, w1_raw, gathered, g_mx, w2_mx, w1_mx, da_mx, dx_banks, results = {}, {}, {}, {}, {}, {}, {}, {}, {}, {}
         da_planes, da_mixed, relu_a, dh_planes, g_mixed = {}, {}, {}, {}, {}
 
-        def listed(e):
-            return offsets[:, e * C // 16 : (e + 1) * C // 16]
+        def listed(e, lo=0, hi=C):
+            return offsets[:, (e * C + lo) // 16 : (e * C + hi) // 16]
 
         def load_tokens(t):
             nc.sync.dma_start(tokens[t][:], dy_rows[:, t, :])
 
-        def load_gate(e):
-            nc.sync.dma_start(gates[e][:], gate[0:P, e * C : (e + 1) * C])
+        def load_gate_rows(queue, rows, experts):
+            queue.dma_start(rows[:], gate[0].rearrange("(e p c) -> p e c", p=P, c=J)[:, experts, :])
+
+        def spread_gate(e):
+            spread = psum.tile([P, J, P], F32, name=f"spread{e in (1, 2)}", offset=(J + (e in (1, 2))) * BANK)
+            for c in range(J):
+                nc.tensor.transpose(spread[:, c, :], gate_rows[e][:, c : c + 1].to_broadcast([P, P]), identity[:])
+            if e < E - 1:
+                gates[e] = placed("gate", [P, C], F32, (FIRST_GATE_AT, SECOND_GATE_AT, W2_RAW_AT[1][0])[e])
+            else:
+                gates[e] = held.tile([P, C], F32, name="last_gate")
+            nc.scalar.activation(gates[e][:].rearrange("m (p c) -> m p c", c=J), spread[:].rearrange("m c p -> m p c"), COPY)
 
         def load_w2(e, h):
-            w2_raw[e, h] = work.tile([P, J, P * J], F32, name="w2_raw", bufs=4)
+            w2_raw[e, h] = placed("w2_raw", [P, J, P * J], F32, W2_RAW_AT[h][e % 2] - (64 if e < 2 and h == 0 else 0))
             rows = w2[e].rearrange("(p j) i -> p j i", j=J)
             nc.sync.dma_start(w2_raw[e, h][:], rows[:, :, h * P * J : (h + 1) * P * J])
 
         def load_a(e, h):
-            if (e, h) == (0, 1):
-                a_raw[e, h] = placed("a_first", [P, J, C], F32, FIRST_A_AT)
+            if h:
+                a_raw[e, h] = placed("a_raw", [P, J, C], F32, (FIRST_A_AT, A_RAW_AT[1] - 64, A_RAW_AT[0], A_RAW_AT[1])[e])
             else:
-                a_raw[e, h] = work.tile([P, J, C], F32, name="a_raw", bufs=4)
+                a_raw[e, h] = work.tile([P, J, C], F32, name="a_raw", bufs=2)
             nc.sync.dma_start(a_raw[e, h][:], a_rows[h][:, :, e * C : (e + 1) * C])
 
         def load_w1(e, h):
             w1_raw[e, h] = work.tile([P, J, K], F32, name="w1_raw", bufs=4)
             nc.sync.dma_start(w1_raw[e, h][:], w1[e].rearrange("(h p j) k -> h p j k", p=P, j=J)[h])
 
+
+        def load_round(e):
+            if e + 1 < E:
+                load_w2(e + 1, 0)
+            load_w1(e, 0)
+            load_w1(e, 1)
+            if e + 1 < E:
+                load_w2(e + 1, 1)
+                load_a(e + 1, 0)
+                load_a(e + 1, 1)
 
         def placed(name, shape, dtype, at):
             return shared.tile(shape, dtype, name=f"{name}_at{at}", align_bytes=64, offset=at)
@@ -109,19 +144,29 @@ def tile_moe_bdx_mlp_relu2_kernel(tc, dyT, a, w2, w1, gate, offs, out):
         def gather(e):
             gathered[e] = placed("gathered", [P, J, C], F32, GATHERED_AT[e])
             for t in range(J):
-                if e == 0:
-                    nc.vector.tensor_tensor(gathered[e][:, t, :], tokens[t][:].indirect(listed(e)), gates[e][:], MULT)
-                else:
-                    nc.vector.tensor_copy(gathered[e][:, t, :], tokens[t][:].indirect(listed(e)))
+                nc.vector.tensor_copy(gathered[e][:, t, :], tokens[t][:].indirect(listed(e)))
 
-        def interleave_g(e):
-            g_mixed[e, 0] = placed("g_mixed", [P, C, J], BF16, G_MIXED_AT[e])
-            nc.scalar.activation(
-                g_mixed[e, 0][:].rearrange("p (c i) t -> p c t i", i=4), gathered[e][:].rearrange("p t (c i) -> p c t i", i=4), COPY
-            )
+        def gather_plane(e, t):
+            if t % 2 == 0:
+                gathered[e, t // 2] = placed("gathered_pair", [P, 2, C], F32, GATHERED_AT[e] + 2048 * t)
+            to = gathered[e, t // 2][:, t % 2, :]
+            if e == 1 and t < 2:
+                nc.vector.tensor_tensor(to, tokens[t][:].indirect(listed(e)), gates[e][:], MULT)
+            else:
+                nc.vector.tensor_copy(to, tokens[t][:].indirect(listed(e)))
+
+        def gate_pair(e, u):
+            if u == 0:
+                g_mixed[e, 0] = placed("g_mixed", [P, C, J], BF16, G_MIXED_AT[e])
+            to = g_mixed[e, 0][:, :, 2 * u : 2 * u + 2].rearrange("p (c i) t -> p c t i", i=2)
+            source = gathered[e, u][:].rearrange("p t (c i) -> p c t i", i=2)
+            if (e, u) == (1, 0):
+                nc.scalar.activation(to, source, COPY)
+            else:
+                nc.gpsimd.tensor_tensor(to, source, gates[e][:].rearrange("p (c i) -> p c i", i=2).unsqueeze(2).to_broadcast([P, C // 2, 2, 2]), MULT)
 
         def gate_on_gpsimd(e, lo=0, hi=C):
-            g_mixed[e, lo] = placed(f"g_mixed{hi - lo}", [P, hi - lo, J], BF16, G_MIXED_AT[e])
+            g_mixed[e, lo] = placed(f"g_mixed{hi - lo}", [P, hi - lo, J], BF16, G_MIXED_AT[e] if e < E - 1 else LAST_G_AT[lo // (C // 2)])
             nc.gpsimd.tensor_tensor(
                 g_mixed[e, lo][:].rearrange("p (c i) t -> p c t i", i=2),
                 gathered[e][:, :, lo:hi].rearrange("p t (c i) -> p c t i", i=2),
@@ -132,7 +177,7 @@ def tile_moe_bdx_mlp_relu2_kernel(tc, dyT, a, w2, w1, gate, offs, out):
         def quantize_g(e, lo=0, hi=C):
             if lo == 0:
                 codes = work.tile([P, C], U32, name="g_codes", bufs=3, align_bytes=64)
-                g_mx[e] = codes, scale_plane("g_scales", C, 2, {0: SECOND_GATE_AT + 1024, 1: FIRST_A_AT + 2368, 2: FIRST_A_AT + 2880}.get(e))
+                g_mx[e] = codes, scale_plane("g_scales", C, 1, {0: SECOND_GATE_AT + 1024, 1: W2_RAW_AT[0][0] - 512, 2: W2_RAW_AT[0][1] - 512, 3: batch_at(2) + 512}[e])
             codes, scales = g_mx[e]
             nc.vector.quantize_mx(
                 out=codes[:, lo:hi].bitcast(E5M2), scales=scales[:, lo:hi], in_=g_mixed[e, lo][:].rearrange("p c t -> p (c t)")
@@ -140,36 +185,33 @@ def tile_moe_bdx_mlp_relu2_kernel(tc, dyT, a, w2, w1, gate, offs, out):
 
         def quantize_w2(e, h):
             codes = work.tile([P, P * J], U32, name="w2_codes", bufs=4, align_bytes=64)
-            scales = scale_plane("w2_scales", P * J, 2, (batch_at(e - 1) if e else SECOND_GATE_AT) + 512 * h)
+            scales = scale_plane("w2_scales", P * J, 2, (batch_at(e - 1), W1_HEAD_AT[e > 1])[h] if e else SECOND_GATE_AT + 512 * h)
             w2_mx[e, h] = codes, scales
-            mixed = placed("w2_mixed", [P, J, P, J], BF16, (W2_MIXED_AT if e else FIRST_W2_MIXED_AT)[h])
+            mixed = placed("w2_mixed", [P, J, P, J], BF16, ((W2_MIXED_AT[0], W2_MIXED_AT[1][e % 2]) if e else FIRST_W2_MIXED_AT)[h])
             nc.scalar.activation(
                 mixed[:].rearrange("p t m j -> p m j t"), w2_raw[e, h][:].rearrange("p j (m t) -> p m j t", t=J), COPY
             )
             nc.vector.quantize_mx(out=codes[:].bitcast(E4M3), scales=scales[:], in_=mixed[:].rearrange("p t m j -> p (t m j)"))
 
-        def quantize_w1(e):
-            head = placed("w1_head", [P, W1_HEAD, J], BF16, W1_HEAD_AT if e < E - 1 else W2_MIXED_AT[0])
-            tail = placed("w1_tail", [P, HALVES * K - W1_HEAD, J], BF16, W1_TAIL_AT if e < E - 1 else W1_TAIL_AT + 64)
-            codes = work.tile([P, HALVES * K], U32, name="w1_codes", align_bytes=64)
-            scales = scale_plane("w1_scales", HALVES * K, 2, W2_MIXED_AT[0] + 576 if e < E - 1 else batch_at(e) + 1536)
-            cut = W1_HEAD - K
-            pieces = (
-                (head[:, 0:K, :], w1_raw[e, 0][:]),
-                (head[:, K:W1_HEAD, :], w1_raw[e, 1][:, :, 0:cut]),
-                (tail[:], w1_raw[e, 1][:, :, cut:K]),
+        def mix_w1(e, lo, hi, at):
+            w1_mixed[e, lo] = placed(f"w1_mixed{hi - lo}", [P, hi - lo, J], BF16, at)
+            for h in range(HALVES):
+                first, end = max(lo, h * K), min(hi, (h + 1) * K)
+                if first < end:
+                    nc.scalar.activation(
+                        w1_mixed[e, lo][:, first - lo : end - lo, :].rearrange("p (c i) j -> p c j i", i=4),
+                        w1_raw[e, h][:, :, first - h * K : end - h * K].rearrange("p j (c i) -> p c j i", i=4),
+                        COPY,
+                    )
+
+        def quantize_w1(e, lo, hi):
+            if e not in w1_mx:
+                codes = work.tile([P, HALVES * K], U32, name="w1_codes", align_bytes=64)
+                w1_mx[e] = codes, scale_plane("w1_scales", HALVES * K, 2, W2_MIXED_AT[0] + 1088 if e < E - 1 else batch_at(e) + 1536)
+            codes, scales = w1_mx[e]
+            nc.vector.quantize_mx(
+                out=codes[:, lo:hi].bitcast(E4M3), scales=scales[:, lo:hi], in_=w1_mixed[e, lo][:].rearrange("p c j -> p (c j)")
             )
-            for piece, (to, source) in enumerate(pieces):
-                to, source = to.rearrange("p (c i) j -> p c j i", i=4), source.rearrange("p j (c i) -> p c j i", i=4)
-                if piece == 1 and 0 < e < E - 1:
-                    nc.vector.tensor_copy(to, source)
-                else:
-                    nc.scalar.activation(to, source, COPY)
-            for mixed, cols in ((head, slice(0, W1_HEAD)), (tail, slice(W1_HEAD, HALVES * K))):
-                nc.vector.quantize_mx(
-                    out=codes[:, cols].bitcast(E4M3), scales=scales[:, cols], in_=mixed[:].rearrange("p c j -> p (c j)")
-                )
-            w1_mx[e] = codes, scales
 
         def hidden_sums(e, h, t):
             w2_codes, w2_scales = w2_mx[e, h]
@@ -188,13 +230,13 @@ def tile_moe_bdx_mlp_relu2_kernel(tc, dyT, a, w2, w1, gate, offs, out):
             return dh
 
         def product_on_vector(e, h):
-            da = placed("da_planes", [P, J, C], BF16, DA_AT if e else GATHERED_AT[0] + 4096 * h)
+            da = placed("da_planes", [P, J, C], BF16, DA_AT[e % 2] if e else GATHERED_AT[0] + 4096 * h - 64)
             for t in range(J):
                 nc.vector.scalar_tensor_tensor(da[:, t, :], a_raw[e, h][:, t, :], 0.0, hidden_sums(e, h, t)[:], MAX, MULT)
             da_planes[e, h] = da
 
         def interleave_da(e, h):
-            da_mixed[e, h] = placed("da_mixed", [P, C, J], BF16, DA_MIXED_AT + 4096 * h)
+            da_mixed[e, h] = placed("da_mixed", [P, C, J], BF16, DA_MIXED_AT + 4096 if h else DA_MIXED_AT - 64 * e)
             if h:
                 nc.gpsimd.tensor_scalar(
                     da_mixed[e, h][:].rearrange("p (c i) t -> p c t i", i=2),
@@ -205,14 +247,15 @@ def tile_moe_bdx_mlp_relu2_kernel(tc, dyT, a, w2, w1, gate, offs, out):
                     ADD,
                 )
             else:
-                nc.scalar.activation(
-                    da_mixed[e, h][:].rearrange("p (c i) t -> p c t i", i=8),
-                    da_planes[e, h][:].rearrange("p t (c i) -> p c t i", i=8),
-                    COPY,
-                )
+                for slots in (slice(0, C // 2), slice(C // 2, C)):
+                    nc.scalar.activation(
+                        da_mixed[e, h][:, slots, :].rearrange("p (c i) t -> p c t i", i=8),
+                        da_planes[e, h][:, :, slots].rearrange("p t (c i) -> p c t i", i=8),
+                        COPY,
+                    )
 
         def relu_on_gpsimd(e):
-            relu_a[e] = shared.tile([P, C // 2, J, 2], F32, name="relu_a", align_bytes=64, offset=RELU_AT)
+            relu_a[e] = placed("relu_a", [P, C // 2, J, 2], F32, RELU_AT[e % 2])
             nc.gpsimd.tensor_scalar(relu_a[e][:], a_raw[e, 1][:].rearrange("p t (c i) -> p c t i", i=2), F32_MAX, 0.0, MIN, MAX)
 
         def sums_to_sbuf(e, planes):
@@ -233,10 +276,10 @@ def tile_moe_bdx_mlp_relu2_kernel(tc, dyT, a, w2, w1, gate, offs, out):
         def quantize_da(e, h):
             codes = work.tile([P, C], U32, name="da_codes", bufs=3, align_bytes=64)
             if e < E - 1:
-                at = W2_MIXED_AT[h] + 64
+                at = W2_RAW_AT[0][(e + 1) % 2] if h else W2_MIXED_AT[0] + 64
             else:
                 at = None if h else batch_at(e) + 1024
-            scales = scale_plane("da_scales", C, 2, at)
+            scales = scale_plane("da_scales", C, 1, at)
             nc.vector.quantize_mx(
                 out=codes[:].bitcast(E5M2), scales=scales[:], in_=da_mixed[e, h][:].rearrange("p c t -> p (c t)")
             )
@@ -245,7 +288,7 @@ def tile_moe_bdx_mlp_relu2_kernel(tc, dyT, a, w2, w1, gate, offs, out):
         def input_gradient(e, tiles):
             w1_codes, w1_scales = w1_mx[e]
             for k in tiles:
-                dx = bank(J + k if e < E - 1 else k)
+                dx = bank((7, 4, 5)[k] if e < E - 1 else 0)
                 for h in range(HALVES):
                     col = h * K + k * P
                     da_codes, da_scales = da_mx[e, h]
@@ -260,97 +303,109 @@ def tile_moe_bdx_mlp_relu2_kernel(tc, dyT, a, w2, w1, gate, offs, out):
                     )
                 dx_banks[e, k] = dx
 
-        def copy_out(e, k):
-            if e == E - 2 and k == K_TILES - 1:
-                plane = placed("late_result", [P, C], F32, DA_MIXED_AT)[:]
+        def copy_out(e, k, lo=0, hi=C):
+            if lo:
+                plane = placed("late_result", [P, hi - lo], F32, DA_MIXED_AT)[:]
+            elif k == 0 and e < E - 1:
+                plane = placed("first_result", [P, C], F32, W2_MIXED_AT[1][(e + 1) % 2] + 64)[:]
             else:
-                plane = work.tile([P, C], F32, name="result", bufs=3)[:]
-            nc.scalar.activation(plane, dx_banks[e, k][:], COPY, scale=2.0)
-            results[e, k] = plane
+                plane = work.tile([P, C], F32, name="result", bufs=2)[:, lo:hi]
+            nc.scalar.activation(plane, dx_banks[e, k][:, lo:hi], COPY, scale=twos[e][:] if k == 1 and e < E - 1 else 2.0)
+            results[e, k, lo] = plane
 
-        def scatter(e, k):
-            nc.vector.tensor_copy(windows[k][:].indirect(listed(e)), results[e, k])
+        def scatter(e, k, lo=0, hi=C):
+            nc.vector.tensor_copy(windows[k][:].indirect(listed(e, lo, hi)), results[e, k, lo])
             if e == E - 1:
                 nc.sync.dma_start(out[k * P : (k + 1) * P, :], windows[k][:])
 
+        second_row = held.tile([P, 1, J], F32, name="second_row")
+        outer_rows = held.tile([P, 2, J], F32, name="outer_rows")
+        late_row = placed("late_row", [P, 1, J], F32, GATHERED_AT[2])
+        third_row = held.tile([P, J], F32, name="third_row")
+        gate_rows.update({0: outer_rows[:, 0, :], 1: second_row[:, 0, :], 2: third_row[:], 3: outer_rows[:, 1, :]})
+        load_gate_rows(nc.scalar, second_row, slice(1, 2))
+        nc.sync.dma_start(offsets[:], offs)
         load_tokens(0)
-        load_gate(0)
+        load_gate_rows(nc.sync, outer_rows, slice(0, E, E - 1))
         for t in range(1, J):
             load_tokens(t)
-        load_gate(1)
+        load_gate_rows(nc.sync, late_row, slice(2, 3))
         load_w2(0, 0)
         load_w2(0, 1)
         load_w1(0, 0)
         load_a(0, 0)
-        load_gate(2)
         load_a(0, 1)
+        load_w2(1, 0)
         load_w1(0, 1)
-        for e in range(1, E):
-            load_w2(e, 1)
-            load_w2(e, 0)
-            if e > 1:
-                load_w1(e - 1, 0)
-                load_w1(e - 1, 1)
-            load_a(e, 0)
-            load_a(e, 1)
-            if e == 1:
-                load_gate(3)
-        load_w1(E - 1, 0)
-        load_w1(E - 1, 1)
+        load_w2(1, 1)
+        load_a(1, 0)
+        load_a(1, 1)
 
-        gather(0)
-        interleave_g(0)
-        gather(1)
-        gate_on_gpsimd(1)
+        for e in (1, 0, 3):
+            spread_gate(e)
+        for e, t in ((0, 0), (1, 0), (1, 1), (0, 1)):
+            gather_plane(e, t)
+        gate_pair(1, 0)
+        gate_pair(0, 0)
+        for t in (2, 3):
+            gather_plane(0, t)
+            gather_plane(1, t)
+        gate_pair(0, 1)
+        gate_pair(1, 1)
+        nc.scalar.copy(third_row[:], late_row[:, 0, :])
         gather(2)
         quantize_g(0)
         quantize_w2(0, 0)
+        quantize_g(1)
         quantize_w2(0, 1)
+        spread_gate(2)
         gate_on_gpsimd(2)
         product_on_vector(0, 0)
         product_on_vector(0, 1)
         gather(3)
         interleave_da(0, 0)
         interleave_da(0, 1)
-        quantize_g(1)
-        quantize_w2(1, 1)
-        quantize_g(2)
-        quantize_w2(1, 0)
-        quantize_da(0, 0)
-        quantize_da(0, 1)
-        quantize_w1(0)
-        for e in range(E - 1):
-            last = e == E - 2
-            sums_to_sbuf(e + 1, [0])
+        for e in range(E):
+            last = e == E - 1
+            if e == E - 2:
+                quantize_g(E - 1, 0, C // 2)
+                quantize_g(E - 1, C // 2, C)
+            if not last:
+                quantize_w2(e + 1, 0)
+                quantize_da(e, 1)
+            if e == 0:
+                quantize_g(2)
+            quantize_da(e, 0)
+            mix_w1(e, 0, W1_HEAD, W1_HEAD_AT[e > 0])
+            mix_w1(e, W1_HEAD, HALVES * K, W1_TAIL_AT[e > 0])
+            quantize_w1(e, 0, W1_HEAD)
+            if last:
+                quantize_da(e, 1)
+            quantize_w1(e, W1_HEAD, HALVES * K)
+            if not last:
+                quantize_w2(e + 1, 1)
+            if last:
+                continue
+            load_round(e + 1)
             input_gradient(e, [0])
+            copy_out(e, 0)
             product_on_vector(e + 1, 0)
             relu_on_gpsimd(e + 1)
-            copy_out(e, 0)
-            sums_to_sbuf(e + 1, [1, 2, 3])
-            product_on_gpsimd(e + 1)
-            if not last:
+            held_back = e == E - 2
+            if not held_back:
                 gate_on_gpsimd(E - 1, e * C // 2, (e + 1) * C // 2)
+            sums_to_sbuf(e + 1, range(J))
+            product_on_gpsimd(e + 1)
             input_gradient(e, [1, 2])
             copy_out(e, 1)
-            if not last:
-                copy_out(e, 2)
+            copy_out(e, 2, 0, C // 2 if held_back else C)
             scatter(e, 0)
             scatter(e, 1)
-            if not last:
-                scatter(e, 2)
+            scatter(e, 2, 0, C // 2 if held_back else C)
             interleave_da(e + 1, 0)
-            if not last:
-                quantize_w2(e + 2, 1)
-                quantize_w2(e + 2, 0)
-                quantize_g(E - 1, e * C // 2, (e + 1) * C // 2)
-            quantize_da(e + 1, 1)
-            quantize_da(e + 1, 0)
-            quantize_w1(e + 1)
-            if last:
-                copy_out(e, 2)
-                scatter(e, 2)
-        input_gradient(E - 1, range(K_TILES))
+        copy_out(E - 2, 2, C // 2, C)
+        scatter(E - 2, 2, C // 2, C)
         for k in range(K_TILES):
+            input_gradient(E - 1, [k])
             copy_out(E - 1, k)
-        for k in range(K_TILES):
             scatter(E - 1, k)

@@ -29,7 +29,7 @@ W2_MIXED_AT = (18368, (12224, 0))
 RELU_AT = (4096, 4032)
 GATHERED_AT = (22464, 30656, 52160, 30720)
 W1_TAIL_AT = (12224, GATHERED_AT[0] + 4096)
-W1_HEAD_AT = (14272, GATHERED_AT[0])
+W1_HEAD_AT = (14272, GATHERED_AT[0], GATHERED_AT[2], GATHERED_AT[0])
 FIRST_A_AT = 38848
 DH_AT = FIRST_A_AT + 4096
 DH_SHIFT = 1024
@@ -89,7 +89,7 @@ def tile_moe_bdx_mlp_relu2_kernel(tc, dyT, a, w2, w1, gate, offs, out):
             queue.dma_start(rows[:], gate[0].rearrange("(e p c) -> p e c", p=P, c=J)[:, experts, :])
 
         def spread_gate(e):
-            spread = psum.tile([P, J, P], F32, name=f"spread{e in (1, 2)}", offset=(J + (e in (1, 2))) * BANK)
+            spread = psum.tile([P, J, P], F32, name=f"spread{e in (1, 2)}", offset=(7 if e in (1, 2) else J) * BANK)
             for c in range(J):
                 nc.tensor.transpose(spread[:, c, :], gate_rows[e][:, c : c + 1].to_broadcast([P, P]), identity[:])
             if e < E - 1:
@@ -118,11 +118,11 @@ def tile_moe_bdx_mlp_relu2_kernel(tc, dyT, a, w2, w1, gate, offs, out):
         def load_round(e):
             if e + 1 < E:
                 load_w2(e + 1, 0)
-            load_w1(e, 0)
             load_w1(e, 1)
             if e + 1 < E:
-                load_w2(e + 1, 1)
                 load_a(e + 1, 0)
+                load_w2(e + 1, 1)
+                load_w1(e + 1, 0)
                 load_a(e + 1, 1)
 
         def placed(name, shape, dtype, at):
@@ -185,7 +185,7 @@ def tile_moe_bdx_mlp_relu2_kernel(tc, dyT, a, w2, w1, gate, offs, out):
 
         def quantize_w2(e, h):
             codes = work.tile([P, P * J], U32, name="w2_codes", bufs=4, align_bytes=64)
-            scales = scale_plane("w2_scales", P * J, 2, (batch_at(e - 1), W1_HEAD_AT[e > 1])[h] if e else SECOND_GATE_AT + 512 * h)
+            scales = scale_plane("w2_scales", P * J, 2, (batch_at(e - 1), W1_HEAD_AT[e - 1])[h] if e else SECOND_GATE_AT + 512 * h)
             w2_mx[e, h] = codes, scales
             mixed = placed("w2_mixed", [P, J, P, J], BF16, ((W2_MIXED_AT[0], W2_MIXED_AT[1][e % 2]) if e else FIRST_W2_MIXED_AT)[h])
             nc.scalar.activation(
@@ -193,16 +193,17 @@ def tile_moe_bdx_mlp_relu2_kernel(tc, dyT, a, w2, w1, gate, offs, out):
             )
             nc.vector.quantize_mx(out=codes[:].bitcast(E4M3), scales=scales[:], in_=mixed[:].rearrange("p t m j -> p (t m j)"))
 
-        def mix_w1(e, lo, hi, at):
-            w1_mixed[e, lo] = placed(f"w1_mixed{hi - lo}", [P, hi - lo, J], BF16, at)
-            for h in range(HALVES):
-                first, end = max(lo, h * K), min(hi, (h + 1) * K)
-                if first < end:
-                    nc.scalar.activation(
-                        w1_mixed[e, lo][:, first - lo : end - lo, :].rearrange("p (c i) j -> p c j i", i=4),
-                        w1_raw[e, h][:, :, first - h * K : end - h * K].rearrange("p j (c i) -> p c j i", i=4),
-                        COPY,
-                    )
+        def mix_w1(e, lo, hi):
+            first = 0 if lo < W1_HEAD else W1_HEAD
+            if lo == 0:
+                w1_mixed[e, 0] = placed("w1_head", [P, W1_HEAD, J], BF16, W1_HEAD_AT[e])
+            if lo == W1_HEAD:
+                w1_mixed[e, lo] = placed("w1_tail", [P, hi - lo, J], BF16, W1_TAIL_AT[e > 0])
+            nc.scalar.activation(
+                w1_mixed[e, first][:, lo - first : hi - first, :].rearrange("p (c i) j -> p c j i", i=4),
+                w1_raw[e, lo // K][:, :, lo % K : (hi - 1) % K + 1].rearrange("p j (c i) -> p c j i", i=4),
+                COPY,
+            )
 
         def quantize_w1(e, lo, hi):
             if e not in w1_mx:
@@ -337,8 +338,9 @@ def tile_moe_bdx_mlp_relu2_kernel(tc, dyT, a, w2, w1, gate, offs, out):
         load_a(0, 1)
         load_w2(1, 0)
         load_w1(0, 1)
-        load_w2(1, 1)
         load_a(1, 0)
+        load_w2(1, 1)
+        load_w1(1, 0)
         load_a(1, 1)
 
         for e in (1, 0, 3):
@@ -363,6 +365,7 @@ def tile_moe_bdx_mlp_relu2_kernel(tc, dyT, a, w2, w1, gate, offs, out):
         product_on_vector(0, 0)
         product_on_vector(0, 1)
         gather(3)
+        mix_w1(0, 0, K)
         interleave_da(0, 0)
         interleave_da(0, 1)
         for e in range(E):
@@ -376,8 +379,8 @@ def tile_moe_bdx_mlp_relu2_kernel(tc, dyT, a, w2, w1, gate, offs, out):
             if e == 0:
                 quantize_g(2)
             quantize_da(e, 0)
-            mix_w1(e, 0, W1_HEAD, W1_HEAD_AT[e > 0])
-            mix_w1(e, W1_HEAD, HALVES * K, W1_TAIL_AT[e > 0])
+            mix_w1(e, K, W1_HEAD)
+            mix_w1(e, W1_HEAD, HALVES * K)
             quantize_w1(e, 0, W1_HEAD)
             if last:
                 quantize_da(e, 1)
@@ -386,6 +389,7 @@ def tile_moe_bdx_mlp_relu2_kernel(tc, dyT, a, w2, w1, gate, offs, out):
                 quantize_w2(e + 1, 1)
             if last:
                 continue
+            mix_w1(e + 1, 0, K)
             load_round(e + 1)
             input_gradient(e, [0])
             copy_out(e, 0)

@@ -28,18 +28,20 @@ COPY = mybir.ActivationFunctionType.Copy
 W2_MIXED_AT = (18368, (12224, 0))
 RELU_AT = (4096, 4032)
 GATHERED_AT = (22464, 30656, 52160, 30720)
-W1_TAIL_AT = (12224, GATHERED_AT[0] + 4096)
-W1_HEAD_AT = (14272, GATHERED_AT[0], GATHERED_AT[2], GATHERED_AT[0])
 FIRST_A_AT = 38848
 DH_AT = FIRST_A_AT + 4096
 DH_SHIFT = 1024
 FIRST_GATE_AT = GATHERED_AT[2] + 8192
 SECOND_GATE_AT = FIRST_GATE_AT + 2048
-DA_MIXED_AT = SECOND_GATE_AT + 2048 + 192
+DA_MIXED_AT = SECOND_GATE_AT + 2048
 G_MIXED_AT = (3968, 8064, DA_MIXED_AT + 8192)
-W2_RAW_AT = ((G_MIXED_AT[2] + 4608, G_MIXED_AT[2] + 13312), (G_MIXED_AT[2] + 21504, G_MIXED_AT[2] + 33728))
-DA_AT = (W2_RAW_AT[1][0] + 8128, W2_RAW_AT[1][0] + 8192)
-A_RAW_AT = (W2_RAW_AT[1][1] + 8192, W2_RAW_AT[1][1] + 18432)
+TWOS_AT = G_MIXED_AT[2] + 4096
+W2_RAW_AT = (TWOS_AT + 2048, TWOS_AT + 18432)
+A_RAW_AT = (W2_RAW_AT[1] + 16384, W2_RAW_AT[1] + 26624)
+W1_TAIL_AT = A_RAW_AT[1] + 8192
+DA_AT = W1_TAIL_AT + 1984
+W1_RAW_AT = (DA_AT + 4096, DA_AT + 10240)
+W1_HEAD_AT = (W2_RAW_AT[0] + 2048, GATHERED_AT[0], GATHERED_AT[2], GATHERED_AT[0])
 LAST_G_AT = (A_RAW_AT[1] - 2048, A_RAW_AT[0])
 FIRST_W2_MIXED_AT = (W2_MIXED_AT[0], G_MIXED_AT[2] - 4032)
 W1_HEAD = 512
@@ -60,18 +62,18 @@ def tile_moe_bdx_mlp_relu2_kernel(tc, dyT, a, w2, w1, gate, offs, out):
         windows = [held.tile([P, T], F32, name=f"window{k}", tag=f"columns{k}") for k in range(K_TILES)]
 
         identity = held.tile([P, P], F32, name="identity")
-        ones = held.tile([P, Q], F32, name="ones")
+        steps = held.tile([P, Q], F32, name="steps")
         column = held.tile([P, Q], F32, name="column", align_bytes=64)
         row = held.tile([P, Q], F32, name="row", align_bytes=64)
         nc.vector.memset(identity[:], 0.0)
-        nc.vector.memset(ones[:], 1.0)
-        nc.vector.tensor_tensor_scan(column[:], ones[:], ones[:], 0.0, MULT, ADD)
+        nc.vector.memset(steps[:], 1.0)
+        nc.vector.tensor_tensor_scan(column[:], steps[:], steps[:], 0.0, MULT, ADD)
         nc.vector.transpose(row[:], column[:])
         for first in range(0, P, Q):
             rows = slice(first, first + Q)
             nc.vector.tensor_tensor(identity[rows, rows], column[rows, :], row[rows, :], mybir.AluOpType.is_equal)
-        gate_rows, w1_mixed = {}, {}
-        twos = [shared.tile([P, 1], F32, name=f"two{e}", align_bytes=64, offset=DA_MIXED_AT - 64 * (e + 1)) for e in range(E - 1)]
+        gate_rows, w1_mixed, w2_mixed = {}, {}, {}
+        twos = [shared.tile([P, 1], F32, name=f"two{e}", align_bytes=64, offset=TWOS_AT + 512 * e) for e in range(E - 1)]
         for two in twos:
             nc.vector.memset(two[:], 2.0)
         dy_rows = dyT.rearrange("(p t) s -> p t s", t=J)
@@ -93,15 +95,14 @@ def tile_moe_bdx_mlp_relu2_kernel(tc, dyT, a, w2, w1, gate, offs, out):
             for c in range(J):
                 nc.tensor.transpose(spread[:, c, :], gate_rows[e][:, c : c + 1].to_broadcast([P, P]), identity[:])
             if e < E - 1:
-                gates[e] = placed("gate", [P, C], F32, (FIRST_GATE_AT, SECOND_GATE_AT, W2_RAW_AT[1][0])[e])
+                gates[e] = placed("gate", [P, C], F32, (FIRST_GATE_AT, SECOND_GATE_AT, W2_RAW_AT[0])[e])
             else:
                 gates[e] = held.tile([P, C], F32, name="last_gate")
             nc.scalar.activation(gates[e][:].rearrange("m (p c) -> m p c", c=J), spread[:].rearrange("m c p -> m p c"), COPY)
 
-        def load_w2(e, h):
-            w2_raw[e, h] = placed("w2_raw", [P, J, P * J], F32, W2_RAW_AT[h][e % 2] - (64 if e < 2 and h == 0 else 0))
-            rows = w2[e].rearrange("(p j) i -> p j i", j=J)
-            nc.sync.dma_start(w2_raw[e, h][:], rows[:, :, h * P * J : (h + 1) * P * J])
+        def load_w2(e):
+            w2_raw[e] = placed("w2_raw", [P, J, H], F32, W2_RAW_AT[e % 2] - (0 if e else 64))
+            nc.sync.dma_start(w2_raw[e][:], w2[e].rearrange("(p j) i -> p j i", j=J))
 
         def load_a(e, h):
             if h:
@@ -111,17 +112,19 @@ def tile_moe_bdx_mlp_relu2_kernel(tc, dyT, a, w2, w1, gate, offs, out):
             nc.sync.dma_start(a_raw[e, h][:], a_rows[h][:, :, e * C : (e + 1) * C])
 
         def load_w1(e, h):
-            w1_raw[e, h] = work.tile([P, J, K], F32, name="w1_raw", bufs=4)
+            if h:
+                w1_raw[e, h] = placed("w1_raw", [P, J, K], F32, W1_RAW_AT[e % 2])
+            else:
+                w1_raw[e, h] = work.tile([P, J, K], F32, name="w1_raw", bufs=2)
             nc.sync.dma_start(w1_raw[e, h][:], w1[e].rearrange("(h p j) k -> h p j k", p=P, j=J)[h])
 
 
         def load_round(e):
             if e + 1 < E:
-                load_w2(e + 1, 0)
+                load_w2(e + 1)
+                load_a(e + 1, 0)
             load_w1(e, 1)
             if e + 1 < E:
-                load_a(e + 1, 0)
-                load_w2(e + 1, 1)
                 load_w1(e + 1, 0)
                 load_a(e + 1, 1)
 
@@ -177,28 +180,34 @@ def tile_moe_bdx_mlp_relu2_kernel(tc, dyT, a, w2, w1, gate, offs, out):
         def quantize_g(e, lo=0, hi=C):
             if lo == 0:
                 codes = work.tile([P, C], U32, name="g_codes", bufs=3, align_bytes=64)
-                g_mx[e] = codes, scale_plane("g_scales", C, 1, {0: SECOND_GATE_AT + 1024, 1: W2_RAW_AT[0][0] - 512, 2: W2_RAW_AT[0][1] - 512, 3: batch_at(2) + 512}[e])
+                g_mx[e] = codes, scale_plane("g_scales", C, 1, {0: SECOND_GATE_AT + 1024, 1: W2_RAW_AT[0] - 512, 2: FIRST_A_AT + 2880, 3: batch_at(2) + 512}[e])
             codes, scales = g_mx[e]
             nc.vector.quantize_mx(
                 out=codes[:, lo:hi].bitcast(E5M2), scales=scales[:, lo:hi], in_=g_mixed[e, lo][:].rearrange("p c t -> p (c t)")
             )
 
+        def mix_w2(e, h):
+            at = (W2_MIXED_AT[0], W2_MIXED_AT[1][e % 2]) if e else FIRST_W2_MIXED_AT
+            w2_mixed[e, h] = placed("w2_mixed", [P, J, P, J], BF16, at[h])
+            nc.scalar.activation(
+                w2_mixed[e, h][:].rearrange("p t m j -> p m j t"),
+                w2_raw[e][:, :, h * P * J : (h + 1) * P * J].rearrange("p j (m t) -> p m j t", t=J),
+                COPY,
+                scale=twos[e - 1][:] if e and h == 0 else 2.0,
+            )
+
         def quantize_w2(e, h):
             codes = work.tile([P, P * J], U32, name="w2_codes", bufs=4, align_bytes=64)
-            scales = scale_plane("w2_scales", P * J, 2, (batch_at(e - 1), W1_HEAD_AT[e - 1])[h] if e else SECOND_GATE_AT + 512 * h)
+            scales = scale_plane("w2_scales", P * J, 2, (batch_at(e - 1), W1_RAW_AT[(e - 1) % 2])[h] if e else SECOND_GATE_AT + 512 * h)
             w2_mx[e, h] = codes, scales
-            mixed = placed("w2_mixed", [P, J, P, J], BF16, ((W2_MIXED_AT[0], W2_MIXED_AT[1][e % 2]) if e else FIRST_W2_MIXED_AT)[h])
-            nc.scalar.activation(
-                mixed[:].rearrange("p t m j -> p m j t"), w2_raw[e, h][:].rearrange("p j (m t) -> p m j t", t=J), COPY
-            )
-            nc.vector.quantize_mx(out=codes[:].bitcast(E4M3), scales=scales[:], in_=mixed[:].rearrange("p t m j -> p (t m j)"))
+            nc.vector.quantize_mx(out=codes[:].bitcast(E4M3), scales=scales[:], in_=w2_mixed[e, h][:].rearrange("p t m j -> p (t m j)"))
 
         def mix_w1(e, lo, hi):
             first = 0 if lo < W1_HEAD else W1_HEAD
             if lo == 0:
                 w1_mixed[e, 0] = placed("w1_head", [P, W1_HEAD, J], BF16, W1_HEAD_AT[e])
             if lo == W1_HEAD:
-                w1_mixed[e, lo] = placed("w1_tail", [P, hi - lo, J], BF16, W1_TAIL_AT[e > 0])
+                w1_mixed[e, lo] = placed("w1_tail", [P, hi - lo, J], BF16, W1_TAIL_AT)
             nc.scalar.activation(
                 w1_mixed[e, first][:, lo - first : hi - first, :].rearrange("p (c i) j -> p c j i", i=4),
                 w1_raw[e, lo // K][:, :, lo % K : (hi - 1) % K + 1].rearrange("p j (c i) -> p c j i", i=4),
@@ -231,13 +240,13 @@ def tile_moe_bdx_mlp_relu2_kernel(tc, dyT, a, w2, w1, gate, offs, out):
             return dh
 
         def product_on_vector(e, h):
-            da = placed("da_planes", [P, J, C], BF16, DA_AT[e % 2] if e else GATHERED_AT[0] + 4096 * h - 64)
+            da = placed("da_planes", [P, J, C], BF16, DA_AT if e else (W2_RAW_AT[0] + 6144, GATHERED_AT[0] + 4096)[h])
             for t in range(J):
                 nc.vector.scalar_tensor_tensor(da[:, t, :], a_raw[e, h][:, t, :], 0.0, hidden_sums(e, h, t)[:], MAX, MULT)
             da_planes[e, h] = da
 
         def interleave_da(e, h):
-            da_mixed[e, h] = placed("da_mixed", [P, C, J], BF16, DA_MIXED_AT + 4096 if h else DA_MIXED_AT - 64 * e)
+            da_mixed[e, h] = placed("da_mixed", [P, C, J], BF16, DA_MIXED_AT + 4096 * h)
             if h:
                 nc.gpsimd.tensor_scalar(
                     da_mixed[e, h][:].rearrange("p (c i) t -> p c t i", i=2),
@@ -277,7 +286,7 @@ def tile_moe_bdx_mlp_relu2_kernel(tc, dyT, a, w2, w1, gate, offs, out):
         def quantize_da(e, h):
             codes = work.tile([P, C], U32, name="da_codes", bufs=3, align_bytes=64)
             if e < E - 1:
-                at = W2_RAW_AT[0][(e + 1) % 2] if h else W2_MIXED_AT[0] + 64
+                at = TWOS_AT + 512 * e if h else W2_MIXED_AT[0] + 64
             else:
                 at = None if h else batch_at(e) + 1024
             scales = scale_plane("da_scales", C, 1, at)
@@ -311,7 +320,7 @@ def tile_moe_bdx_mlp_relu2_kernel(tc, dyT, a, w2, w1, gate, offs, out):
                 plane = placed("first_result", [P, C], F32, W2_MIXED_AT[1][(e + 1) % 2] + 64)[:]
             else:
                 plane = work.tile([P, C], F32, name="result", bufs=2)[:, lo:hi]
-            nc.scalar.activation(plane, dx_banks[e, k][:, lo:hi], COPY, scale=twos[e][:] if k == 1 and e < E - 1 else 2.0)
+            nc.scalar.activation(plane, dx_banks[e, k][:, lo:hi], COPY)
             results[e, k, lo] = plane
 
         def scatter(e, k, lo=0, hi=C):
@@ -331,15 +340,13 @@ def tile_moe_bdx_mlp_relu2_kernel(tc, dyT, a, w2, w1, gate, offs, out):
         for t in range(1, J):
             load_tokens(t)
         load_gate_rows(nc.sync, late_row, slice(2, 3))
-        load_w2(0, 0)
-        load_w2(0, 1)
+        load_w2(0)
         load_w1(0, 0)
         load_a(0, 0)
         load_a(0, 1)
-        load_w2(1, 0)
-        load_w1(0, 1)
+        load_w2(1)
         load_a(1, 0)
-        load_w2(1, 1)
+        load_w1(0, 1)
         load_w1(1, 0)
         load_a(1, 1)
 
@@ -356,11 +363,13 @@ def tile_moe_bdx_mlp_relu2_kernel(tc, dyT, a, w2, w1, gate, offs, out):
         gate_pair(1, 1)
         nc.scalar.copy(third_row[:], late_row[:, 0, :])
         gather(2)
+        mix_w2(0, 0)
+        mix_w2(0, 1)
+        spread_gate(2)
         quantize_g(0)
         quantize_w2(0, 0)
         quantize_g(1)
         quantize_w2(0, 1)
-        spread_gate(2)
         gate_on_gpsimd(2)
         product_on_vector(0, 0)
         product_on_vector(0, 1)
@@ -368,16 +377,17 @@ def tile_moe_bdx_mlp_relu2_kernel(tc, dyT, a, w2, w1, gate, offs, out):
         mix_w1(0, 0, K)
         interleave_da(0, 0)
         interleave_da(0, 1)
+        quantize_g(2)
         for e in range(E):
             last = e == E - 1
             if e == E - 2:
                 quantize_g(E - 1, 0, C // 2)
                 quantize_g(E - 1, C // 2, C)
             if not last:
+                mix_w2(e + 1, 0)
+                mix_w2(e + 1, 1)
                 quantize_w2(e + 1, 0)
                 quantize_da(e, 1)
-            if e == 0:
-                quantize_g(2)
             quantize_da(e, 0)
             mix_w1(e, K, W1_HEAD)
             mix_w1(e, W1_HEAD, HALVES * K)

@@ -36,7 +36,7 @@ SECOND_GATE_AT = FIRST_GATE_AT + 2048
 DA_MIXED_AT = SECOND_GATE_AT + 2048
 G_MIXED_AT = (3968, 8064, DA_MIXED_AT + 8192)
 TWOS_AT = G_MIXED_AT[2] + 4096
-W2_RAW_AT = (TWOS_AT + 2048, TWOS_AT + 18432)
+W2_RAW_AT = (TWOS_AT + 2560, TWOS_AT + 18944)
 A_RAW_AT = (W2_RAW_AT[1] + 16384, W2_RAW_AT[1] + 26624)
 W1_TAIL_AT = A_RAW_AT[1] + 8192
 DA_AT = W1_TAIL_AT + 1984
@@ -73,7 +73,7 @@ def tile_moe_bdx_mlp_relu2_kernel(tc, dyT, a, w2, w1, gate, offs, out):
             rows = slice(first, first + Q)
             nc.vector.tensor_tensor(identity[rows, rows], column[rows, :], row[rows, :], mybir.AluOpType.is_equal)
         gate_rows, w1_mixed, w2_mixed = {}, {}, {}
-        twos = [shared.tile([P, 1], F32, name=f"two{e}", align_bytes=64, offset=TWOS_AT + 512 * e) for e in range(E - 1)]
+        twos = [shared.tile([P, 32], F32, name=f"two{e}", align_bytes=64, offset=TWOS_AT + (448, 1024, 1536)[e]) for e in range(E - 1)]
         for two in twos:
             nc.vector.memset(two[:], 2.0)
         dy_rows = dyT.rearrange("(p t) s -> p t s", t=J)
@@ -180,7 +180,7 @@ def tile_moe_bdx_mlp_relu2_kernel(tc, dyT, a, w2, w1, gate, offs, out):
         def quantize_g(e, lo=0, hi=C):
             if lo == 0:
                 codes = work.tile([P, C], U32, name="g_codes", bufs=3, align_bytes=64)
-                g_mx[e] = codes, scale_plane("g_scales", C, 1, {0: SECOND_GATE_AT + 1024, 1: W2_RAW_AT[0] - 512, 2: FIRST_A_AT + 2880, 3: batch_at(2) + 512}[e])
+                g_mx[e] = codes, scale_plane("g_scales", C, 1, {0: SECOND_GATE_AT + 1024, 1: W2_RAW_AT[0] - 512, 2: TWOS_AT, 3: batch_at(2) + 512}[e])
             codes, scales = g_mx[e]
             nc.vector.quantize_mx(
                 out=codes[:, lo:hi].bitcast(E5M2), scales=scales[:, lo:hi], in_=g_mixed[e, lo][:].rearrange("p c t -> p (c t)")
@@ -193,7 +193,7 @@ def tile_moe_bdx_mlp_relu2_kernel(tc, dyT, a, w2, w1, gate, offs, out):
                 w2_mixed[e, h][:].rearrange("p t m j -> p m j t"),
                 w2_raw[e][:, :, h * P * J : (h + 1) * P * J].rearrange("p j (m t) -> p m j t", t=J),
                 COPY,
-                scale=twos[e - 1][:] if e and h == 0 else 2.0,
+                scale=twos[e - 1][:, 0:1] if e and h == 0 else 2.0,
             )
 
         def quantize_w2(e, h):
@@ -247,22 +247,14 @@ def tile_moe_bdx_mlp_relu2_kernel(tc, dyT, a, w2, w1, gate, offs, out):
 
         def interleave_da(e, h):
             da_mixed[e, h] = placed("da_mixed", [P, C, J], BF16, DA_MIXED_AT + 4096 * h)
-            if h:
-                nc.gpsimd.tensor_scalar(
-                    da_mixed[e, h][:].rearrange("p (c i) t -> p c t i", i=2),
-                    da_planes[e, h][:].rearrange("p t (c i) -> p c t i", i=2),
-                    1.0,
-                    0.0,
-                    MULT,
-                    ADD,
-                )
-            else:
-                for slots in (slice(0, C // 2), slice(C // 2, C)):
-                    nc.scalar.activation(
-                        da_mixed[e, h][:, slots, :].rearrange("p (c i) t -> p c t i", i=8),
-                        da_planes[e, h][:, :, slots].rearrange("p t (c i) -> p c t i", i=8),
-                        COPY,
-                    )
+            for slots in (slice(0, C // 2), slice(C // 2, C)):
+                to, source = da_mixed[e, h][:, slots, :], da_planes[e, h][:, :, slots]
+                if h and slots.start:
+                    to, source = to.rearrange("p (c i) t -> p c t i", i=2), source.rearrange("p t (c i) -> p c t i", i=2)
+                    nc.gpsimd.tensor_scalar(to, source, 1.0, 0.0, MULT, ADD)
+                else:
+                    to, source = to.rearrange("p (c i) t -> p c t i", i=8), source.rearrange("p t (c i) -> p c t i", i=8)
+                    nc.scalar.activation(to, source, COPY)
 
         def relu_on_gpsimd(e):
             relu_a[e] = placed("relu_a", [P, C // 2, J, 2], F32, RELU_AT[e % 2])
@@ -286,7 +278,7 @@ def tile_moe_bdx_mlp_relu2_kernel(tc, dyT, a, w2, w1, gate, offs, out):
         def quantize_da(e, h):
             codes = work.tile([P, C], U32, name="da_codes", bufs=3, align_bytes=64)
             if e < E - 1:
-                at = TWOS_AT + 512 * e if h else W2_MIXED_AT[0] + 64
+                at = TWOS_AT + 512 * (e + 1) if h else W2_MIXED_AT[0] + 64
             else:
                 at = None if h else batch_at(e) + 1024
             scales = scale_plane("da_scales", C, 1, at)
@@ -377,7 +369,6 @@ def tile_moe_bdx_mlp_relu2_kernel(tc, dyT, a, w2, w1, gate, offs, out):
         mix_w1(0, 0, K)
         interleave_da(0, 0)
         interleave_da(0, 1)
-        quantize_g(2)
         for e in range(E):
             last = e == E - 1
             if e == E - 2:
@@ -388,6 +379,8 @@ def tile_moe_bdx_mlp_relu2_kernel(tc, dyT, a, w2, w1, gate, offs, out):
                 mix_w2(e + 1, 1)
                 quantize_w2(e + 1, 0)
                 quantize_da(e, 1)
+            if e == 0:
+                quantize_g(2)
             quantize_da(e, 0)
             mix_w1(e, K, W1_HEAD)
             mix_w1(e, W1_HEAD, HALVES * K)

@@ -25,8 +25,11 @@ MIN = mybir.AluOpType.min
 F32_MAX = 3.4028234663852886e38
 COPY = mybir.ActivationFunctionType.Copy
 
-W2_MIXED_AT = (18368, (12224, 0))
-RELU_AT = (4096, 4032)
+BANK = 2048
+W1_HEAD = 512
+
+W2_MIXED_AT = (18368, (12224, 0, 12160))
+RELU_AT = (3968, 4096)
 GATHERED_AT = (22464, 30656, 52160, 30720)
 FIRST_A_AT = 38848
 DH_AT = FIRST_A_AT + 4096
@@ -37,15 +40,13 @@ DA_MIXED_AT = SECOND_GATE_AT + 2048
 G_MIXED_AT = (3968, 8064, DA_MIXED_AT + 8192)
 TWOS_AT = G_MIXED_AT[2] + 4096
 W2_RAW_AT = (TWOS_AT + 2560, TWOS_AT + 18944)
-A_RAW_AT = (W2_RAW_AT[1] + 16384, W2_RAW_AT[1] + 26624)
+A_RAW_AT = (W2_RAW_AT[1] + 16384, W2_RAW_AT[1] + 24576)
 W1_TAIL_AT = A_RAW_AT[1] + 8192
 DA_AT = W1_TAIL_AT + 1984
 W1_RAW_AT = (DA_AT + 4096, DA_AT + 10240)
 W1_HEAD_AT = (W2_RAW_AT[0] + 2048, GATHERED_AT[0], GATHERED_AT[2], GATHERED_AT[0])
-LAST_G_AT = (A_RAW_AT[1] - 2048, A_RAW_AT[0])
+LAST_G_AT = (16256, A_RAW_AT[0])
 FIRST_W2_MIXED_AT = (W2_MIXED_AT[0], G_MIXED_AT[2] - 4032)
-W1_HEAD = 512
-BANK = 2048
 
 
 def tile_moe_bdx_mlp_relu2_kernel(tc, dyT, a, w2, w1, gate, offs, out):
@@ -70,19 +71,44 @@ def tile_moe_bdx_mlp_relu2_kernel(tc, dyT, a, w2, w1, gate, offs, out):
         nc.vector.tensor_tensor_scan(column[:], steps[:], steps[:], 0.0, MULT, ADD)
         nc.vector.transpose(row[:], column[:])
         for first in range(0, P, Q):
-            rows = slice(first, first + Q)
-            nc.vector.tensor_tensor(identity[rows, rows], column[rows, :], row[rows, :], mybir.AluOpType.is_equal)
-        gate_rows, w1_mixed, w2_mixed = {}, {}, {}
-        twos = [shared.tile([P, 32], F32, name=f"two{e}", align_bytes=64, offset=TWOS_AT + (448, 1024, 1536)[e]) for e in range(E - 1)]
+            square = slice(first, first + Q)
+            nc.vector.tensor_tensor(identity[square, square], column[square, :], row[square, :], mybir.AluOpType.is_equal)
+
+        twos = [
+            shared.tile([P, 32], F32, name=f"two{e}", align_bytes=64, offset=TWOS_AT + at) for e, at in enumerate((448, 1024, 1536))
+        ]
         for two in twos:
-            nc.vector.memset(two[:], 2.0)
+            nc.vector.memset(two[:, 0:1], 2.0)
+
         dy_rows = dyT.rearrange("(p t) s -> p t s", t=J)
         a_rows = a.rearrange("(h p t) s -> h p t s", p=P, t=J)
-        w2_raw, a_raw, w1_raw, gathered, g_mx, w2_mx, w1_mx, da_mx, dx_banks, results = {}, {}, {}, {}, {}, {}, {}, {}, {}, {}
-        da_planes, da_mixed, relu_a, dh_planes, g_mixed = {}, {}, {}, {}, {}
+        w2_raw, a_raw, w1_raw, gathered, gate_rows = {}, {}, {}, {}, {}
+        g_mixed, w2_mixed, w1_mixed, da_mixed = {}, {}, {}, {}
+        g_mx, w2_mx, w1_mx, da_mx = {}, {}, {}, {}
+        da_planes, dh_planes, relu_a, dx_banks, results = {}, {}, {}, {}, {}
+
+        def placed(name, shape, dtype, at):
+            return shared.tile(shape, dtype, name=f"{name}_at{at}", align_bytes=64, offset=at)
+
+        def bank(b):
+            return psum.tile([P, C], F32, name=f"bank{b}", offset=b * BANK)
+
+        def batch_at(e):
+            if e == 0:
+                return FIRST_A_AT + 64
+            return DH_AT if e % 2 else DH_AT + 8192
 
         def listed(e, lo=0, hi=C):
             return offsets[:, (e * C + lo) // 16 : (e * C + hi) // 16]
+
+        def in_pairs(planes):
+            return planes.rearrange("p t (c i) -> p c t i", i=2)
+
+        def mixed_in_pairs(mixed):
+            return mixed.rearrange("p (c i) t -> p c t i", i=2)
+
+        def gate_in_pairs(e, lo, hi, planes):
+            return gates[e][:, lo:hi].rearrange("p (c i) -> p c i", i=2).unsqueeze(2).to_broadcast([P, (hi - lo) // 2, planes, 2])
 
         def load_tokens(t):
             nc.sync.dma_start(tokens[t][:], dy_rows[:, t, :])
@@ -90,34 +116,23 @@ def tile_moe_bdx_mlp_relu2_kernel(tc, dyT, a, w2, w1, gate, offs, out):
         def load_gate_rows(queue, rows, experts):
             queue.dma_start(rows[:], gate[0].rearrange("(e p c) -> p e c", p=P, c=J)[:, experts, :])
 
-        def spread_gate(e):
-            spread = psum.tile([P, J, P], F32, name=f"spread{e in (1, 2)}", offset=(7 if e in (1, 2) else J) * BANK)
-            for c in range(J):
-                nc.tensor.transpose(spread[:, c, :], gate_rows[e][:, c : c + 1].to_broadcast([P, P]), identity[:])
-            if e < E - 1:
-                gates[e] = placed("gate", [P, C], F32, (FIRST_GATE_AT, SECOND_GATE_AT, W2_RAW_AT[0])[e])
-            else:
-                gates[e] = held.tile([P, C], F32, name="last_gate")
-            nc.scalar.activation(gates[e][:].rearrange("m (p c) -> m p c", c=J), spread[:].rearrange("m c p -> m p c"), COPY)
-
         def load_w2(e):
             w2_raw[e] = placed("w2_raw", [P, J, H], F32, W2_RAW_AT[e % 2] - (0 if e else 64))
             nc.sync.dma_start(w2_raw[e][:], w2[e].rearrange("(p j) i -> p j i", j=J))
 
         def load_a(e, h):
             if h:
-                a_raw[e, h] = placed("a_raw", [P, J, C], F32, (FIRST_A_AT, A_RAW_AT[1] - 64, A_RAW_AT[0], A_RAW_AT[1])[e])
+                a_raw[e, h] = placed("a_raw", [P, J, C], F32, A_RAW_AT[e % 2] if e else FIRST_A_AT)
             else:
-                a_raw[e, h] = work.tile([P, J, C], F32, name="a_raw", bufs=2)
+                a_raw[e, h] = work.tile([P, J, C], F32, name="a_raw")
             nc.sync.dma_start(a_raw[e, h][:], a_rows[h][:, :, e * C : (e + 1) * C])
 
         def load_w1(e, h):
             if h:
                 w1_raw[e, h] = placed("w1_raw", [P, J, K], F32, W1_RAW_AT[e % 2])
             else:
-                w1_raw[e, h] = work.tile([P, J, K], F32, name="w1_raw", bufs=2)
+                w1_raw[e, h] = work.tile([P, J, K], F32, name="w1_raw")
             nc.sync.dma_start(w1_raw[e, h][:], w1[e].rearrange("(h p j) k -> h p j k", p=P, j=J)[h])
-
 
         def load_round(e):
             if e + 1 < E:
@@ -128,21 +143,15 @@ def tile_moe_bdx_mlp_relu2_kernel(tc, dyT, a, w2, w1, gate, offs, out):
                 load_w1(e + 1, 0)
                 load_a(e + 1, 1)
 
-        def placed(name, shape, dtype, at):
-            return shared.tile(shape, dtype, name=f"{name}_at{at}", align_bytes=64, offset=at)
-
-        def bank(b):
-            return psum.tile([P, C], F32, name=f"bank{b}", offset=b * BANK)
-
-        def scale_plane(name, width, bufs, at):
-            if at is None:
-                return work.tile([P, width], U8, name=name, bufs=bufs, align_bytes=64)
-            return placed(name, [P, width], U8, at)
-
-        def batch_at(e):
-            if e == 0:
-                return FIRST_A_AT + 64
-            return DH_AT if e % 2 else DH_AT + 8192
+        def spread_gate(e):
+            spread = psum.tile([P, J, P], F32, name=f"spread{e in (1, 2)}", offset=(7 if e in (1, 2) else J) * BANK)
+            for c in range(J):
+                nc.tensor.transpose(spread[:, c, :], gate_rows[e][:, c : c + 1].to_broadcast([P, P]), identity[:])
+            if e < E - 1:
+                gates[e] = placed("gate", [P, C], F32, (FIRST_GATE_AT, SECOND_GATE_AT, W2_RAW_AT[0])[e])
+            else:
+                gates[e] = held.tile([P, C], F32, name="last_gate")
+            nc.scalar.activation(gates[e][:].rearrange("m (p c) -> m p c", c=J), spread[:].rearrange("m c p -> m p c"), COPY)
 
         def gather(e):
             gathered[e] = placed("gathered", [P, J, C], F32, GATHERED_AT[e])
@@ -161,33 +170,31 @@ def tile_moe_bdx_mlp_relu2_kernel(tc, dyT, a, w2, w1, gate, offs, out):
         def gate_pair(e, u):
             if u == 0:
                 g_mixed[e, 0] = placed("g_mixed", [P, C, J], BF16, G_MIXED_AT[e])
-            to = g_mixed[e, 0][:, :, 2 * u : 2 * u + 2].rearrange("p (c i) t -> p c t i", i=2)
-            source = gathered[e, u][:].rearrange("p t (c i) -> p c t i", i=2)
+            to = mixed_in_pairs(g_mixed[e, 0][:, :, 2 * u : 2 * u + 2])
             if (e, u) == (1, 0):
-                nc.scalar.activation(to, source, COPY)
+                nc.scalar.activation(to, in_pairs(gathered[e, u][:]), COPY)
             else:
-                nc.gpsimd.tensor_tensor(to, source, gates[e][:].rearrange("p (c i) -> p c i", i=2).unsqueeze(2).to_broadcast([P, C // 2, 2, 2]), MULT)
+                nc.gpsimd.tensor_tensor(to, in_pairs(gathered[e, u][:]), gate_in_pairs(e, 0, C, 2), MULT)
 
         def gate_on_gpsimd(e, lo=0, hi=C):
-            g_mixed[e, lo] = placed(f"g_mixed{hi - lo}", [P, hi - lo, J], BF16, G_MIXED_AT[e] if e < E - 1 else LAST_G_AT[lo // (C // 2)])
+            at = G_MIXED_AT[e] if e < E - 1 else LAST_G_AT[lo // (C // 2)]
+            g_mixed[e, lo] = placed(f"g_mixed{hi - lo}", [P, hi - lo, J], BF16, at)
             nc.gpsimd.tensor_tensor(
-                g_mixed[e, lo][:].rearrange("p (c i) t -> p c t i", i=2),
-                gathered[e][:, :, lo:hi].rearrange("p t (c i) -> p c t i", i=2),
-                gates[e][:, lo:hi].rearrange("p (c i) -> p c i", i=2).unsqueeze(2).to_broadcast([P, (hi - lo) // 2, J, 2]),
-                MULT,
+                mixed_in_pairs(g_mixed[e, lo][:]), in_pairs(gathered[e][:, :, lo:hi]), gate_in_pairs(e, lo, hi, J), MULT
             )
 
         def quantize_g(e, lo=0, hi=C):
             if lo == 0:
                 codes = work.tile([P, C], U32, name="g_codes", bufs=3, align_bytes=64)
-                g_mx[e] = codes, scale_plane("g_scales", C, 1, {0: SECOND_GATE_AT + 1024, 1: W2_RAW_AT[0] - 512, 2: TWOS_AT, 3: batch_at(2) + 512}[e])
+                at = (SECOND_GATE_AT + 1024, W2_RAW_AT[0] - 512, TWOS_AT, batch_at(2) + 512)[e]
+                g_mx[e] = codes, placed("g_scales", [P, C], U8, at)
             codes, scales = g_mx[e]
             nc.vector.quantize_mx(
                 out=codes[:, lo:hi].bitcast(E5M2), scales=scales[:, lo:hi], in_=g_mixed[e, lo][:].rearrange("p c t -> p (c t)")
             )
 
         def mix_w2(e, h):
-            at = (W2_MIXED_AT[0], W2_MIXED_AT[1][e % 2]) if e else FIRST_W2_MIXED_AT
+            at = (W2_MIXED_AT[0], W2_MIXED_AT[1][e - 1]) if e else FIRST_W2_MIXED_AT
             w2_mixed[e, h] = placed("w2_mixed", [P, J, P, J], BF16, at[h])
             nc.scalar.activation(
                 w2_mixed[e, h][:].rearrange("p t m j -> p m j t"),
@@ -198,7 +205,8 @@ def tile_moe_bdx_mlp_relu2_kernel(tc, dyT, a, w2, w1, gate, offs, out):
 
         def quantize_w2(e, h):
             codes = work.tile([P, P * J], U32, name="w2_codes", bufs=4, align_bytes=64)
-            scales = scale_plane("w2_scales", P * J, 2, (batch_at(e - 1), W1_RAW_AT[(e - 1) % 2])[h] if e else SECOND_GATE_AT + 512 * h)
+            at = (batch_at(e - 1), W1_RAW_AT[(e - 1) % 2])[h] if e else SECOND_GATE_AT + 512 * h
+            scales = placed("w2_scales", [P, P * J], U8, at)
             w2_mx[e, h] = codes, scales
             nc.vector.quantize_mx(out=codes[:].bitcast(E4M3), scales=scales[:], in_=w2_mixed[e, h][:].rearrange("p t m j -> p (t m j)"))
 
@@ -215,9 +223,10 @@ def tile_moe_bdx_mlp_relu2_kernel(tc, dyT, a, w2, w1, gate, offs, out):
             )
 
         def quantize_w1(e, lo, hi):
-            if e not in w1_mx:
+            if lo == 0:
                 codes = work.tile([P, HALVES * K], U32, name="w1_codes", align_bytes=64)
-                w1_mx[e] = codes, scale_plane("w1_scales", HALVES * K, 2, W2_MIXED_AT[0] + 1088 if e < E - 1 else batch_at(e) + 1536)
+                at = W2_MIXED_AT[0] + 1088 if e < E - 1 else batch_at(e) + 1536
+                w1_mx[e] = codes, placed("w1_scales", [P, HALVES * K], U8, at)
             codes, scales = w1_mx[e]
             nc.vector.quantize_mx(
                 out=codes[:, lo:hi].bitcast(E4M3), scales=scales[:, lo:hi], in_=w1_mixed[e, lo][:].rearrange("p c j -> p (c j)")
@@ -245,43 +254,37 @@ def tile_moe_bdx_mlp_relu2_kernel(tc, dyT, a, w2, w1, gate, offs, out):
                 nc.vector.scalar_tensor_tensor(da[:, t, :], a_raw[e, h][:, t, :], 0.0, hidden_sums(e, h, t)[:], MAX, MULT)
             da_planes[e, h] = da
 
-        def interleave_da(e, h):
+        def mix_da(e, h):
             da_mixed[e, h] = placed("da_mixed", [P, C, J], BF16, DA_MIXED_AT + 4096 * h)
             for slots in (slice(0, C // 2), slice(C // 2, C)):
                 to, source = da_mixed[e, h][:, slots, :], da_planes[e, h][:, :, slots]
                 if h and slots.start:
-                    to, source = to.rearrange("p (c i) t -> p c t i", i=2), source.rearrange("p t (c i) -> p c t i", i=2)
-                    nc.gpsimd.tensor_scalar(to, source, 1.0, 0.0, MULT, ADD)
+                    nc.gpsimd.tensor_scalar(mixed_in_pairs(to), in_pairs(source), 1.0, 0.0, MULT, ADD)
                 else:
                     to, source = to.rearrange("p (c i) t -> p c t i", i=8), source.rearrange("p t (c i) -> p c t i", i=8)
                     nc.scalar.activation(to, source, COPY)
 
         def relu_on_gpsimd(e):
             relu_a[e] = placed("relu_a", [P, C // 2, J, 2], F32, RELU_AT[e % 2])
-            nc.gpsimd.tensor_scalar(relu_a[e][:], a_raw[e, 1][:].rearrange("p t (c i) -> p c t i", i=2), F32_MAX, 0.0, MIN, MAX)
+            nc.gpsimd.tensor_scalar(relu_a[e][:], in_pairs(a_raw[e, 1][:]), F32_MAX, 0.0, MIN, MAX)
 
-        def sums_to_sbuf(e, planes):
-            if e not in dh_planes:
-                dh_planes[e] = placed("dh_planes", [P, J, C], F32, DH_AT if e % 2 else DH_AT + DH_SHIFT)
-            for t in planes:
+        def sums_to_sbuf(e):
+            dh_planes[e] = placed("dh_planes", [P, J, C], F32, DH_AT if e % 2 else DH_AT + DH_SHIFT)
+            for t in range(J):
                 nc.scalar.activation(dh_planes[e][:, t, :], hidden_sums(e, 1, t)[:], COPY)
 
         def product_on_gpsimd(e):
             da_mixed[e, 1] = placed("da_mixed", [P, C, J], BF16, DA_MIXED_AT + 4096)
-            nc.gpsimd.tensor_tensor(
-                da_mixed[e, 1][:].rearrange("p (c i) t -> p c t i", i=2),
-                dh_planes[e][:].rearrange("p t (c i) -> p c t i", i=2),
-                relu_a[e][:],
-                MULT,
-            )
+            nc.gpsimd.tensor_tensor(mixed_in_pairs(da_mixed[e, 1][:]), in_pairs(dh_planes[e][:]), relu_a[e][:], MULT)
 
         def quantize_da(e, h):
             codes = work.tile([P, C], U32, name="da_codes", bufs=3, align_bytes=64)
             if e < E - 1:
-                at = TWOS_AT + 512 * (e + 1) if h else W2_MIXED_AT[0] + 64
+                scales = placed("da_scales", [P, C], U8, TWOS_AT + 512 * (e + 1) if h else W2_MIXED_AT[0] + 64)
+            elif h:
+                scales = work.tile([P, C], U8, name="da_scales", bufs=1, align_bytes=64)
             else:
-                at = None if h else batch_at(e) + 1024
-            scales = scale_plane("da_scales", C, 1, at)
+                scales = placed("da_scales", [P, C], U8, batch_at(e) + 1024)
             nc.vector.quantize_mx(
                 out=codes[:].bitcast(E5M2), scales=scales[:], in_=da_mixed[e, h][:].rearrange("p c t -> p (c t)")
             )
@@ -307,13 +310,13 @@ def tile_moe_bdx_mlp_relu2_kernel(tc, dyT, a, w2, w1, gate, offs, out):
 
         def copy_out(e, k, lo=0, hi=C):
             if lo:
-                plane = placed("late_result", [P, hi - lo], F32, DA_MIXED_AT)[:]
+                result = placed("late_result", [P, hi - lo], F32, DA_MIXED_AT)[:]
             elif k == 0 and e < E - 1:
-                plane = placed("first_result", [P, C], F32, W2_MIXED_AT[1][(e + 1) % 2] + 64)[:]
+                result = placed("first_result", [P, C], F32, W2_MIXED_AT[1][e] + 128)[:]
             else:
-                plane = work.tile([P, C], F32, name="result", bufs=2)[:, lo:hi]
-            nc.scalar.activation(plane, dx_banks[e, k][:, lo:hi], COPY)
-            results[e, k, lo] = plane
+                result = work.tile([P, C], F32, name="result")[:, lo:hi]
+            nc.scalar.activation(result, dx_banks[e, k][:, lo:hi], COPY)
+            results[e, k, lo] = result
 
         def scatter(e, k, lo=0, hi=C):
             nc.vector.tensor_copy(windows[k][:].indirect(listed(e, lo, hi)), results[e, k, lo])
@@ -336,11 +339,7 @@ def tile_moe_bdx_mlp_relu2_kernel(tc, dyT, a, w2, w1, gate, offs, out):
         load_w1(0, 0)
         load_a(0, 0)
         load_a(0, 1)
-        load_w2(1)
-        load_a(1, 0)
-        load_w1(0, 1)
-        load_w1(1, 0)
-        load_a(1, 1)
+        load_round(0)
 
         for e in (1, 0, 3):
             spread_gate(e)
@@ -355,6 +354,7 @@ def tile_moe_bdx_mlp_relu2_kernel(tc, dyT, a, w2, w1, gate, offs, out):
         gate_pair(1, 1)
         nc.scalar.copy(third_row[:], late_row[:, 0, :])
         gather(2)
+
         mix_w2(0, 0)
         mix_w2(0, 1)
         spread_gate(2)
@@ -367,8 +367,9 @@ def tile_moe_bdx_mlp_relu2_kernel(tc, dyT, a, w2, w1, gate, offs, out):
         product_on_vector(0, 1)
         gather(3)
         mix_w1(0, 0, K)
-        interleave_da(0, 0)
-        interleave_da(0, 1)
+        mix_da(0, 0)
+        mix_da(0, 1)
+
         for e in range(E):
             last = e == E - 1
             if e == E - 2:
@@ -388,28 +389,31 @@ def tile_moe_bdx_mlp_relu2_kernel(tc, dyT, a, w2, w1, gate, offs, out):
             if last:
                 quantize_da(e, 1)
             quantize_w1(e, W1_HEAD, HALVES * K)
-            if not last:
-                quantize_w2(e + 1, 1)
             if last:
                 continue
+            quantize_w2(e + 1, 1)
+
             mix_w1(e + 1, 0, K)
             load_round(e + 1)
             input_gradient(e, [0])
             copy_out(e, 0)
             product_on_vector(e + 1, 0)
+            if e == 0:
+                gate_on_gpsimd(E - 1, 0, C // 2)
             relu_on_gpsimd(e + 1)
-            held_back = e == E - 2
-            if not held_back:
-                gate_on_gpsimd(E - 1, e * C // 2, (e + 1) * C // 2)
-            sums_to_sbuf(e + 1, range(J))
+            if e == 1:
+                gate_on_gpsimd(E - 1, C // 2, C)
+            sums_to_sbuf(e + 1)
             product_on_gpsimd(e + 1)
             input_gradient(e, [1, 2])
+            slots_now = C // 2 if e == E - 2 else C
             copy_out(e, 1)
-            copy_out(e, 2, 0, C // 2 if held_back else C)
+            copy_out(e, 2, 0, slots_now)
             scatter(e, 0)
             scatter(e, 1)
-            scatter(e, 2, 0, C // 2 if held_back else C)
-            interleave_da(e + 1, 0)
+            scatter(e, 2, 0, slots_now)
+            mix_da(e + 1, 0)
+
         copy_out(E - 2, 2, C // 2, C)
         scatter(E - 2, 2, C // 2, C)
         for k in range(K_TILES):

@@ -8,6 +8,8 @@ J = 4
 Q = 32
 HALVES = H // (P * J)
 K_TILES = K // P
+GROUP = 128
+PIECE = 256
 FLOPS = 2 * E * C * (N * H + H * K)
 BYTES = 4 * (N * T + H * E * C + E * N * H + E * H * K + E * C + K * T) + 2 * P * (E * C // 16)
 
@@ -21,46 +23,53 @@ E5M2 = mybir.dt.float8_e5m2_x4
 MULT = mybir.AluOpType.mult
 MAX = mybir.AluOpType.max
 ADD = mybir.AluOpType.add
-MIN = mybir.AluOpType.min
-F32_MAX = 3.4028234663852886e38
 COPY = mybir.ActivationFunctionType.Copy
 
 BANK = 2048
-W1_HEAD = 512
+DH_BANKS = 5
+A_PITCH = 512
 
-W2_MIXED_AT = (18368, (12224, 0, 12160))
-RELU_AT = (3968, 4096)
-GATHERED_AT = (22464, 30656, 52160, 30720)
-FIRST_A_AT = 38848
-DH_AT = FIRST_A_AT + 4096
-DH_SHIFT = 1024
-FIRST_GATE_AT = GATHERED_AT[2] + 8192
-SECOND_GATE_AT = FIRST_GATE_AT + 2048
-DA_MIXED_AT = SECOND_GATE_AT + 2048
-G_MIXED_AT = (3968, 8064, DA_MIXED_AT + 8192)
-TWOS_AT = G_MIXED_AT[2] + 4096
-W2_RAW_AT = (TWOS_AT + 2560, TWOS_AT + 18944)
-A_RAW_AT = (W2_RAW_AT[1] + 16384, W2_RAW_AT[1] + 24576)
-W1_TAIL_AT = A_RAW_AT[1] + 8192
-DA_AT = W1_TAIL_AT + 1984
-W1_RAW_AT = (DA_AT + 4096, DA_AT + 10240)
-W1_HEAD_AT = (W2_RAW_AT[0] + 2048, GATHERED_AT[0], GATHERED_AT[2], GATHERED_AT[0])
-LAST_G_AT = (16256, A_RAW_AT[0])
-FIRST_W2_MIXED_AT = (W2_MIXED_AT[0], G_MIXED_AT[2] - 4032)
+RINGS = {
+    "w2_raw": (16384, 2),
+    "a_raw": (8448, 4),
+    "w1_raw": (12288, 2),
+    "gathered": (8192, 4),
+    "gate": (2048, 2),
+    "g_mixed": (4096, 3),
+    "g_codes": (2048, 2),
+    "g_scales": (512, 2),
+    "w2_mixed": (4096, 3),
+    "w2_codes": (2048, 3),
+    "w2_scales": (512, 2),
+    "w1_mixed": (3072, 2),
+    "w1_codes": (1536, 2),
+    "da_mixed": (4096, 3),
+    "da_codes": (2048, 3),
+    "da_scales": (512, 3),
+    "result": (2048, 6),
+}
+
+
+def ring_at(name, index):
+    start = 0
+    for other, (size, places) in RINGS.items():
+        if other == name:
+            return start + size * (index % places)
+        start = start + size * places
+    raise ValueError(name)
 
 
 def tile_moe_bdx_mlp_relu2_kernel(tc, dyT, a, w2, w1, gate, offs, out):
     nc = tc.nc
     with ExitStack() as ctx:
         held = ctx.enter_context(tc.tile_pool(name="held", bufs=1))
-        work = ctx.enter_context(tc.tile_pool(name="work", bufs=2))
-        shared = ctx.enter_context(tc.tile_pool(name="shared", bufs=1))
+        rings = ctx.enter_context(tc.tile_pool(name="rings", bufs=1))
         psum = ctx.enter_context(tc.psum_pool(name="psum", bufs=1))
 
         offsets = held.tile([P, E * C // 16], U16, name="offsets")
-        gates = {}
         tokens = [held.tile([P, T], F32, name=f"tokens{t}", tag=f"columns{t}") for t in range(J)]
         windows = [held.tile([P, T], F32, name=f"window{k}", tag=f"columns{k}") for k in range(K_TILES)]
+        gate_rows = held.tile([P, E, J], F32, name="gate_rows")
 
         identity = held.tile([P, P], F32, name="identity")
         steps = held.tile([P, Q], F32, name="steps")
@@ -74,349 +83,254 @@ def tile_moe_bdx_mlp_relu2_kernel(tc, dyT, a, w2, w1, gate, offs, out):
             square = slice(first, first + Q)
             nc.vector.tensor_tensor(identity[square, square], column[square, :], row[square, :], mybir.AluOpType.is_equal)
 
-        twos = [
-            shared.tile([P, 32], F32, name=f"two{e}", align_bytes=64, offset=TWOS_AT + at) for e, at in enumerate((448, 1024, 1536))
-        ]
-        for two in twos:
-            nc.vector.memset(two[:, 0:1], 2.0)
-
         dy_rows = dyT.rearrange("(p t) s -> p t s", t=J)
         a_rows = a.rearrange("(h p t) s -> h p t s", p=P, t=J)
-        w2_raw, a_raw, w1_raw, gathered, gate_rows = {}, {}, {}, {}, {}
+        w2_raw, a_raw, w1_raw, gathered, spread, gates = {}, {}, {}, {}, {}, {}
         g_mixed, w2_mixed, w1_mixed, da_mixed = {}, {}, {}, {}
         g_mx, w2_mx, w1_mx, da_mx = {}, {}, {}, {}
-        da_planes, dh_planes, relu_a, dx_banks, results = {}, {}, {}, {}, {}
+        dx_banks, results = {}, {}
 
         def placed(name, shape, dtype, at):
-            return shared.tile(shape, dtype, name=f"{name}_at{at}", align_bytes=64, offset=at)
+            return rings.tile(shape, dtype, name=f"{name}_at{at}", align_bytes=64, offset=at)
 
-        def bank(b):
-            return psum.tile([P, C], F32, name=f"bank{b}", offset=b * BANK)
-
-        def batch_at(e):
-            if e == 0:
-                return FIRST_A_AT + 64
-            return DH_AT if e % 2 else DH_AT + 8192
+        def in_ring(name, index, shape, dtype):
+            return placed(name, shape, dtype, ring_at(name, index))
 
         def listed(e, lo=0, hi=C):
             return offsets[:, (e * C + lo) // 16 : (e * C + hi) // 16]
 
-        def in_pairs(planes):
-            return planes.rearrange("p t (c i) -> p c t i", i=2)
-
-        def mixed_in_pairs(mixed):
-            return mixed.rearrange("p (c i) t -> p c t i", i=2)
-
-        def gate_in_pairs(e, lo, hi, planes):
-            return gates[e][:, lo:hi].rearrange("p (c i) -> p c i", i=2).unsqueeze(2).to_broadcast([P, (hi - lo) // 2, planes, 2])
-
-        def load_tokens(t):
-            nc.sync.dma_start(tokens[t][:], dy_rows[:, t, :])
-
-        def load_gate_rows(queue, rows, experts):
-            queue.dma_start(rows[:], gate[0].rearrange("(e p c) -> p e c", p=P, c=J)[:, experts, :])
-
         def load_w2(e):
-            w2_raw[e] = placed("w2_raw", [P, J, H], F32, W2_RAW_AT[e % 2] - (0 if e else 64))
+            w2_raw[e] = in_ring("w2_raw", e, [P, J, H], F32)
             nc.sync.dma_start(w2_raw[e][:], w2[e].rearrange("(p j) i -> p j i", j=J))
 
         def load_a(e, h):
-            if h:
-                a_raw[e, h] = placed("a_raw", [P, J, C], F32, A_RAW_AT[e % 2] if e else FIRST_A_AT)
-            else:
-                a_raw[e, h] = work.tile([P, J, C], F32, name="a_raw")
-            nc.sync.dma_start(a_raw[e, h][:], a_rows[h][:, :, e * C : (e + 1) * C])
+            tile = in_ring("a_raw", HALVES * e + h, [P, J, A_PITCH], F32)
+            a_raw[e, h] = tile
+            nc.sync.dma_start(tile[:, :, 0:C], a_rows[h][:, :, e * C : (e + 1) * C])
 
-        def load_w1(e, h):
-            if h:
-                w1_raw[e, h] = placed("w1_raw", [P, J, K], F32, W1_RAW_AT[e % 2])
-            else:
-                w1_raw[e, h] = work.tile([P, J, K], F32, name="w1_raw")
-            nc.sync.dma_start(w1_raw[e, h][:], w1[e].rearrange("(h p j) k -> h p j k", p=P, j=J)[h])
-
-        def load_round(e):
-            if e + 1 < E:
-                load_w2(e + 1)
-                load_a(e + 1, 0)
-            load_w1(e, 1)
-            if e + 1 < E:
-                load_w1(e + 1, 0)
-                load_a(e + 1, 1)
+        def load_w1(e):
+            w1_raw[e] = in_ring("w1_raw", e, [P, HALVES, J, K], F32)
+            nc.sync.dma_start(
+                w1_raw[e][:].rearrange("p h j k -> p h (j k)"), w1[e].rearrange("(h p j) k -> p h (j k)", p=P, j=J)
+            )
 
         def spread_gate(e):
-            spread = psum.tile([P, J, P], F32, name=f"spread{e in (1, 2)}", offset=(7 if e in (1, 2) else J) * BANK)
+            spread[e] = psum.tile([P, J, P], F32, name=f"spread{e}", offset=(DH_BANKS + e if e < E - 1 else DH_BANKS - 1) * BANK)
             for c in range(J):
-                nc.tensor.transpose(spread[:, c, :], gate_rows[e][:, c : c + 1].to_broadcast([P, P]), identity[:])
-            if e < E - 1:
-                gates[e] = placed("gate", [P, C], F32, (FIRST_GATE_AT, SECOND_GATE_AT, W2_RAW_AT[0])[e])
-            else:
-                gates[e] = held.tile([P, C], F32, name="last_gate")
-            nc.scalar.activation(gates[e][:].rearrange("m (p c) -> m p c", c=J), spread[:].rearrange("m c p -> m p c"), COPY)
+                nc.tensor.transpose(spread[e][:, c, :], gate_rows[:, e, c : c + 1].to_broadcast([P, P]), identity[:])
 
-        def gather(e):
-            gathered[e] = placed("gathered", [P, J, C], F32, GATHERED_AT[e])
-            for t in range(J):
+        def gate_to_sbuf(e):
+            gates[e] = in_ring("gate", e, [P, C], F32)
+            nc.scalar.activation(gates[e][:].rearrange("m (p c) -> m p c", c=J), spread[e][:].rearrange("m c p -> m p c"), COPY)
+
+        def gather(e, t, on_scalar):
+            if t == 0:
+                gathered[e] = in_ring("gathered", e, [P, J, C], F32)
+            if on_scalar:
+                nc.scalar.activation(gathered[e][:, t, :], tokens[t][:].indirect(listed(e)), COPY)
+            else:
                 nc.vector.tensor_copy(gathered[e][:, t, :], tokens[t][:].indirect(listed(e)))
 
-        def gather_plane(e, t):
-            if t % 2 == 0:
-                gathered[e, t // 2] = placed("gathered_pair", [P, 2, C], F32, GATHERED_AT[e] + 2048 * t)
-            to = gathered[e, t // 2][:, t % 2, :]
-            if e == 1 and t < 2:
-                nc.vector.tensor_tensor(to, tokens[t][:].indirect(listed(e)), gates[e][:], MULT)
+        def new_g_mixed(e):
+            at = ring_at("g_mixed", e) if e < E - 1 else ring_at("gathered", 0)
+            g_mixed[e] = placed("g_mixed", [P, C, J], BF16, at)
+            return g_mixed[e]
+
+        def gate_on_vector(e):
+            nc.vector.tensor_tensor(
+                new_g_mixed(e)[:].rearrange("m (p c) t -> m p t c", c=J),
+                gathered[e][:].rearrange("m t (p c) -> m p t c", c=J),
+                spread[e][:].rearrange("m c p -> m p c").unsqueeze(2).to_broadcast([P, P, J, J]),
+                MULT,
+            )
+
+        def gate_on_gpsimd(e):
+            to = new_g_mixed(e)
+            for lo in range(0, C, C // 2):
+                slots = slice(lo, lo + C // 2)
+                nc.gpsimd.tensor_tensor(
+                    to[:, slots, :].rearrange("p (c i) t -> p c t i", i=2),
+                    gathered[e][:, :, slots].rearrange("p t (c i) -> p c t i", i=2),
+                    gates[e][:, slots].rearrange("p (c i) -> p c i", i=2).unsqueeze(2).to_broadcast([P, C // 4, J, 2]),
+                    MULT,
+                )
+
+        def quantize(codes, scales, mixed, fmt):
+            nc.vector.quantize_mx(out=codes.bitcast(fmt), scales=scales, in_=mixed)
+
+        def quantize_g(e):
+            g_mx[e] = in_ring("g_codes", e, [P, C], U32), in_ring("g_scales", e, [P, C], U8)
+            quantize(g_mx[e][0][:], g_mx[e][1][:], g_mixed[e][:].rearrange("p c t -> p (c t)"), E5M2)
+
+        def cast(to, source, factor, on_scalar):
+            if on_scalar:
+                nc.scalar.activation(to, source, COPY, scale=factor)
             else:
-                nc.vector.tensor_copy(to, tokens[t][:].indirect(listed(e)))
+                nc.gpsimd.tensor_scalar(to, source, factor, 0.0, MULT, ADD)
 
-        def gate_pair(e, u):
-            if u == 0:
-                g_mixed[e, 0] = placed("g_mixed", [P, C, J], BF16, G_MIXED_AT[e])
-            to = mixed_in_pairs(g_mixed[e, 0][:, :, 2 * u : 2 * u + 2])
-            if (e, u) == (1, 0):
-                nc.scalar.activation(to, in_pairs(gathered[e, u][:]), COPY)
-            else:
-                nc.gpsimd.tensor_tensor(to, in_pairs(gathered[e, u][:]), gate_in_pairs(e, 0, C, 2), MULT)
-
-        def gate_on_gpsimd(e, lo=0, hi=C):
-            at = G_MIXED_AT[e] if e < E - 1 else LAST_G_AT[lo // (C // 2)]
-            g_mixed[e, lo] = placed(f"g_mixed{hi - lo}", [P, hi - lo, J], BF16, at)
-            nc.gpsimd.tensor_tensor(
-                mixed_in_pairs(g_mixed[e, lo][:]), in_pairs(gathered[e][:, :, lo:hi]), gate_in_pairs(e, lo, hi, J), MULT
-            )
-
-        def quantize_g(e, lo=0, hi=C):
-            if lo == 0:
-                codes = work.tile([P, C], U32, name="g_codes", bufs=3, align_bytes=64)
-                at = (SECOND_GATE_AT + 1024, W2_RAW_AT[0] - 512, TWOS_AT, batch_at(2) + 512)[e]
-                g_mx[e] = codes, placed("g_scales", [P, C], U8, at)
-            codes, scales = g_mx[e]
-            nc.vector.quantize_mx(
-                out=codes[:, lo:hi].bitcast(E5M2), scales=scales[:, lo:hi], in_=g_mixed[e, lo][:].rearrange("p c t -> p (c t)")
-            )
-
-        def mix_w2(e, h):
-            at = (W2_MIXED_AT[0], W2_MIXED_AT[1][e - 1]) if e else FIRST_W2_MIXED_AT
-            w2_mixed[e, h] = placed("w2_mixed", [P, J, P, J], BF16, at[h])
-            nc.scalar.activation(
-                w2_mixed[e, h][:].rearrange("p t m j -> p m j t"),
-                w2_raw[e][:, :, h * P * J : (h + 1) * P * J].rearrange("p j (m t) -> p m j t", t=J),
-                COPY,
-                scale=twos[e - 1][:, 0:1] if e and h == 0 else 2.0,
-            )
+        def mix_w2(e, h, on_scalar):
+            w2_mixed[e, h] = in_ring("w2_mixed", HALVES * e + h, [P, J, P, J], BF16)
+            to = w2_mixed[e, h][:].rearrange("p t m j -> p m j t")
+            source = w2_raw[e][:, :, h * P * J : (h + 1) * P * J].rearrange("p j (m t) -> p m j t", t=J)
+            for t in range(0, J, 2):
+                cast(to[:, :, :, t : t + 2], source[:, :, :, t : t + 2], 2.0, on_scalar)
 
         def quantize_w2(e, h):
-            codes = work.tile([P, P * J], U32, name="w2_codes", bufs=4, align_bytes=64)
-            at = (batch_at(e - 1), W1_RAW_AT[(e - 1) % 2])[h] if e else SECOND_GATE_AT + 512 * h
-            scales = placed("w2_scales", [P, P * J], U8, at)
+            codes = in_ring("w2_codes", HALVES * e + h, [P, P * J], U32)
+            if h:
+                scales = placed("w2_scales", [P, P * J], U8, ring_at("a_raw", HALVES * e))
+            else:
+                scales = in_ring("w2_scales", e, [P, P * J], U8)
             w2_mx[e, h] = codes, scales
-            nc.vector.quantize_mx(out=codes[:].bitcast(E4M3), scales=scales[:], in_=w2_mixed[e, h][:].rearrange("p t m j -> p (t m j)"))
+            quantize(codes[:], scales[:], w2_mixed[e, h][:].rearrange("p t m j -> p (t m j)"), E4M3)
 
-        def mix_w1(e, lo, hi):
-            first = 0 if lo < W1_HEAD else W1_HEAD
-            if lo == 0:
-                w1_mixed[e, 0] = placed("w1_head", [P, W1_HEAD, J], BF16, W1_HEAD_AT[e])
-            if lo == W1_HEAD:
-                w1_mixed[e, lo] = placed("w1_tail", [P, hi - lo, J], BF16, W1_TAIL_AT)
-            nc.scalar.activation(
-                w1_mixed[e, first][:, lo - first : hi - first, :].rearrange("p (c i) j -> p c j i", i=4),
-                w1_raw[e, lo // K][:, :, lo % K : (hi - 1) % K + 1].rearrange("p j (c i) -> p c j i", i=4),
-                COPY,
+        def mix_w1(e, h, on_scalar):
+            w1_mixed[e, h] = in_ring("w1_mixed", h, [P, K, J], BF16)
+            cast(
+                w1_mixed[e, h][:].rearrange("p (c i) j -> p c j i", i=2),
+                w1_raw[e][:, h, :, :].rearrange("p j (c i) -> p c j i", i=2),
+                1.0,
+                on_scalar,
             )
 
-        def quantize_w1(e, lo, hi):
-            if lo == 0:
-                codes = work.tile([P, HALVES * K], U32, name="w1_codes", align_bytes=64)
-                at = W2_MIXED_AT[0] + 1088 if e < E - 1 else batch_at(e) + 1536
-                w1_mx[e] = codes, placed("w1_scales", [P, HALVES * K], U8, at)
-            codes, scales = w1_mx[e]
-            nc.vector.quantize_mx(
-                out=codes[:, lo:hi].bitcast(E4M3), scales=scales[:, lo:hi], in_=w1_mixed[e, lo][:].rearrange("p c j -> p (c j)")
-            )
+        def quantize_w1(e, h):
+            codes = in_ring("w1_codes", h, [P, K], U32)
+            scales = placed("w1_scales", [P, K], U8, ring_at("a_raw", HALVES * e + 1) + K * h)
+            w1_mx[e, h] = codes, scales
+            quantize(codes[:], scales[:], w1_mixed[e, h][:].rearrange("p c j -> p (c j)"), E4M3)
 
-        def hidden_sums(e, h, t):
+        def form_da(e, h):
             w2_codes, w2_scales = w2_mx[e, h]
             g_codes, g_scales = g_mx[e]
-            dh = bank(h * J + t)
-            col = t * P
-            nc.tensor.matmul_mx(
-                out=dh[:],
-                lhsT=w2_codes[:, col : col + P].bitcast(E4M3),
-                lhsT_scale=w2_scales[:, col : col + P],
-                rhs=g_codes[:].bitcast(E5M2),
-                rhs_scale=g_scales[:],
-                start=True,
-                stop=True,
-            )
-            return dh
-
-        def product_on_vector(e, h):
-            da = placed("da_planes", [P, J, C], BF16, DA_AT if e else (W2_RAW_AT[0] + 6144, GATHERED_AT[0] + 4096)[h])
-            for t in range(J):
-                nc.vector.scalar_tensor_tensor(da[:, t, :], a_raw[e, h][:, t, :], 0.0, hidden_sums(e, h, t)[:], MAX, MULT)
-            da_planes[e, h] = da
-
-        def mix_da(e, h):
-            da_mixed[e, h] = placed("da_mixed", [P, C, J], BF16, DA_MIXED_AT + 4096 * h)
-            for slots in (slice(0, C // 2), slice(C // 2, C)):
-                to, source = da_mixed[e, h][:, slots, :], da_planes[e, h][:, :, slots]
-                if h and slots.start:
-                    nc.gpsimd.tensor_scalar(mixed_in_pairs(to), in_pairs(source), 1.0, 0.0, MULT, ADD)
-                else:
-                    to, source = to.rearrange("p (c i) t -> p c t i", i=8), source.rearrange("p t (c i) -> p c t i", i=8)
-                    nc.scalar.activation(to, source, COPY)
-
-        def relu_on_gpsimd(e):
-            relu_a[e] = placed("relu_a", [P, C // 2, J, 2], F32, RELU_AT[e % 2])
-            nc.gpsimd.tensor_scalar(relu_a[e][:], in_pairs(a_raw[e, 1][:]), F32_MAX, 0.0, MIN, MAX)
-
-        def sums_to_sbuf(e):
-            dh_planes[e] = placed("dh_planes", [P, J, C], F32, DH_AT if e % 2 else DH_AT + DH_SHIFT)
-            for t in range(J):
-                nc.scalar.activation(dh_planes[e][:, t, :], hidden_sums(e, 1, t)[:], COPY)
-
-        def product_on_gpsimd(e):
-            da_mixed[e, 1] = placed("da_mixed", [P, C, J], BF16, DA_MIXED_AT + 4096)
-            nc.gpsimd.tensor_tensor(mixed_in_pairs(da_mixed[e, 1][:]), in_pairs(dh_planes[e][:]), relu_a[e][:], MULT)
+            da_mixed[e, h] = in_ring("da_mixed", HALVES * e + h, [P, C, J], BF16)
+            for s in range(C // GROUP):
+                slots = slice(s * GROUP, (s + 1) * GROUP)
+                b = ((HALVES * e + h) * (C // GROUP) + s) % DH_BANKS
+                dh = psum.tile([P, J, GROUP], F32, name=f"dh{b}", offset=b * BANK)
+                for t in range(J):
+                    cols = slice(t * P, (t + 1) * P)
+                    nc.tensor.matmul_mx(
+                        out=dh[:, t, :],
+                        lhsT=w2_codes[:, cols].bitcast(E4M3),
+                        lhsT_scale=w2_scales[:, cols],
+                        rhs=g_codes[:, slots].bitcast(E5M2),
+                        rhs_scale=g_scales[:, slots],
+                        start=True,
+                        stop=True,
+                    )
+                nc.vector.scalar_tensor_tensor(
+                    da_mixed[e, h][:, slots, :],
+                    a_raw[e, h][:, :, slots].rearrange("p t c -> p c t"),
+                    0.0,
+                    dh[:].rearrange("p t c -> p c t"),
+                    MAX,
+                    MULT,
+                )
 
         def quantize_da(e, h):
-            codes = work.tile([P, C], U32, name="da_codes", bufs=3, align_bytes=64)
-            if e < E - 1:
-                scales = placed("da_scales", [P, C], U8, TWOS_AT + 512 * (e + 1) if h else W2_MIXED_AT[0] + 64)
-            elif h:
-                scales = work.tile([P, C], U8, name="da_scales", bufs=1, align_bytes=64)
+            index = HALVES * e + h
+            da_mx[e, h] = in_ring("da_codes", index, [P, C], U32), in_ring("da_scales", index, [P, C], U8)
+            quantize(da_mx[e, h][0][:], da_mx[e, h][1][:], da_mixed[e, h][:].rearrange("p c t -> p (c t)"), E5M2)
+
+        def input_gradient(e, k):
+            dx = psum.tile([P, C], F32, name=f"dx{k}", offset=(DH_BANKS + k) * BANK)
+            cols = slice(k * P, (k + 1) * P)
+            for h in range(HALVES):
+                nc.tensor.matmul_mx(
+                    out=dx[:],
+                    lhsT=w1_mx[e, h][0][:, cols].bitcast(E4M3),
+                    lhsT_scale=w1_mx[e, h][1][:, cols],
+                    rhs=da_mx[e, h][0][:].bitcast(E5M2),
+                    rhs_scale=da_mx[e, h][1][:],
+                    start=(h == 0),
+                    stop=(h == HALVES - 1),
+                )
+            dx_banks[e, k] = dx
+
+        def copy_out(e, k, on_scalar):
+            results[e, k] = in_ring("result", K_TILES * e + k, [P, C], F32)
+            if on_scalar:
+                nc.scalar.activation(results[e, k][:], dx_banks[e, k][:], COPY)
             else:
-                scales = placed("da_scales", [P, C], U8, batch_at(e) + 1024)
-            nc.vector.quantize_mx(
-                out=codes[:].bitcast(E5M2), scales=scales[:], in_=da_mixed[e, h][:].rearrange("p c t -> p (c t)")
-            )
-            da_mx[e, h] = codes, scales
+                nc.vector.tensor_copy(results[e, k][:], dx_banks[e, k][:])
 
-        def input_gradient(e, tiles):
-            w1_codes, w1_scales = w1_mx[e]
-            for k in tiles:
-                dx = bank((7, 4, 5)[k] if e < E - 1 else 0)
-                for h in range(HALVES):
-                    col = h * K + k * P
-                    da_codes, da_scales = da_mx[e, h]
-                    nc.tensor.matmul_mx(
-                        out=dx[:],
-                        lhsT=w1_codes[:, col : col + P].bitcast(E4M3),
-                        lhsT_scale=w1_scales[:, col : col + P],
-                        rhs=da_codes[:].bitcast(E5M2),
-                        rhs_scale=da_scales[:],
-                        start=(h == 0),
-                        stop=(h == HALVES - 1),
-                    )
-                dx_banks[e, k] = dx
-
-        def copy_out(e, k, lo=0, hi=C):
-            if lo:
-                result = placed("late_result", [P, hi - lo], F32, DA_MIXED_AT)[:]
-            elif k == 0 and e < E - 1:
-                result = placed("first_result", [P, C], F32, W2_MIXED_AT[1][e] + 128)[:]
+        def scatter(e, k, lo, hi, on_scalar):
+            to = windows[k][:].indirect(listed(e, lo, hi))
+            if on_scalar:
+                nc.scalar.activation(to, results[e, k][:, lo:hi], COPY)
             else:
-                result = work.tile([P, C], F32, name="result")[:, lo:hi]
-            nc.scalar.activation(result, dx_banks[e, k][:, lo:hi], COPY)
-            results[e, k, lo] = result
+                nc.vector.tensor_copy(to, results[e, k][:, lo:hi])
 
-        def scatter(e, k, lo=0, hi=C):
-            nc.vector.tensor_copy(windows[k][:].indirect(listed(e, lo, hi)), results[e, k, lo])
-            if e == E - 1:
-                nc.sync.dma_start(out[k * P : (k + 1) * P, :], windows[k][:])
+        def store(k):
+            nc.sync.dma_start(out[k * P : (k + 1) * P, :], windows[k][:])
 
-        second_row = held.tile([P, 1, J], F32, name="second_row")
-        outer_rows = held.tile([P, 2, J], F32, name="outer_rows")
-        late_row = placed("late_row", [P, 1, J], F32, GATHERED_AT[2])
-        third_row = held.tile([P, J], F32, name="third_row")
-        gate_rows.update({0: outer_rows[:, 0, :], 1: second_row[:, 0, :], 2: third_row[:], 3: outer_rows[:, 1, :]})
-        load_gate_rows(nc.scalar, second_row, slice(1, 2))
+        nc.scalar.dma_start(gate_rows[:], gate[0].rearrange("(e p c) -> p e c", p=P, c=J))
         nc.sync.dma_start(offsets[:], offs)
-        load_tokens(0)
-        load_gate_rows(nc.sync, outer_rows, slice(0, E, E - 1))
-        for t in range(1, J):
-            load_tokens(t)
-        load_gate_rows(nc.sync, late_row, slice(2, 3))
-        load_w2(0)
-        load_w1(0, 0)
-        load_a(0, 0)
-        load_a(0, 1)
-        load_round(0)
-
-        for e in (1, 0, 3):
-            spread_gate(e)
-        for e, t in ((0, 0), (1, 0), (1, 1), (0, 1)):
-            gather_plane(e, t)
-        gate_pair(1, 0)
-        gate_pair(0, 0)
-        for t in (2, 3):
-            gather_plane(0, t)
-            gather_plane(1, t)
-        gate_pair(0, 1)
-        gate_pair(1, 1)
-        nc.scalar.copy(third_row[:], late_row[:, 0, :])
-        gather(2)
-
-        mix_w2(0, 0)
-        mix_w2(0, 1)
-        spread_gate(2)
-        quantize_g(0)
-        quantize_w2(0, 0)
-        quantize_g(1)
-        quantize_w2(0, 1)
-        gate_on_gpsimd(2)
-        product_on_vector(0, 0)
-        product_on_vector(0, 1)
-        gather(3)
-        mix_w1(0, 0, K)
-        mix_da(0, 0)
-        mix_da(0, 1)
+        for t in range(J):
+            nc.sync.dma_start(tokens[t][:], dy_rows[:, t, :])
+        for e in range(E):
+            load_w2(e)
+            load_a(e, 0)
+            load_w1(e)
+            load_a(e, 1)
+            if e == 1:
+                break
 
         for e in range(E):
-            last = e == E - 1
-            if e == E - 2:
-                quantize_g(E - 1, 0, C // 2)
-                quantize_g(E - 1, C // 2, C)
-            if not last:
-                mix_w2(e + 1, 0)
-                mix_w2(e + 1, 1)
-                quantize_w2(e + 1, 0)
-                quantize_da(e, 1)
-            if e == 0:
-                quantize_g(2)
+            spread_gate(e)
+        gate_to_sbuf(3)
+        gate_to_sbuf(2)
+        for t in range(J):
+            gather(0, t, False)
+            gather(1, t, True)
+            gather(2, t, t == J - 1)
+            gather(3, t, True)
+        gate_on_vector(0)
+        gate_on_vector(1)
+        gate_on_gpsimd(2)
+        gate_on_gpsimd(3)
+        quantize_g(0)
+        quantize_g(1)
+
+        for e in range(E):
+            first, last = e == 0, e == E - 1
+            mix_w2(e, 0, first)
+            mix_w2(e, 1, first)
+            mix_w1(e, 0, first)
+            mix_w1(e, 1, first)
+            if e + 2 < E:
+                load_w2(e + 2)
+            quantize_w2(e, 0)
+            form_da(e, 0)
+            quantize_w2(e, 1)
             quantize_da(e, 0)
-            mix_w1(e, K, W1_HEAD)
-            mix_w1(e, W1_HEAD, HALVES * K)
-            quantize_w1(e, 0, W1_HEAD)
-            if last:
-                quantize_da(e, 1)
-            quantize_w1(e, W1_HEAD, HALVES * K)
-            if last:
-                continue
-            quantize_w2(e + 1, 1)
+            form_da(e, 1)
+            quantize_w1(e, 0)
+            quantize_w1(e, 1)
+            quantize_da(e, 1)
+            for k in range(K_TILES):
+                input_gradient(e, k)
+            if e + 2 < E:
+                load_a(e + 2, 0)
+                load_w1(e + 2)
+                load_a(e + 2, 1)
+                quantize_g(e + 2)
+            if not last:
+                for k in range(K_TILES):
+                    copy_out(e, k, True)
+                for lo in range(0, C, PIECE):
+                    for k in range(K_TILES):
+                        scatter(e, k, lo, lo + PIECE, True)
 
-            mix_w1(e + 1, 0, K)
-            load_round(e + 1)
-            input_gradient(e, [0])
-            copy_out(e, 0)
-            product_on_vector(e + 1, 0)
-            if e == 0:
-                gate_on_gpsimd(E - 1, 0, C // 2)
-            relu_on_gpsimd(e + 1)
-            if e == 1:
-                gate_on_gpsimd(E - 1, C // 2, C)
-            sums_to_sbuf(e + 1)
-            product_on_gpsimd(e + 1)
-            input_gradient(e, [1, 2])
-            slots_now = C // 2 if e == E - 2 else C
-            copy_out(e, 1)
-            copy_out(e, 2, 0, slots_now)
-            scatter(e, 0)
-            scatter(e, 1)
-            scatter(e, 2, 0, slots_now)
-            mix_da(e + 1, 0)
-
-        copy_out(E - 2, 2, C // 2, C)
-        scatter(E - 2, 2, C // 2, C)
-        for k in range(K_TILES):
-            input_gradient(E - 1, [k])
-            copy_out(E - 1, k)
-            scatter(E - 1, k)
+        e = E - 1
+        copy_out(e, 0, True)
+        copy_out(e, 1, False)
+        copy_out(e, 2, True)
+        scatter(e, 0, 0, PIECE, True)
+        scatter(e, 1, 0, C, False)
+        scatter(e, 0, PIECE, C, True)
+        store(0)
+        store(1)
+        scatter(e, 2, 0, PIECE, True)
+        scatter(e, 2, PIECE, C, False)
+        store(2)

@@ -40,7 +40,7 @@ RINGS = {
     "g_scales": (512, 2),
     "w2_mixed": (4096, 3),
     "w2_codes": (2048, 3),
-    "w2_scales": (512, 2),
+    "w2_scales": (512, 3),
     "w1_mixed": (3072, 2),
     "w1_codes": (1536, 2),
     "da_mixed": (4096, 3),
@@ -162,36 +162,30 @@ def tile_moe_bdx_mlp_relu2_kernel(tc, dyT, a, w2, w1, gate, offs, out):
             g_mx[e] = in_ring("g_codes", e, [P, C], U32), in_ring("g_scales", e, [P, C], U8)
             quantize(g_mx[e][0][:], g_mx[e][1][:], g_mixed[e][:].rearrange("p c t -> p (c t)"), E5M2)
 
-        def cast(to, source, factor, on_scalar):
-            if on_scalar:
-                nc.scalar.activation(to, source, COPY, scale=factor)
-            else:
-                nc.gpsimd.tensor_scalar(to, source, factor, 0.0, MULT, ADD)
-
         def mix_w2(e, h, on_scalar):
             w2_mixed[e, h] = in_ring("w2_mixed", HALVES * e + h, [P, J, P, J], BF16)
             to = w2_mixed[e, h][:].rearrange("p t m j -> p m j t")
             source = w2_raw[e][:, :, h * P * J : (h + 1) * P * J].rearrange("p j (m t) -> p m j t", t=J)
-            for t in range(0, J, 2):
-                cast(to[:, :, :, t : t + 2], source[:, :, :, t : t + 2], 2.0, on_scalar)
+            if on_scalar:
+                nc.scalar.activation(to, source, COPY, scale=2.0)
+            else:
+                nc.vector.tensor_scalar(to, source, 2.0, None, MULT)
 
         def quantize_w2(e, h):
             codes = in_ring("w2_codes", HALVES * e + h, [P, P * J], U32)
-            if h:
-                scales = placed("w2_scales", [P, P * J], U8, ring_at("a_raw", HALVES * e))
-            else:
-                scales = in_ring("w2_scales", e, [P, P * J], U8)
+            scales = in_ring("w2_scales", HALVES * e + h, [P, P * J], U8)
             w2_mx[e, h] = codes, scales
             quantize(codes[:], scales[:], w2_mixed[e, h][:].rearrange("p t m j -> p (t m j)"), E4M3)
 
         def mix_w1(e, h, on_scalar):
             w1_mixed[e, h] = in_ring("w1_mixed", h, [P, K, J], BF16)
-            cast(
-                w1_mixed[e, h][:].rearrange("p (c i) j -> p c j i", i=2),
-                w1_raw[e][:, h, :, :].rearrange("p j (c i) -> p c j i", i=2),
-                1.0,
-                on_scalar,
-            )
+            to, source = w1_mixed[e, h][:], w1_raw[e][:, h, :, :]
+            if on_scalar:
+                nc.scalar.activation(
+                    to.rearrange("p (c i) j -> p c j i", i=2), source.rearrange("p j (c i) -> p c j i", i=2), COPY
+                )
+            else:
+                nc.gpsimd.tensor_scalar(to, source.rearrange("p j c -> p c j"), 1.0, 0.0, MULT, ADD)
 
         def quantize_w1(e, h):
             codes = in_ring("w1_codes", h, [P, K], U32)
@@ -301,8 +295,8 @@ def tile_moe_bdx_mlp_relu2_kernel(tc, dyT, a, w2, w1, gate, offs, out):
             if e + 2 < E:
                 load_w2(e + 2)
             quantize_w2(e, 0)
-            form_da(e, 0)
             quantize_w2(e, 1)
+            form_da(e, 0)
             quantize_da(e, 0)
             form_da(e, 1)
             quantize_w1(e, 0)

@@ -45,7 +45,6 @@ RINGS = {
     "w1_codes": (1536, 2),
     "da_mixed": (4096, 3),
     "da_codes": (2048, 3),
-    "da_scales": (512, 3),
     "result": (2048, 6),
 }
 
@@ -146,12 +145,12 @@ def tile_moe_bdx_mlp_relu2_kernel(tc, dyT, a, w2, w1, gate, offs, out):
 
         def gate_on_gpsimd(e):
             to = new_g_mixed(e)
-            for lo in range(0, C, C // 2):
-                slots = slice(lo, lo + C // 2)
+            for lo in range(0, C, C // 4):
+                slots = slice(lo, lo + C // 4)
                 nc.gpsimd.tensor_tensor(
                     to[:, slots, :].rearrange("p (c i) t -> p c t i", i=2),
                     gathered[e][:, :, slots].rearrange("p t (c i) -> p c t i", i=2),
-                    gates[e][:, slots].rearrange("p (c i) -> p c i", i=2).unsqueeze(2).to_broadcast([P, C // 4, J, 2]),
+                    gates[e][:, slots].rearrange("p (c i) -> p c i", i=2).unsqueeze(2).to_broadcast([P, C // 8, J, 2]),
                     MULT,
                 )
 
@@ -163,7 +162,8 @@ def tile_moe_bdx_mlp_relu2_kernel(tc, dyT, a, w2, w1, gate, offs, out):
             quantize(g_mx[e][0][:], g_mx[e][1][:], g_mixed[e][:].rearrange("p c t -> p (c t)"), E5M2)
 
         def mix_w2(e, h, on_scalar):
-            w2_mixed[e, h] = in_ring("w2_mixed", HALVES * e + h, [P, J, P, J], BF16)
+            at = ring_at("w2_mixed", HALVES * e + h) if e or h else ring_at("gathered", 0)
+            w2_mixed[e, h] = placed("w2_mixed", [P, J, P, J], BF16, at)
             to = w2_mixed[e, h][:].rearrange("p t m j -> p m j t")
             source = w2_raw[e][:, :, h * P * J : (h + 1) * P * J].rearrange("p j (m t) -> p m j t", t=J)
             if on_scalar:
@@ -223,7 +223,8 @@ def tile_moe_bdx_mlp_relu2_kernel(tc, dyT, a, w2, w1, gate, offs, out):
 
         def quantize_da(e, h):
             index = HALVES * e + h
-            da_mx[e, h] = in_ring("da_codes", index, [P, C], U32), in_ring("da_scales", index, [P, C], U8)
+            scales = placed("da_scales", [P, C], U8, ring_at("a_raw", HALVES * e + 1) + 1024 + 512 * h)
+            da_mx[e, h] = in_ring("da_codes", index, [P, C], U32), scales
             quantize(da_mx[e, h][0][:], da_mx[e, h][1][:], da_mixed[e, h][:].rearrange("p c t -> p (c t)"), E5M2)
 
         def input_gradient(e, k):
@@ -282,7 +283,6 @@ def tile_moe_bdx_mlp_relu2_kernel(tc, dyT, a, w2, w1, gate, offs, out):
         gate_on_vector(0)
         gate_on_vector(1)
         gate_on_gpsimd(2)
-        gate_on_gpsimd(3)
         quantize_g(0)
         quantize_g(1)
 
@@ -295,10 +295,14 @@ def tile_moe_bdx_mlp_relu2_kernel(tc, dyT, a, w2, w1, gate, offs, out):
             if e + 2 < E:
                 load_w2(e + 2)
             quantize_w2(e, 0)
+            if first:
+                gate_on_gpsimd(3)
+                form_da(e, 0)
             quantize_w2(e, 1)
-            form_da(e, 0)
-            quantize_da(e, 0)
+            if not first:
+                form_da(e, 0)
             form_da(e, 1)
+            quantize_da(e, 0)
             quantize_w1(e, 0)
             quantize_w1(e, 1)
             quantize_da(e, 1)

@@ -27,7 +27,7 @@ COPY = mybir.ActivationFunctionType.Copy
 
 BANK = 2048
 DH_BANKS = 5
-A_PITCH = 512
+A_PITCH = 521
 
 RINGS = {
     "w2_raw": (16384, 2),
@@ -38,10 +38,9 @@ RINGS = {
     "g_mixed": (4096, 3),
     "g_codes": (2048, 2),
     "g_scales": (512, 2),
-    "w2_mixed": (4096, 3),
+    "w_mixed": (4096, 2),
     "w2_codes": (2048, 3),
     "w2_scales": (512, 3),
-    "w1_mixed": (3072, 2),
     "w1_codes": (1536, 2),
     "da_mixed": (4096, 3),
     "da_codes": (2048, 3),
@@ -66,8 +65,8 @@ def tile_moe_bdx_mlp_relu2_kernel(tc, dyT, a, w2, w1, gate, offs, out):
         psum = ctx.enter_context(tc.psum_pool(name="psum", bufs=1))
 
         offsets = held.tile([P, E * C // 16], U16, name="offsets")
-        tokens = [held.tile([P, T], F32, name=f"tokens{t}", tag=f"columns{t}") for t in range(J)]
-        windows = [held.tile([P, T], F32, name=f"window{k}", tag=f"columns{k}") for k in range(K_TILES)]
+        tokens = [held.tile([P, T], F32, name=f"tokens{t}", tag=f"columns{t}", align_bytes=256) for t in range(J)]
+        windows = [held.tile([P, T], F32, name=f"window{k}", tag=f"columns{k}", align_bytes=256) for k in range(K_TILES)]
         gate_rows = held.tile([P, E, J], F32, name="gate_rows")
 
         identity = held.tile([P, P], F32, name="identity")
@@ -90,7 +89,7 @@ def tile_moe_bdx_mlp_relu2_kernel(tc, dyT, a, w2, w1, gate, offs, out):
         dx_banks, results = {}, {}
 
         def placed(name, shape, dtype, at):
-            return rings.tile(shape, dtype, name=f"{name}_at{at}", align_bytes=64, offset=at)
+            return rings.tile(shape, dtype, name=f"{name}_at{at}", align_bytes=64 if at % 256 else 256, offset=at)
 
         def in_ring(name, index, shape, dtype):
             return placed(name, shape, dtype, ring_at(name, index))
@@ -162,7 +161,7 @@ def tile_moe_bdx_mlp_relu2_kernel(tc, dyT, a, w2, w1, gate, offs, out):
             quantize(g_mx[e][0][:], g_mx[e][1][:], g_mixed[e][:].rearrange("p c t -> p (c t)"), E5M2)
 
         def mix_w2(e, h, on_scalar):
-            at = ring_at("w2_mixed", HALVES * e + h) if e or h else ring_at("gathered", 0)
+            at = ring_at("w_mixed", h) if e or h else ring_at("gathered", 0)
             w2_mixed[e, h] = placed("w2_mixed", [P, J, P, J], BF16, at)
             to = w2_mixed[e, h][:].rearrange("p t m j -> p m j t")
             source = w2_raw[e][:, :, h * P * J : (h + 1) * P * J].rearrange("p j (m t) -> p m j t", t=J)
@@ -178,7 +177,7 @@ def tile_moe_bdx_mlp_relu2_kernel(tc, dyT, a, w2, w1, gate, offs, out):
             quantize(codes[:], scales[:], w2_mixed[e, h][:].rearrange("p t m j -> p (t m j)"), E4M3)
 
         def mix_w1(e, h, on_scalar):
-            w1_mixed[e, h] = in_ring("w1_mixed", h, [P, K, J], BF16)
+            w1_mixed[e, h] = placed("w1_mixed", [P, K, J], BF16, ring_at("w_mixed", 1 - h if e else h))
             to, source = w1_mixed[e, h][:], w1_raw[e][:, h, :, :]
             if on_scalar:
                 nc.scalar.activation(
@@ -290,8 +289,6 @@ def tile_moe_bdx_mlp_relu2_kernel(tc, dyT, a, w2, w1, gate, offs, out):
             first, last = e == 0, e == E - 1
             mix_w2(e, 0, first)
             mix_w2(e, 1, first)
-            mix_w1(e, 0, first)
-            mix_w1(e, 1, first)
             if e + 2 < E:
                 load_w2(e + 2)
             quantize_w2(e, 0)
@@ -299,6 +296,8 @@ def tile_moe_bdx_mlp_relu2_kernel(tc, dyT, a, w2, w1, gate, offs, out):
                 gate_on_gpsimd(3)
                 form_da(e, 0)
             quantize_w2(e, 1)
+            mix_w1(e, 0, first)
+            mix_w1(e, 1, first)
             if not first:
                 form_da(e, 0)
             form_da(e, 1)

@@ -27,24 +27,27 @@ COPY = mybir.ActivationFunctionType.Copy
 
 BANK = 2048
 DH_BANKS = 5
-A_PITCH = 521
 
 RINGS = {
     "w2_raw": (16384, 2),
-    "a_raw": (8448, 4),
+    "gate": (2048, 2),
+    "a_raw": (8192, 4),
     "w1_raw": (12288, 2),
     "gathered": (8192, 4),
-    "gate": (2048, 2),
-    "g_mixed": (4096, 3),
-    "g_codes": (2048, 2),
-    "g_scales": (512, 2),
-    "w_mixed": (4096, 2),
+    "last_tokens": (8192, 1),
+    "past_tokens": (2048, 1),
+    "g_mixed": (4096, 1),
+    "g_half": (2048, 1),
+    "g_codes": (1024, 8),
+    "g_scales": (512, 1),
+    "w_mixed": (9216, 1),
+    "first_w1": (3072, 2),
     "w2_codes": (2048, 3),
     "w2_scales": (512, 3),
     "w1_codes": (1536, 2),
-    "da_mixed": (4096, 3),
+    "da_mixed": (4096, 2),
     "da_codes": (2048, 3),
-    "result": (2048, 6),
+    "results": (6144, 2),
 }
 
 
@@ -65,7 +68,8 @@ def tile_moe_bdx_mlp_relu2_kernel(tc, dyT, a, w2, w1, gate, offs, out):
         psum = ctx.enter_context(tc.psum_pool(name="psum", bufs=1))
 
         offsets = held.tile([P, E * C // 16], U16, name="offsets")
-        tokens = [held.tile([P, T], F32, name=f"tokens{t}", tag=f"columns{t}", align_bytes=256) for t in range(J)]
+        tokens = [held.tile([P, T], F32, name=f"tokens{t}", tag=f"columns{t}", align_bytes=256) for t in range(K_TILES)]
+        tokens.append(rings.tile([P, T], F32, name="last_tokens", align_bytes=256, offset=ring_at("last_tokens", 0)))
         windows = [held.tile([P, T], F32, name=f"window{k}", tag=f"columns{k}", align_bytes=256) for k in range(K_TILES)]
         gate_rows = held.tile([P, E, J], F32, name="gate_rows")
 
@@ -94,17 +98,29 @@ def tile_moe_bdx_mlp_relu2_kernel(tc, dyT, a, w2, w1, gate, offs, out):
         def in_ring(name, index, shape, dtype):
             return placed(name, shape, dtype, ring_at(name, index))
 
+        twos_at = (ring_at("a_raw", 0) - 64, ring_at("results", 0))
+        twos = [placed("two", [P, 32], F32, at) for at in twos_at]
+        for two in twos:
+            nc.vector.memset(two[:, 0:1], 2.0)
+
+        first_a_at = ring_at("results", 0) + 256
+
         def listed(e, lo=0, hi=C):
             return offsets[:, (e * C + lo) // 16 : (e * C + hi) // 16]
+
+        def batch_at(e, h):
+            return ring_at("a_raw", HALVES * e + 1) + (4096 if e == E - 1 else 0)
 
         def load_w2(e):
             w2_raw[e] = in_ring("w2_raw", e, [P, J, H], F32)
             nc.sync.dma_start(w2_raw[e][:], w2[e].rearrange("(p j) i -> p j i", j=J))
 
-        def load_a(e, h):
-            tile = in_ring("a_raw", HALVES * e + h, [P, J, A_PITCH], F32)
-            a_raw[e, h] = tile
-            nc.sync.dma_start(tile[:, :, 0:C], a_rows[h][:, :, e * C : (e + 1) * C])
+        def load_a(e, h, lo=0, hi=C):
+            at = ring_at("a_raw", HALVES * e + h) + 16 * (C - hi) if e or h else first_a_at
+            tile = placed(f"a_raw{hi - lo}", [P, J, hi - lo], F32, at)
+            for first in range(lo, hi, GROUP):
+                a_raw[e, h, first] = tile[:, :, first - lo : first - lo + GROUP]
+            nc.sync.dma_start(tile[:], a_rows[h][:, :, e * C + lo : e * C + hi])
 
         def load_w1(e):
             w1_raw[e] = in_ring("w1_raw", e, [P, HALVES, J, K], F32)
@@ -113,13 +129,15 @@ def tile_moe_bdx_mlp_relu2_kernel(tc, dyT, a, w2, w1, gate, offs, out):
             )
 
         def spread_gate(e):
-            spread[e] = psum.tile([P, J, P], F32, name=f"spread{e}", offset=(DH_BANKS + e if e < E - 1 else DH_BANKS - 1) * BANK)
+            spread[e] = psum.tile([P, J, P], F32, name=f"spread{e}", offset=(5, 7, 4, 6)[e] * BANK)
             for c in range(J):
                 nc.tensor.transpose(spread[e][:, c, :], gate_rows[:, e, c : c + 1].to_broadcast([P, P]), identity[:])
 
-        def gate_to_sbuf(e):
-            gates[e] = in_ring("gate", e, [P, C], F32)
-            nc.scalar.activation(gates[e][:].rearrange("m (p c) -> m p c", c=J), spread[e][:].rearrange("m c p -> m p c"), COPY)
+        def gate_to_sbuf(e, lo, at):
+            gates[e] = placed(f"gate{lo}", [P, C - lo], F32, at)
+            nc.scalar.activation(
+                gates[e][:].rearrange("m (p c) -> m p c", c=J), spread[e][:, :, lo // J :].rearrange("m c p -> m p c"), COPY
+            )
 
         def gather(e, t, on_scalar):
             if t == 0:
@@ -129,55 +147,60 @@ def tile_moe_bdx_mlp_relu2_kernel(tc, dyT, a, w2, w1, gate, offs, out):
             else:
                 nc.vector.tensor_copy(gathered[e][:, t, :], tokens[t][:].indirect(listed(e)))
 
-        def new_g_mixed(e):
-            at = ring_at("g_mixed", e) if e < E - 1 else ring_at("gathered", 0)
-            g_mixed[e] = placed("g_mixed", [P, C, J], BF16, at)
-            return g_mixed[e]
-
-        def gate_on_vector(e):
+        def gate_on_vector(e, hi, at):
+            g_mixed[e, 0] = placed(f"g_mixed{hi}", [P, hi, J], BF16, at)
             nc.vector.tensor_tensor(
-                new_g_mixed(e)[:].rearrange("m (p c) t -> m p t c", c=J),
-                gathered[e][:].rearrange("m t (p c) -> m p t c", c=J),
-                spread[e][:].rearrange("m c p -> m p c").unsqueeze(2).to_broadcast([P, P, J, J]),
+                g_mixed[e, 0][:].rearrange("m (p c) t -> m p t c", c=J),
+                gathered[e][:, :, 0:hi].rearrange("m t (p c) -> m p t c", c=J),
+                spread[e][:, :, 0 : hi // J].rearrange("m c p -> m p c").unsqueeze(2).to_broadcast([P, hi // J, J, J]),
                 MULT,
             )
 
-        def gate_on_gpsimd(e):
-            to = new_g_mixed(e)
-            for lo in range(0, C, C // 4):
-                slots = slice(lo, lo + C // 4)
-                nc.gpsimd.tensor_tensor(
-                    to[:, slots, :].rearrange("p (c i) t -> p c t i", i=2),
-                    gathered[e][:, :, slots].rearrange("p t (c i) -> p c t i", i=2),
-                    gates[e][:, slots].rearrange("p (c i) -> p c i", i=2).unsqueeze(2).to_broadcast([P, C // 8, J, 2]),
-                    MULT,
-                )
+        def gate_on_gpsimd(e, lo, hi, at):
+            g_mixed[e, lo] = placed(f"g_mixed{hi - lo}", [P, hi - lo, J], BF16, at)
+            held_from = C - gates[e].shape[1]
+            nc.gpsimd.tensor_tensor(
+                g_mixed[e, lo][:].rearrange("p (c i) t -> p c t i", i=2),
+                gathered[e][:, :, lo:hi].rearrange("p t (c i) -> p c t i", i=2),
+                gates[e][:, lo - held_from : hi - held_from]
+                .rearrange("p (c i) -> p c i", i=2)
+                .unsqueeze(2)
+                .to_broadcast([P, (hi - lo) // 2, J, 2]),
+                MULT,
+            )
 
         def quantize(codes, scales, mixed, fmt):
             nc.vector.quantize_mx(out=codes.bitcast(fmt), scales=scales, in_=mixed)
 
-        def quantize_g(e):
-            g_mx[e] = in_ring("g_codes", e, [P, C], U32), in_ring("g_scales", e, [P, C], U8)
-            quantize(g_mx[e][0][:], g_mx[e][1][:], g_mixed[e][:].rearrange("p c t -> p (c t)"), E5M2)
+        def quantize_g(e, lo, hi, at):
+            codes = placed(f"g_codes{hi - lo}", [P, hi - lo], U32, ring_at("g_codes", 0) + 4 * (C * e + lo))
+            scales = placed(f"g_scales{hi - lo}", [P, hi - lo], U8, at)
+            quantize(codes[:], scales[:], g_mixed[e, lo][:].rearrange("p c t -> p (c t)"), E5M2)
+            for first in range(lo, hi, GROUP):
+                cols = slice(first - lo, first - lo + GROUP)
+                g_mx[e, first // GROUP] = codes[:, cols], scales[:, cols]
 
-        def mix_w2(e, h, on_scalar):
-            at = ring_at("w_mixed", h) if e or h else ring_at("gathered", 0)
+        def mix_w2(e, h, planes_on_scalar):
+            at = ring_at("w_mixed", 0) + (5056, 960)[h] if e or not h else ring_at("gathered", 0)
             w2_mixed[e, h] = placed("w2_mixed", [P, J, P, J], BF16, at)
             to = w2_mixed[e, h][:].rearrange("p t m j -> p m j t")
             source = w2_raw[e][:, :, h * P * J : (h + 1) * P * J].rearrange("p j (m t) -> p m j t", t=J)
-            if on_scalar:
-                nc.scalar.activation(to, source, COPY, scale=2.0)
-            else:
-                nc.vector.tensor_scalar(to, source, 2.0, None, MULT)
+            if planes_on_scalar:
+                t = slice(0, planes_on_scalar)
+                nc.scalar.activation(to[:, :, :, t], source[:, :, :, t], COPY, scale=twos[e][:, 0:1] if h else 2.0)
+            if planes_on_scalar < J:
+                t = slice(planes_on_scalar, J)
+                nc.vector.tensor_scalar(to[:, :, :, t], source[:, :, :, t], 2.0, None, MULT)
 
         def quantize_w2(e, h):
             codes = in_ring("w2_codes", HALVES * e + h, [P, P * J], U32)
-            scales = in_ring("w2_scales", HALVES * e + h, [P, P * J], U8)
+            at = ring_at("gathered", 0) + 2048 + 512 * h if e == 1 else ring_at("w2_scales", HALVES * e + h)
+            scales = placed("w2_scales", [P, P * J], U8, at)
             w2_mx[e, h] = codes, scales
             quantize(codes[:], scales[:], w2_mixed[e, h][:].rearrange("p t m j -> p (t m j)"), E4M3)
 
         def mix_w1(e, h, on_scalar):
-            w1_mixed[e, h] = placed("w1_mixed", [P, K, J], BF16, ring_at("w_mixed", 1 - h if e else h))
+            w1_mixed[e, h] = placed("w1_mixed", [P, K, J], BF16, (ring_at("w_mixed", 0) + 1024 if e else ring_at("first_w1", 0)) + 3072 * h)
             to, source = w1_mixed[e, h][:], w1_raw[e][:, h, :, :]
             if on_scalar:
                 nc.scalar.activation(
@@ -188,15 +211,17 @@ def tile_moe_bdx_mlp_relu2_kernel(tc, dyT, a, w2, w1, gate, offs, out):
 
         def quantize_w1(e, h):
             codes = in_ring("w1_codes", h, [P, K], U32)
-            scales = placed("w1_scales", [P, K], U8, ring_at("a_raw", HALVES * e + 1) + K * h)
+            scales = placed("w1_scales", [P, K], U8, batch_at(e, h) + K * h)
             w1_mx[e, h] = codes, scales
             quantize(codes[:], scales[:], w1_mixed[e, h][:].rearrange("p c j -> p (c j)"), E4M3)
 
-        def form_da(e, h):
+        def form_da(e, h, lo=0, hi=C):
             w2_codes, w2_scales = w2_mx[e, h]
-            g_codes, g_scales = g_mx[e]
-            da_mixed[e, h] = in_ring("da_mixed", HALVES * e + h, [P, C, J], BF16)
-            for s in range(C // GROUP):
+            at = ring_at("da_mixed", h) if e > 2 or h else ring_at("last_tokens", 0) + (0, 4096, 6144)[e]
+            if lo:
+                at = ring_at("w_mixed", 0) + 4096
+            da_mixed[e, h, lo] = placed(f"da_mixed{hi - lo}", [P, hi - lo, J], BF16, at)
+            for s in range(lo // GROUP, hi // GROUP):
                 slots = slice(s * GROUP, (s + 1) * GROUP)
                 b = ((HALVES * e + h) * (C // GROUP) + s) % DH_BANKS
                 dh = psum.tile([P, J, GROUP], F32, name=f"dh{b}", offset=b * BANK)
@@ -206,57 +231,69 @@ def tile_moe_bdx_mlp_relu2_kernel(tc, dyT, a, w2, w1, gate, offs, out):
                         out=dh[:, t, :],
                         lhsT=w2_codes[:, cols].bitcast(E4M3),
                         lhsT_scale=w2_scales[:, cols],
-                        rhs=g_codes[:, slots].bitcast(E5M2),
-                        rhs_scale=g_scales[:, slots],
+                        rhs=g_mx[e, s][0].bitcast(E5M2),
+                        rhs_scale=g_mx[e, s][1],
                         start=True,
                         stop=True,
                     )
                 nc.vector.scalar_tensor_tensor(
-                    da_mixed[e, h][:, slots, :],
-                    a_raw[e, h][:, :, slots].rearrange("p t c -> p c t"),
+                    da_mixed[e, h, lo][:, s * GROUP - lo : (s + 1) * GROUP - lo, :],
+                    a_raw[e, h, s * GROUP].rearrange("p t c -> p c t"),
                     0.0,
                     dh[:].rearrange("p t c -> p c t"),
                     MAX,
                     MULT,
                 )
 
-        def quantize_da(e, h):
-            index = HALVES * e + h
-            scales = placed("da_scales", [P, C], U8, ring_at("a_raw", HALVES * e + 1) + 1024 + 512 * h)
-            da_mx[e, h] = in_ring("da_codes", index, [P, C], U32), scales
-            quantize(da_mx[e, h][0][:], da_mx[e, h][1][:], da_mixed[e, h][:].rearrange("p c t -> p (c t)"), E5M2)
+        def quantize_da(e, h, lo=0, hi=C):
+            codes = placed(f"da_codes{hi - lo}", [P, hi - lo], U32, ring_at("da_codes", HALVES * e + h) + 4 * lo)
+            at = batch_at(e, h) + 1024 + 512 * h + lo
+            scales = placed(f"da_scales{hi - lo}", [P, hi - lo], U8, at)
+            quantize(codes[:], scales[:], da_mixed[e, h, lo][:].rearrange("p c t -> p (c t)"), E5M2)
+            for first in range(lo, hi, PIECE):
+                da_mx[e, h, first] = codes, scales, lo
 
-        def input_gradient(e, k):
-            dx = psum.tile([P, C], F32, name=f"dx{k}", offset=(DH_BANKS + k) * BANK)
+        def input_gradient(e, k, lo=0, hi=C):
+            b = DH_BANKS + k if lo == 0 else k
+            dx = psum.tile([P, hi - lo], F32, name=f"dx{b}_{hi - lo}", offset=b * BANK)
             cols = slice(k * P, (k + 1) * P)
             for h in range(HALVES):
+                codes, scales, first = da_mx[e, h, lo]
                 nc.tensor.matmul_mx(
                     out=dx[:],
                     lhsT=w1_mx[e, h][0][:, cols].bitcast(E4M3),
                     lhsT_scale=w1_mx[e, h][1][:, cols],
-                    rhs=da_mx[e, h][0][:].bitcast(E5M2),
-                    rhs_scale=da_mx[e, h][1][:],
+                    rhs=codes[:, lo - first : hi - first].bitcast(E5M2),
+                    rhs_scale=scales[:, lo - first : hi - first],
                     start=(h == 0),
                     stop=(h == HALVES - 1),
                 )
-            dx_banks[e, k] = dx
+            dx_banks[e, k, lo] = dx
 
-        def copy_out(e, k, on_scalar):
-            results[e, k] = in_ring("result", K_TILES * e + k, [P, C], F32)
+        def copy_out(e, k, on_scalar, lo=0, hi=C):
+            if e not in results:
+                results[e] = in_ring("results", e, [P, K_TILES, C], F32)
             if on_scalar:
-                nc.scalar.activation(results[e, k][:], dx_banks[e, k][:], COPY)
+                nc.scalar.activation(results[e][:, k, lo:hi], dx_banks[e, k, lo][:], COPY)
             else:
-                nc.vector.tensor_copy(results[e, k][:], dx_banks[e, k][:])
+                nc.vector.tensor_copy(results[e][:, k, lo:hi], dx_banks[e, k, lo][:])
 
         def scatter(e, k, lo, hi, on_scalar):
             to = windows[k][:].indirect(listed(e, lo, hi))
             if on_scalar:
-                nc.scalar.activation(to, results[e, k][:, lo:hi], COPY)
+                nc.scalar.activation(to, results[e][:, k, lo:hi], COPY)
             else:
-                nc.vector.tensor_copy(to, results[e, k][:, lo:hi])
+                nc.vector.tensor_copy(to, results[e][:, k, lo:hi])
 
-        def store(k):
-            nc.sync.dma_start(out[k * P : (k + 1) * P, :], windows[k][:])
+        def put_back(e):
+            for k in range(K_TILES):
+                copy_out(e, k, True)
+            for lo in range(0, C, PIECE):
+                for k in range(K_TILES):
+                    scatter(e, k, lo, lo + PIECE, True)
+
+        def store(k, queue):
+            queue.dma_start(out[k * P : (k + 1) * P, :], windows[k][:])
 
         nc.scalar.dma_start(gate_rows[:], gate[0].rearrange("(e p c) -> p e c", p=P, c=J))
         nc.sync.dma_start(offsets[:], offs)
@@ -270,64 +307,93 @@ def tile_moe_bdx_mlp_relu2_kernel(tc, dyT, a, w2, w1, gate, offs, out):
             if e == 1:
                 break
 
-        for e in range(E):
+        for e in (1, 0, 2, 3):
             spread_gate(e)
-        gate_to_sbuf(3)
-        gate_to_sbuf(2)
+        gate_to_sbuf(1, 0, ring_at("gate", 0))
         for t in range(J):
             gather(0, t, False)
             gather(1, t, True)
-            gather(2, t, t == J - 1)
+            if t < J - 1:
+                gather(2, t, False)
             gather(3, t, True)
-        gate_on_vector(0)
-        gate_on_vector(1)
-        gate_on_gpsimd(2)
-        quantize_g(0)
-        quantize_g(1)
+        gather(2, J - 1, True)
+        gate_on_vector(0, C, ring_at("g_mixed", 0))
+        gate_on_gpsimd(1, 0, C // 2, ring_at("g_half", 0))
+        spare = ring_at("last_tokens", 0)
 
         for e in range(E):
-            first, last = e == 0, e == E - 1
-            mix_w2(e, 0, first)
-            mix_w2(e, 1, first)
+            first = e == 0
+            if first:
+                quantize_g(0, 0, C, ring_at("g_scales", 0))
+            mix_w2(e, 0, J if e == 1 else 0)
+            mix_w2(e, 1, (J, 2, 0, 0)[e])
+            if first:
+                gate_to_sbuf(2, 0, ring_at("gate", 1))
+            else:
+                put_back(e - 1)
             if e + 2 < E:
                 load_w2(e + 2)
             quantize_w2(e, 0)
-            if first:
-                gate_on_gpsimd(3)
-                form_da(e, 0)
             quantize_w2(e, 1)
+            if first:
+                gate_on_gpsimd(1, C // 2, C, ring_at("gathered", 0))
+                gate_on_gpsimd(2, 0, C, ring_at("gathered", 0) + 2048)
+            if e in (1, 2):
+                gate_on_gpsimd(3, (e + 1) * GROUP, (e + 2) * GROUP, ring_at("w_mixed", 0))
             mix_w1(e, 0, first)
             mix_w1(e, 1, first)
-            if not first:
-                form_da(e, 0)
+            form_da(e, 0)
+            if first:
+                gate_on_vector(3, C // 2, first_a_at)
+                gate_to_sbuf(3, C // 2, ring_at("gate", 0))
+            if e == E - 1:
+                break
             form_da(e, 1)
             quantize_da(e, 0)
             quantize_w1(e, 0)
             quantize_w1(e, 1)
             quantize_da(e, 1)
+            if first:
+                quantize_g(1, 0, C // 2, spare)
+                quantize_g(1, C // 2, C, spare + 256)
+                quantize_g(3, 0, C // 2, spare + 512)
+                quantize_g(2, 0, C, spare + 1024)
+            if e in (1, 2):
+                quantize_g(3, (e + 1) * GROUP, (e + 2) * GROUP, spare + 2048 + 2048 * e)
             for k in range(K_TILES):
                 input_gradient(e, k)
             if e + 2 < E:
                 load_a(e + 2, 0)
                 load_w1(e + 2)
-                load_a(e + 2, 1)
-                quantize_g(e + 2)
-            if not last:
-                for k in range(K_TILES):
-                    copy_out(e, k, True)
-                for lo in range(0, C, PIECE):
-                    for k in range(K_TILES):
-                        scatter(e, k, lo, lo + PIECE, True)
+                if first:
+                    load_a(e + 2, 1)
+                else:
+                    load_a(e + 2, 1, 0, PIECE)
+                    load_a(e + 2, 1, PIECE, C)
 
         e = E - 1
-        copy_out(e, 0, True)
-        copy_out(e, 1, False)
-        copy_out(e, 2, True)
+        form_da(e, 1, 0, PIECE)
+        quantize_da(e, 0)
+        quantize_w1(e, 0)
+        quantize_w1(e, 1)
+        quantize_da(e, 1, 0, PIECE)
+        for k in (1, 0, 2):
+            input_gradient(e, k, 0, PIECE)
+        form_da(e, 1, PIECE, C)
+        quantize_da(e, 1, PIECE, C)
+        for k in (1, 2, 0):
+            input_gradient(e, k, PIECE, C)
+        copy_out(e, 1, True, 0, PIECE)
+        copy_out(e, 0, True, 0, PIECE)
+        scatter(e, 1, 0, PIECE, True)
+        copy_out(e, 2, False, 0, PIECE)
+        copy_out(e, 1, False, PIECE, C)
+        copy_out(e, 2, False, PIECE, C)
+        scatter(e, 1, PIECE, C, False)
+        store(1, nc.sync)
         scatter(e, 0, 0, PIECE, True)
-        scatter(e, 1, 0, C, False)
+        copy_out(e, 0, True, PIECE, C)
         scatter(e, 0, PIECE, C, True)
-        store(0)
-        store(1)
-        scatter(e, 2, 0, PIECE, True)
-        scatter(e, 2, PIECE, C, False)
-        store(2)
+        store(0, nc.scalar)
+        scatter(e, 2, 0, C, False)
+        store(2, nc.sync)

@@ -25,22 +25,22 @@ MAX = mybir.AluOpType.max
 ADD = mybir.AluOpType.add
 COPY = mybir.ActivationFunctionType.Copy
 
+KEPT_FROM = T - 3 * PIECE
 BANK = 2048
 DH_BANKS = 5
 
 RINGS = {
     "w2_raw": (16384, 2),
-    "gate": (2048, 2),
     "a_raw": (8192, 4),
-    "w1_raw": (12288, 2),
+    "w1_raw": (6144, 4),
+    "w1_past": (2048, 1),
     "gathered": (8192, 4),
     "last_tokens": (8192, 1),
-    "past_tokens": (2048, 1),
-    "g_mixed": (4096, 1),
-    "g_half": (2048, 1),
+    "g_mixed": (4096, 3),
     "g_codes": (1024, 8),
+    "gate": (2048, 2),
     "g_scales": (512, 1),
-    "w_mixed": (9216, 1),
+    "w_mixed": (8192, 1),
     "first_w1": (3072, 2),
     "w2_codes": (2048, 3),
     "w2_scales": (512, 3),
@@ -48,6 +48,7 @@ RINGS = {
     "da_mixed": (4096, 2),
     "da_codes": (2048, 3),
     "results": (6144, 2),
+    "kept": (3072, 1),
 }
 
 
@@ -90,7 +91,7 @@ def tile_moe_bdx_mlp_relu2_kernel(tc, dyT, a, w2, w1, gate, offs, out):
         w2_raw, a_raw, w1_raw, gathered, spread, gates = {}, {}, {}, {}, {}, {}
         g_mixed, w2_mixed, w1_mixed, da_mixed = {}, {}, {}, {}
         g_mx, w2_mx, w1_mx, da_mx = {}, {}, {}, {}
-        dx_banks, results = {}, {}
+        dx_banks, results, kept = {}, {}, []
 
         def placed(name, shape, dtype, at):
             return rings.tile(shape, dtype, name=f"{name}_at{at}", align_bytes=64 if at % 256 else 256, offset=at)
@@ -98,35 +99,38 @@ def tile_moe_bdx_mlp_relu2_kernel(tc, dyT, a, w2, w1, gate, offs, out):
         def in_ring(name, index, shape, dtype):
             return placed(name, shape, dtype, ring_at(name, index))
 
-        twos_at = (ring_at("a_raw", 0) - 64, ring_at("results", 0))
+        twos_at = (ring_at("g_scales", 0) - 64, ring_at("results", 0))
         twos = [placed("two", [P, 32], F32, at) for at in twos_at]
         for two in twos:
             nc.vector.memset(two[:, 0:1], 2.0)
 
-        first_a_at = ring_at("results", 0) + 256
 
         def listed(e, lo=0, hi=C):
             return offsets[:, (e * C + lo) // 16 : (e * C + hi) // 16]
 
+        w1_places = [ring_at("w1_raw", place) for place in range(4)]
+        w1_at = ((w1_places[0], w1_places[3]), w1_places[1:3], (w1_places[0], ring_at("a_raw", 1)), w1_places[1:3])
+
+        def a_at(e, h):
+            return w1_places[3] if (e, h) == (2, 1) else ring_at("a_raw", HALVES * e + h)
+
         def batch_at(e, h):
-            return ring_at("a_raw", HALVES * e + 1) + (4096 if e == E - 1 else 0)
+            return a_at(e, 1) + (4096 if e == E - 1 else 0)
 
         def load_w2(e):
             w2_raw[e] = in_ring("w2_raw", e, [P, J, H], F32)
             nc.sync.dma_start(w2_raw[e][:], w2[e].rearrange("(p j) i -> p j i", j=J))
 
         def load_a(e, h, lo=0, hi=C):
-            at = ring_at("a_raw", HALVES * e + h) + 16 * (C - hi) if e or h else first_a_at
+            at = a_at(e, h) + 16 * (C - hi)
             tile = placed(f"a_raw{hi - lo}", [P, J, hi - lo], F32, at)
             for first in range(lo, hi, GROUP):
                 a_raw[e, h, first] = tile[:, :, first - lo : first - lo + GROUP]
             nc.sync.dma_start(tile[:], a_rows[h][:, :, e * C + lo : e * C + hi])
 
-        def load_w1(e):
-            w1_raw[e] = in_ring("w1_raw", e, [P, HALVES, J, K], F32)
-            nc.sync.dma_start(
-                w1_raw[e][:].rearrange("p h j k -> p h (j k)"), w1[e].rearrange("(h p j) k -> p h (j k)", p=P, j=J)
-            )
+        def load_w1(e, h):
+            w1_raw[e, h] = placed("w1_raw", [P, J, K], F32, w1_at[e][h])
+            nc.sync.dma_start(w1_raw[e, h][:], w1[e].rearrange("(h p j) k -> h p j k", p=P, j=J)[h])
 
         def spread_gate(e):
             spread[e] = psum.tile([P, J, P], F32, name=f"spread{e}", offset=(5, 7, 4, 6)[e] * BANK)
@@ -181,27 +185,27 @@ def tile_moe_bdx_mlp_relu2_kernel(tc, dyT, a, w2, w1, gate, offs, out):
                 g_mx[e, first // GROUP] = codes[:, cols], scales[:, cols]
 
         def mix_w2(e, h, planes_on_scalar):
-            at = ring_at("w_mixed", 0) + (5056, 960)[h] if e or not h else ring_at("gathered", 0)
+            at = ring_at("w_mixed", 0) + (4096, 0)[h] if e or not h else ring_at("gathered", 0)
             w2_mixed[e, h] = placed("w2_mixed", [P, J, P, J], BF16, at)
             to = w2_mixed[e, h][:].rearrange("p t m j -> p m j t")
             source = w2_raw[e][:, :, h * P * J : (h + 1) * P * J].rearrange("p j (m t) -> p m j t", t=J)
             if planes_on_scalar:
                 t = slice(0, planes_on_scalar)
-                nc.scalar.activation(to[:, :, :, t], source[:, :, :, t], COPY, scale=twos[e][:, 0:1] if h else 2.0)
+                nc.scalar.activation(to[:, :, :, t], source[:, :, :, t], COPY, scale=twos[e][:, 0:1] if e == h else 2.0)
             if planes_on_scalar < J:
-                t = slice(planes_on_scalar, J)
-                nc.vector.tensor_scalar(to[:, :, :, t], source[:, :, :, t], 2.0, None, MULT)
+                for t in range(planes_on_scalar, J, 2):
+                    nc.vector.tensor_scalar(to[:, :, :, t : t + 2], source[:, :, :, t : t + 2], 2.0, None, MULT)
 
         def quantize_w2(e, h):
             codes = in_ring("w2_codes", HALVES * e + h, [P, P * J], U32)
-            at = ring_at("gathered", 0) + 2048 + 512 * h if e == 1 else ring_at("w2_scales", HALVES * e + h)
+            at = ring_at("gathered", 0) + 512 * h if e == 1 else ring_at("w2_scales", HALVES * e + h)
             scales = placed("w2_scales", [P, P * J], U8, at)
             w2_mx[e, h] = codes, scales
             quantize(codes[:], scales[:], w2_mixed[e, h][:].rearrange("p t m j -> p (t m j)"), E4M3)
 
         def mix_w1(e, h, on_scalar):
-            w1_mixed[e, h] = placed("w1_mixed", [P, K, J], BF16, (ring_at("w_mixed", 0) + 1024 if e else ring_at("first_w1", 0)) + 3072 * h)
-            to, source = w1_mixed[e, h][:], w1_raw[e][:, h, :, :]
+            w1_mixed[e, h] = placed("w1_mixed", [P, K, J], BF16, (ring_at("w_mixed", 0) if e else ring_at("first_w1", 0)) + 3072 * h)
+            to, source = w1_mixed[e, h][:], w1_raw[e, h][:]
             if on_scalar:
                 nc.scalar.activation(
                     to.rearrange("p (c i) j -> p c j i", i=2), source.rearrange("p j (c i) -> p c j i", i=2), COPY
@@ -217,9 +221,9 @@ def tile_moe_bdx_mlp_relu2_kernel(tc, dyT, a, w2, w1, gate, offs, out):
 
         def form_da(e, h, lo=0, hi=C):
             w2_codes, w2_scales = w2_mx[e, h]
-            at = ring_at("da_mixed", h) if e > 2 or h else ring_at("last_tokens", 0) + (0, 4096, 6144)[e]
+            at = ring_at("da_mixed", h) if e or h else ring_at("last_tokens", 0)
             if lo:
-                at = ring_at("w_mixed", 0) + 4096
+                at = ring_at("w_mixed", 0) + 3072
             da_mixed[e, h, lo] = placed(f"da_mixed{hi - lo}", [P, hi - lo, J], BF16, at)
             for s in range(lo // GROUP, hi // GROUP):
                 slots = slice(s * GROUP, (s + 1) * GROUP)
@@ -254,8 +258,8 @@ def tile_moe_bdx_mlp_relu2_kernel(tc, dyT, a, w2, w1, gate, offs, out):
                 da_mx[e, h, first] = codes, scales, lo
 
         def input_gradient(e, k, lo=0, hi=C):
-            b = DH_BANKS + k if lo == 0 else k
-            dx = psum.tile([P, hi - lo], F32, name=f"dx{b}_{hi - lo}", offset=b * BANK)
+            b = DH_BANKS + k if lo == 0 or k == K_TILES - 1 else k
+            dx = psum.tile([P, hi - lo], F32, name=f"dx{b}_{lo}_{hi}", offset=b * BANK)
             cols = slice(k * P, (k + 1) * P)
             for h in range(HALVES):
                 codes, scales, first = da_mx[e, h, lo]
@@ -268,29 +272,44 @@ def tile_moe_bdx_mlp_relu2_kernel(tc, dyT, a, w2, w1, gate, offs, out):
                     start=(h == 0),
                     stop=(h == HALVES - 1),
                 )
-            dx_banks[e, k, lo] = dx
+            for part in range(lo, hi, PIECE):
+                dx_banks[e, k, part] = dx, lo
 
-        def copy_out(e, k, on_scalar, lo=0, hi=C):
+        def result_at(e, k, lo, hi):
+            if k == K_TILES - 1 and e * C + lo >= KEPT_FROM:
+                if not kept:
+                    kept.append(in_ring("kept", 0, [P, T - KEPT_FROM], F32))
+                return kept[0][:, e * C + lo - KEPT_FROM : e * C + hi - KEPT_FROM]
             if e not in results:
                 results[e] = in_ring("results", e, [P, K_TILES, C], F32)
+            return results[e][:, k, lo:hi]
+
+        def copy_out(e, k, on_scalar, lo=0, hi=C):
+            dx, first = dx_banks[e, k, lo]
             if on_scalar:
-                nc.scalar.activation(results[e][:, k, lo:hi], dx_banks[e, k, lo][:], COPY)
+                nc.scalar.activation(result_at(e, k, lo, hi), dx[:, lo - first : hi - first], COPY)
             else:
-                nc.vector.tensor_copy(results[e][:, k, lo:hi], dx_banks[e, k, lo][:])
+                nc.vector.tensor_copy(result_at(e, k, lo, hi), dx[:, lo - first : hi - first])
 
         def scatter(e, k, lo, hi, on_scalar):
             to = windows[k][:].indirect(listed(e, lo, hi))
             if on_scalar:
-                nc.scalar.activation(to, results[e][:, k, lo:hi], COPY)
+                nc.scalar.activation(to, result_at(e, k, lo, hi), COPY)
             else:
-                nc.vector.tensor_copy(to, results[e][:, k, lo:hi])
+                nc.vector.tensor_copy(to, result_at(e, k, lo, hi))
 
         def put_back(e):
-            for k in range(K_TILES):
-                copy_out(e, k, True)
+            order = (1, 0, 2)
+            for k in order:
+                if e == E - 2 and k == K_TILES - 1:
+                    copy_out(e, k, True, 0, PIECE)
+                    copy_out(e, k, True, PIECE, C)
+                else:
+                    copy_out(e, k, True)
             for lo in range(0, C, PIECE):
-                for k in range(K_TILES):
-                    scatter(e, k, lo, lo + PIECE, True)
+                for k in order:
+                    if not (k == K_TILES - 1 and e * C + lo >= KEPT_FROM):
+                        scatter(e, k, lo, lo + PIECE, True)
 
         def store(k, queue):
             queue.dma_start(out[k * P : (k + 1) * P, :], windows[k][:])
@@ -302,8 +321,9 @@ def tile_moe_bdx_mlp_relu2_kernel(tc, dyT, a, w2, w1, gate, offs, out):
         for e in range(E):
             load_w2(e)
             load_a(e, 0)
-            load_w1(e)
+            load_w1(e, 0)
             load_a(e, 1)
+            load_w1(e, 1)
             if e == 1:
                 break
 
@@ -318,34 +338,30 @@ def tile_moe_bdx_mlp_relu2_kernel(tc, dyT, a, w2, w1, gate, offs, out):
             gather(3, t, True)
         gather(2, J - 1, True)
         gate_on_vector(0, C, ring_at("g_mixed", 0))
-        gate_on_gpsimd(1, 0, C // 2, ring_at("g_half", 0))
-        spare = ring_at("last_tokens", 0)
+        gate_on_gpsimd(1, 0, C, ring_at("g_mixed", 1))
+        gate_on_vector(3, C, ring_at("g_mixed", 2))
 
         for e in range(E):
             first = e == 0
-            if first:
-                quantize_g(0, 0, C, ring_at("g_scales", 0))
-            mix_w2(e, 0, J if e == 1 else 0)
+            mix_w2(e, 0, J if e < 2 else 0)
             mix_w2(e, 1, (J, 2, 0, 0)[e])
             if first:
                 gate_to_sbuf(2, 0, ring_at("gate", 1))
+                quantize_g(0, 0, C, ring_at("g_scales", 0))
             else:
                 put_back(e - 1)
             if e + 2 < E:
                 load_w2(e + 2)
             quantize_w2(e, 0)
+            if first:
+                quantize_g(1, 0, C, ring_at("g_mixed", 0))
+                quantize_g(3, 0, C, ring_at("g_mixed", 0) + 512)
             quantize_w2(e, 1)
             if first:
-                gate_on_gpsimd(1, C // 2, C, ring_at("gathered", 0))
-                gate_on_gpsimd(2, 0, C, ring_at("gathered", 0) + 2048)
-            if e in (1, 2):
-                gate_on_gpsimd(3, (e + 1) * GROUP, (e + 2) * GROUP, ring_at("w_mixed", 0))
+                gate_on_gpsimd(2, 0, C, ring_at("gathered", 0))
             mix_w1(e, 0, first)
             mix_w1(e, 1, first)
             form_da(e, 0)
-            if first:
-                gate_on_vector(3, C // 2, first_a_at)
-                gate_to_sbuf(3, C // 2, ring_at("gate", 0))
             if e == E - 1:
                 break
             form_da(e, 1)
@@ -354,20 +370,17 @@ def tile_moe_bdx_mlp_relu2_kernel(tc, dyT, a, w2, w1, gate, offs, out):
             quantize_w1(e, 1)
             quantize_da(e, 1)
             if first:
-                quantize_g(1, 0, C // 2, spare)
-                quantize_g(1, C // 2, C, spare + 256)
-                quantize_g(3, 0, C // 2, spare + 512)
-                quantize_g(2, 0, C, spare + 1024)
-            if e in (1, 2):
-                quantize_g(3, (e + 1) * GROUP, (e + 2) * GROUP, spare + 2048 + 2048 * e)
-            for k in range(K_TILES):
+                quantize_g(2, 0, C, ring_at("last_tokens", 0))
+            for k in (1, 0, 2):
                 input_gradient(e, k)
             if e + 2 < E:
                 load_a(e + 2, 0)
-                load_w1(e + 2)
+                load_w1(e + 2, 0)
                 if first:
                     load_a(e + 2, 1)
+                    load_w1(e + 2, 1)
                 else:
+                    load_w1(e + 2, 1)
                     load_a(e + 2, 1, 0, PIECE)
                     load_a(e + 2, 1, PIECE, C)
 
@@ -380,20 +393,20 @@ def tile_moe_bdx_mlp_relu2_kernel(tc, dyT, a, w2, w1, gate, offs, out):
         for k in (1, 0, 2):
             input_gradient(e, k, 0, PIECE)
         form_da(e, 1, PIECE, C)
+        copy_out(e, 2, False, 0, PIECE)
         quantize_da(e, 1, PIECE, C)
-        for k in (1, 2, 0):
+        for k in (1, 0, 2):
             input_gradient(e, k, PIECE, C)
         copy_out(e, 1, True, 0, PIECE)
         copy_out(e, 0, True, 0, PIECE)
         scatter(e, 1, 0, PIECE, True)
-        copy_out(e, 2, False, 0, PIECE)
+        scatter(e, 0, 0, PIECE, True)
         copy_out(e, 1, False, PIECE, C)
-        copy_out(e, 2, False, PIECE, C)
         scatter(e, 1, PIECE, C, False)
         store(1, nc.sync)
-        scatter(e, 0, 0, PIECE, True)
         copy_out(e, 0, True, PIECE, C)
+        copy_out(e, 2, False, PIECE, C)
         scatter(e, 0, PIECE, C, True)
         store(0, nc.scalar)
-        scatter(e, 2, 0, C, False)
+        scatter(E - 2, 2, PIECE, 2 * C, False)
         store(2, nc.sync)

@@ -32,6 +32,7 @@ DH_BANKS = 5
 RINGS = {
     "w2_raw": (16384, 2),
     "a_raw": (8192, 4),
+    "first_w1": (3072, 2),
     "w1_raw": (6144, 4),
     "w1_past": (2048, 1),
     "gathered": (8192, 4),
@@ -41,7 +42,6 @@ RINGS = {
     "gate": (2048, 2),
     "g_scales": (512, 1),
     "w_mixed": (8192, 1),
-    "first_w1": (3072, 2),
     "w2_codes": (2048, 3),
     "w2_scales": (512, 3),
     "w1_codes": (1536, 2),
@@ -109,17 +109,26 @@ def tile_moe_bdx_mlp_relu2_kernel(tc, dyT, a, w2, w1, gate, offs, out):
             return offsets[:, (e * C + lo) // 16 : (e * C + hi) // 16]
 
         w1_places = [ring_at("w1_raw", place) for place in range(4)]
-        w1_at = ((w1_places[0], w1_places[3]), w1_places[1:3], (w1_places[0], ring_at("a_raw", 1)), w1_places[1:3])
+        w1_at = (
+            (w1_places[0], w1_places[1]),
+            (w1_places[3], w1_places[2]),
+            (ring_at("last_tokens", 0) + 2048, ring_at("a_raw", 1)),
+            (ring_at("a_raw", 3), ring_at("a_raw", 3) + 6144),
+        )
 
         def a_at(e, h):
-            return w1_places[3] if (e, h) == (2, 1) else ring_at("a_raw", HALVES * e + h)
+            moved = {(2, 1): ring_at("gathered", 0) + 1024, (3, 0): w1_places[3]}
+            return moved.get((e, h), ring_at("a_raw", (0, 1, 3, 2)[(HALVES * e + h) % 4]))
 
         def batch_at(e, h):
             return a_at(e, 1) + (4096 if e == E - 1 else 0)
 
-        def load_w2(e):
-            w2_raw[e] = in_ring("w2_raw", e, [P, J, H], F32)
-            nc.sync.dma_start(w2_raw[e][:], w2[e].rearrange("(p j) i -> p j i", j=J))
+        def load_w2(e, halves=(0, 1)):
+            cols = slice(halves[0] * P * J, (halves[-1] + 1) * P * J)
+            tile = placed(f"w2_raw{len(halves)}", [P, J, len(halves) * P * J], F32, ring_at("w2_raw", e) + 8192 * halves[0])
+            for h in halves:
+                w2_raw[e, h] = tile[:, :, (h - halves[0]) * P * J : (h - halves[0] + 1) * P * J]
+            nc.sync.dma_start(tile[:], w2[e].rearrange("(p j) i -> p j i", j=J)[:, :, cols])
 
         def load_a(e, h, lo=0, hi=C):
             at = a_at(e, h) + 16 * (C - hi)
@@ -188,7 +197,7 @@ def tile_moe_bdx_mlp_relu2_kernel(tc, dyT, a, w2, w1, gate, offs, out):
             at = ring_at("w_mixed", 0) + (4096, 0)[h] if e or not h else ring_at("gathered", 0)
             w2_mixed[e, h] = placed("w2_mixed", [P, J, P, J], BF16, at)
             to = w2_mixed[e, h][:].rearrange("p t m j -> p m j t")
-            source = w2_raw[e][:, :, h * P * J : (h + 1) * P * J].rearrange("p j (m t) -> p m j t", t=J)
+            source = w2_raw[e, h].rearrange("p j (m t) -> p m j t", t=J)
             if planes_on_scalar:
                 t = slice(0, planes_on_scalar)
                 nc.scalar.activation(to[:, :, :, t], source[:, :, :, t], COPY, scale=twos[e][:, 0:1] if e == h else 2.0)
@@ -204,7 +213,8 @@ def tile_moe_bdx_mlp_relu2_kernel(tc, dyT, a, w2, w1, gate, offs, out):
             quantize(codes[:], scales[:], w2_mixed[e, h][:].rearrange("p t m j -> p (t m j)"), E4M3)
 
         def mix_w1(e, h, on_scalar):
-            w1_mixed[e, h] = placed("w1_mixed", [P, K, J], BF16, (ring_at("w_mixed", 0) if e else ring_at("first_w1", 0)) + 3072 * h)
+            at = (ring_at("w_mixed", 0) if e else ring_at("first_w1", 0)) + 3072 * h
+            w1_mixed[e, h] = placed("w1_mixed", [P, K, J], BF16, ring_at("g_mixed", 1) if (e, h) == (1, 1) else at)
             to, source = w1_mixed[e, h][:], w1_raw[e, h][:]
             if on_scalar:
                 nc.scalar.activation(
@@ -221,7 +231,7 @@ def tile_moe_bdx_mlp_relu2_kernel(tc, dyT, a, w2, w1, gate, offs, out):
 
         def form_da(e, h, lo=0, hi=C):
             w2_codes, w2_scales = w2_mx[e, h]
-            at = ring_at("da_mixed", h) if e or h else ring_at("last_tokens", 0)
+            at = {(0, 0): ring_at("last_tokens", 0), (1, 0): ring_at("w_mixed", 0) + 3072}.get((e, h), ring_at("da_mixed", h))
             if lo:
                 at = ring_at("w_mixed", 0) + 3072
             da_mixed[e, h, lo] = placed(f"da_mixed{hi - lo}", [P, hi - lo, J], BF16, at)
@@ -318,14 +328,17 @@ def tile_moe_bdx_mlp_relu2_kernel(tc, dyT, a, w2, w1, gate, offs, out):
         nc.sync.dma_start(offsets[:], offs)
         for t in range(J):
             nc.sync.dma_start(tokens[t][:], dy_rows[:, t, :])
-        for e in range(E):
-            load_w2(e)
-            load_a(e, 0)
-            load_w1(e, 0)
-            load_a(e, 1)
-            load_w1(e, 1)
-            if e == 1:
-                break
+        load_w2(0)
+        load_a(0, 0)
+        load_w1(0, 0)
+        load_a(0, 1)
+        load_w1(0, 1)
+        load_w2(1, (0,))
+        load_w2(1, (1,))
+        load_a(1, 0)
+        load_w1(1, 0)
+        load_a(1, 1)
+        load_w1(1, 1)
 
         for e in (1, 0, 2, 3):
             spread_gate(e)
@@ -344,7 +357,7 @@ def tile_moe_bdx_mlp_relu2_kernel(tc, dyT, a, w2, w1, gate, offs, out):
         for e in range(E):
             first = e == 0
             mix_w2(e, 0, J if e < 2 else 0)
-            mix_w2(e, 1, (J, 2, 0, 0)[e])
+            mix_w2(e, 1, (J, J, 0, 0)[e])
             if first:
                 gate_to_sbuf(2, 0, ring_at("gate", 1))
                 quantize_g(0, 0, C, ring_at("g_scales", 0))

from contextlib import ExitStack

import concourse.mybir as mybir

K, T, E, C, H, N = 384, 2048, 4, 512, 1024, 512
P = 128
J = 4
Q = 32
HALVES = H // (P * J)
K_TILES = K // P
GROUP = 128
PIECE = 256
FLOPS = 2 * E * C * (N * H + H * K)
BYTES = 4 * (N * T + H * E * C + E * N * H + E * H * K + E * C + K * T) + 2 * P * (E * C // 16)

F32 = mybir.dt.float32
BF16 = mybir.dt.bfloat16
U32 = mybir.dt.uint32
U16 = mybir.dt.uint16
U8 = mybir.dt.uint8
E4M3 = mybir.dt.float8_e4m3fn_x4
E5M2 = mybir.dt.float8_e5m2_x4
MULT = mybir.AluOpType.mult
MAX = mybir.AluOpType.max
ADD = mybir.AluOpType.add
COPY = mybir.ActivationFunctionType.Copy

KEPT_FROM = T - 3 * PIECE
BANK = 2048
DH_BANKS = 5

RINGS = {
    "w2_raw": (16384, 2),
    "a_raw": (8192, 4),
    "first_w1": (3072, 2),
    "w1_raw": (6144, 4),
    "w1_past": (2048, 1),
    "gathered": (8192, 4),
    "last_tokens": (8192, 1),
    "g_mixed": (4096, 3),
    "g_codes": (1024, 8),
    "gate": (2048, 2),
    "g_scales": (512, 1),
    "w_mixed": (8192, 1),
    "w2_codes": (2048, 3),
    "w2_scales": (512, 3),
    "w1_codes": (1536, 2),
    "da_mixed": (4096, 2),
    "da_codes": (2048, 3),
    "results": (6144, 2),
    "kept": (3072, 1),
}


def ring_at(name, index):
    start = 0
    for other, (size, places) in RINGS.items():
        if other == name:
            return start + size * (index % places)
        start = start + size * places
    raise ValueError(name)


def tile_moe_bdx_mlp_relu2_kernel(tc, dyT, a, w2, w1, gate, offs, out):
    nc = tc.nc
    with ExitStack() as ctx:
        held = ctx.enter_context(tc.tile_pool(name="held", bufs=1))
        rings = ctx.enter_context(tc.tile_pool(name="rings", bufs=1))
        psum = ctx.enter_context(tc.psum_pool(name="psum", bufs=1))

        offsets = held.tile([P, E * C // 16], U16, name="offsets")
        tokens = [held.tile([P, T], F32, name=f"tokens{t}", tag=f"columns{t}", align_bytes=256) for t in range(K_TILES)]
        tokens.append(rings.tile([P, T], F32, name="last_tokens", align_bytes=256, offset=ring_at("last_tokens", 0)))
        windows = [held.tile([P, T], F32, name=f"window{k}", tag=f"columns{k}", align_bytes=256) for k in range(K_TILES)]
        gate_rows = held.tile([P, E, J], F32, name="gate_rows")

        identity = held.tile([P, P], F32, name="identity")
        steps = held.tile([P, Q], F32, name="steps")
        column = held.tile([P, Q], F32, name="column", align_bytes=64)
        row = held.tile([P, Q], F32, name="row", align_bytes=64)
        nc.vector.memset(identity[:], 0.0)
        nc.vector.memset(steps[:], 1.0)
        nc.vector.tensor_tensor_scan(column[:], steps[:], steps[:], 0.0, MULT, ADD)
        nc.vector.transpose(row[:], column[:])
        for first in range(0, P, Q):
            square = slice(first, first + Q)
            nc.vector.tensor_tensor(identity[square, square], column[square, :], row[square, :], mybir.AluOpType.is_equal)

        dy_rows = dyT.rearrange("(p t) s -> p t s", t=J)
        a_rows = a.rearrange("(h p t) s -> h p t s", p=P, t=J)
        w2_raw, a_raw, w1_raw, gathered, spread, gates = {}, {}, {}, {}, {}, {}
        g_mixed, w2_mixed, w1_mixed, da_mixed = {}, {}, {}, {}
        g_mx, w2_mx, w1_mx, da_mx = {}, {}, {}, {}
        dx_banks, results, kept = {}, {}, []

        def placed(name, shape, dtype, at):
            return rings.tile(shape, dtype, name=f"{name}_at{at}", align_bytes=64 if at % 256 else 256, offset=at)

        def in_ring(name, index, shape, dtype):
            return placed(name, shape, dtype, ring_at(name, index))

        twos_at = (ring_at("g_scales", 0) - 64, ring_at("results", 0))
        twos = [placed("two", [P, 32], F32, at) for at in twos_at]
        for two in twos:
            nc.vector.memset(two[:, 0:1], 2.0)


        def listed(e, lo=0, hi=C):
            return offsets[:, (e * C + lo) // 16 : (e * C + hi) // 16]

        w1_places = [ring_at("w1_raw", place) for place in range(4)]
        w1_at = (
            (w1_places[0], w1_places[1]),
            (w1_places[3], w1_places[2]),
            (ring_at("last_tokens", 0) + 2048, ring_at("a_raw", 1)),
            (ring_at("a_raw", 3), ring_at("a_raw", 3) + 6144),
        )

        def a_at(e, h):
            moved = {(2, 1): ring_at("gathered", 0) + 1024, (3, 0): w1_places[3]}
            return moved.get((e, h), ring_at("a_raw", (0, 1, 3, 2)[(HALVES * e + h) % 4]))

        def batch_at(e, h):
            return a_at(e, 1) + (4096 if e == E - 1 else 0)

        def load_w2(e, halves=(0, 1)):
            cols = slice(halves[0] * P * J, (halves[-1] + 1) * P * J)
            tile = placed(f"w2_raw{len(halves)}", [P, J, len(halves) * P * J], F32, ring_at("w2_raw", e) + 8192 * halves[0])
            for h in halves:
                w2_raw[e, h] = tile[:, :, (h - halves[0]) * P * J : (h - halves[0] + 1) * P * J]
            nc.sync.dma_start(tile[:], w2[e].rearrange("(p j) i -> p j i", j=J)[:, :, cols])

        def load_a(e, h, lo=0, hi=C):
            at = a_at(e, h) + 16 * (C - hi)
            tile = placed(f"a_raw{hi - lo}", [P, J, hi - lo], F32, at)
            for first in range(lo, hi, GROUP):
                a_raw[e, h, first] = tile[:, :, first - lo : first - lo + GROUP]
            nc.sync.dma_start(tile[:], a_rows[h][:, :, e * C + lo : e * C + hi])

        def load_w1(e, h):
            w1_raw[e, h] = placed("w1_raw", [P, J, K], F32, w1_at[e][h])
            nc.sync.dma_start(w1_raw[e, h][:], w1[e].rearrange("(h p j) k -> h p j k", p=P, j=J)[h])

        def spread_gate(e):
            spread[e] = psum.tile([P, J, P], F32, name=f"spread{e}", offset=(5, 7, 4, 6)[e] * BANK)
            for c in range(J):
                nc.tensor.transpose(spread[e][:, c, :], gate_rows[:, e, c : c + 1].to_broadcast([P, P]), identity[:])

        def gate_to_sbuf(e, lo, at):
            gates[e] = placed(f"gate{lo}", [P, C - lo], F32, at)
            nc.scalar.activation(
                gates[e][:].rearrange("m (p c) -> m p c", c=J), spread[e][:, :, lo // J :].rearrange("m c p -> m p c"), COPY
            )

        def gather(e, t, on_scalar):
            if t == 0:
                gathered[e] = in_ring("gathered", e, [P, J, C], F32)
            if on_scalar:
                nc.scalar.activation(gathered[e][:, t, :], tokens[t][:].indirect(listed(e)), COPY)
            else:
                nc.vector.tensor_copy(gathered[e][:, t, :], tokens[t][:].indirect(listed(e)))

        def gate_on_vector(e, hi, at):
            g_mixed[e, 0] = placed(f"g_mixed{hi}", [P, hi, J], BF16, at)
            nc.vector.tensor_tensor(
                g_mixed[e, 0][:].rearrange("m (p c) t -> m p t c", c=J),
                gathered[e][:, :, 0:hi].rearrange("m t (p c) -> m p t c", c=J),
                spread[e][:, :, 0 : hi // J].rearrange("m c p -> m p c").unsqueeze(2).to_broadcast([P, hi // J, J, J]),
                MULT,
            )

        def gate_on_gpsimd(e, lo, hi, at):
            g_mixed[e, lo] = placed(f"g_mixed{hi - lo}", [P, hi - lo, J], BF16, at)
            held_from = C - gates[e].shape[1]
            nc.gpsimd.tensor_tensor(
                g_mixed[e, lo][:].rearrange("p (c i) t -> p c t i", i=2),
                gathered[e][:, :, lo:hi].rearrange("p t (c i) -> p c t i", i=2),
                gates[e][:, lo - held_from : hi - held_from]
                .rearrange("p (c i) -> p c i", i=2)
                .unsqueeze(2)
                .to_broadcast([P, (hi - lo) // 2, J, 2]),
                MULT,
            )

        def quantize(codes, scales, mixed, fmt):
            nc.vector.quantize_mx(out=codes.bitcast(fmt), scales=scales, in_=mixed)

        def quantize_g(e, lo, hi, at):
            codes = placed(f"g_codes{hi - lo}", [P, hi - lo], U32, ring_at("g_codes", 0) + 4 * (C * e + lo))
            scales = placed(f"g_scales{hi - lo}", [P, hi - lo], U8, at)
            quantize(codes[:], scales[:], g_mixed[e, lo][:].rearrange("p c t -> p (c t)"), E5M2)
            for first in range(lo, hi, GROUP):
                cols = slice(first - lo, first - lo + GROUP)
                g_mx[e, first // GROUP] = codes[:, cols], scales[:, cols]

        def mix_w2(e, h, planes_on_scalar):
            at = ring_at("w_mixed", 0) + (4096, 0)[h] if e or not h else ring_at("gathered", 0)
            w2_mixed[e, h] = placed("w2_mixed", [P, J, P, J], BF16, at)
            to = w2_mixed[e, h][:].rearrange("p t m j -> p m j t")
            source = w2_raw[e, h].rearrange("p j (m t) -> p m j t", t=J)
            if planes_on_scalar:
                t = slice(0, planes_on_scalar)
                nc.scalar.activation(to[:, :, :, t], source[:, :, :, t], COPY, scale=twos[e][:, 0:1] if e == h else 2.0)
            if planes_on_scalar < J:
                for t in range(planes_on_scalar, J, 2):
                    nc.vector.tensor_scalar(to[:, :, :, t : t + 2], source[:, :, :, t : t + 2], 2.0, None, MULT)

        def quantize_w2(e, h):
            codes = in_ring("w2_codes", HALVES * e + h, [P, P * J], U32)
            at = ring_at("gathered", 0) + 512 * h if e == 1 else ring_at("w2_scales", HALVES * e + h)
            scales = placed("w2_scales", [P, P * J], U8, at)
            w2_mx[e, h] = codes, scales
            quantize(codes[:], scales[:], w2_mixed[e, h][:].rearrange("p t m j -> p (t m j)"), E4M3)

        def mix_w1(e, h, on_scalar):
            at = (ring_at("w_mixed", 0) if e else ring_at("first_w1", 0)) + 3072 * h
            w1_mixed[e, h] = placed("w1_mixed", [P, K, J], BF16, ring_at("g_mixed", 1) if (e, h) == (1, 1) else at)
            to, source = w1_mixed[e, h][:], w1_raw[e, h][:]
            if on_scalar:
                nc.scalar.activation(
                    to.rearrange("p (c i) j -> p c j i", i=2), source.rearrange("p j (c i) -> p c j i", i=2), COPY
                )
            else:
                nc.gpsimd.tensor_scalar(to, source.rearrange("p j c -> p c j"), 1.0, 0.0, MULT, ADD)

        def quantize_w1(e, h):
            codes = in_ring("w1_codes", h, [P, K], U32)
            scales = placed("w1_scales", [P, K], U8, batch_at(e, h) + K * h)
            w1_mx[e, h] = codes, scales
            quantize(codes[:], scales[:], w1_mixed[e, h][:].rearrange("p c j -> p (c j)"), E4M3)

        def form_da(e, h, lo=0, hi=C):
            w2_codes, w2_scales = w2_mx[e, h]
            at = {(0, 0): ring_at("last_tokens", 0), (1, 0): ring_at("w_mixed", 0) + 3072}.get((e, h), ring_at("da_mixed", h))
            if lo:
                at = ring_at("w_mixed", 0) + 3072
            da_mixed[e, h, lo] = placed(f"da_mixed{hi - lo}", [P, hi - lo, J], BF16, at)
            for s in range(lo // GROUP, hi // GROUP):
                slots = slice(s * GROUP, (s + 1) * GROUP)
                b = ((HALVES * e + h) * (C // GROUP) + s) % DH_BANKS
                dh = psum.tile([P, J, GROUP], F32, name=f"dh{b}", offset=b * BANK)
                for t in range(J):
                    cols = slice(t * P, (t + 1) * P)
                    nc.tensor.matmul_mx(
                        out=dh[:, t, :],
                        lhsT=w2_codes[:, cols].bitcast(E4M3),
                        lhsT_scale=w2_scales[:, cols],
                        rhs=g_mx[e, s][0].bitcast(E5M2),
                        rhs_scale=g_mx[e, s][1],
                        start=True,
                        stop=True,
                    )
                nc.vector.scalar_tensor_tensor(
                    da_mixed[e, h, lo][:, s * GROUP - lo : (s + 1) * GROUP - lo, :],
                    a_raw[e, h, s * GROUP].rearrange("p t c -> p c t"),
                    0.0,
                    dh[:].rearrange("p t c -> p c t"),
                    MAX,
                    MULT,
                )

        def quantize_da(e, h, lo=0, hi=C):
            codes = placed(f"da_codes{hi - lo}", [P, hi - lo], U32, ring_at("da_codes", HALVES * e + h) + 4 * lo)
            at = batch_at(e, h) + 1024 + 512 * h + lo
            scales = placed(f"da_scales{hi - lo}", [P, hi - lo], U8, at)
            quantize(codes[:], scales[:], da_mixed[e, h, lo][:].rearrange("p c t -> p (c t)"), E5M2)
            for first in range(lo, hi, PIECE):
                da_mx[e, h, first] = codes, scales, lo

        def input_gradient(e, k, lo=0, hi=C):
            b = DH_BANKS + k if lo == 0 or k == K_TILES - 1 else k
            dx = psum.tile([P, hi - lo], F32, name=f"dx{b}_{lo}_{hi}", offset=b * BANK)
            cols = slice(k * P, (k + 1) * P)
            for h in range(HALVES):
                codes, scales, first = da_mx[e, h, lo]
                nc.tensor.matmul_mx(
                    out=dx[:],
                    lhsT=w1_mx[e, h][0][:, cols].bitcast(E4M3),
                    lhsT_scale=w1_mx[e, h][1][:, cols],
                    rhs=codes[:, lo - first : hi - first].bitcast(E5M2),
                    rhs_scale=scales[:, lo - first : hi - first],
                    start=(h == 0),
                    stop=(h == HALVES - 1),
                )
            for part in range(lo, hi, PIECE):
                dx_banks[e, k, part] = dx, lo

        def result_at(e, k, lo, hi):
            if k == K_TILES - 1 and e * C + lo >= KEPT_FROM:
                if not kept:
                    kept.append(in_ring("kept", 0, [P, T - KEPT_FROM], F32))
                return kept[0][:, e * C + lo - KEPT_FROM : e * C + hi - KEPT_FROM]
            if e not in results:
                results[e] = in_ring("results", e, [P, K_TILES, C], F32)
            return results[e][:, k, lo:hi]

        def copy_out(e, k, on_scalar, lo=0, hi=C):
            dx, first = dx_banks[e, k, lo]
            if on_scalar:
                nc.scalar.activation(result_at(e, k, lo, hi), dx[:, lo - first : hi - first], COPY)
            else:
                nc.vector.tensor_copy(result_at(e, k, lo, hi), dx[:, lo - first : hi - first])

        def scatter(e, k, lo, hi, on_scalar):
            to = windows[k][:].indirect(listed(e, lo, hi))
            if on_scalar:
                nc.scalar.activation(to, result_at(e, k, lo, hi), COPY)
            else:
                nc.vector.tensor_copy(to, result_at(e, k, lo, hi))

        def put_back(e):
            order = (1, 0, 2)
            for k in order:
                if e == E - 2 and k == K_TILES - 1:
                    copy_out(e, k, True, 0, PIECE)
                    copy_out(e, k, True, PIECE, C)
                else:
                    copy_out(e, k, True)
            for lo in range(0, C, PIECE):
                for k in order:
                    if not (k == K_TILES - 1 and e * C + lo >= KEPT_FROM):
                        scatter(e, k, lo, lo + PIECE, True)

        def store(k, queue):
            queue.dma_start(out[k * P : (k + 1) * P, :], windows[k][:])

        nc.scalar.dma_start(gate_rows[:], gate[0].rearrange("(e p c) -> p e c", p=P, c=J))
        nc.sync.dma_start(offsets[:], offs)
        for t in range(J):
            nc.sync.dma_start(tokens[t][:], dy_rows[:, t, :])
        load_w2(0)
        load_a(0, 0)
        load_w1(0, 0)
        load_a(0, 1)
        load_w1(0, 1)
        load_w2(1, (0,))
        load_w2(1, (1,))
        load_a(1, 0)
        load_w1(1, 0)
        load_a(1, 1)
        load_w1(1, 1)

        for e in (1, 0, 2, 3):
            spread_gate(e)
        gate_to_sbuf(1, 0, ring_at("gate", 0))
        for t in range(J):
            gather(0, t, False)
            gather(1, t, True)
            if t < J - 1:
                gather(2, t, False)
            gather(3, t, True)
        gather(2, J - 1, True)
        gate_on_vector(0, C, ring_at("g_mixed", 0))
        gate_on_gpsimd(1, 0, C, ring_at("g_mixed", 1))
        gate_on_vector(3, C, ring_at("g_mixed", 2))

        for e in range(E):
            first = e == 0
            mix_w2(e, 0, J if e < 2 else 0)
            mix_w2(e, 1, (J, J, 0, 0)[e])
            if first:
                gate_to_sbuf(2, 0, ring_at("gate", 1))
                quantize_g(0, 0, C, ring_at("g_scales", 0))
            else:
                put_back(e - 1)
            if e + 2 < E:
                load_w2(e + 2)
            quantize_w2(e, 0)
            if first:
                quantize_g(1, 0, C, ring_at("g_mixed", 0))
                quantize_g(3, 0, C, ring_at("g_mixed", 0) + 512)
            quantize_w2(e, 1)
            if first:
                gate_on_gpsimd(2, 0, C, ring_at("gathered", 0))
            mix_w1(e, 0, first)
            mix_w1(e, 1, first)
            form_da(e, 0)
            if e == E - 1:
                break
            form_da(e, 1)
            quantize_da(e, 0)
            quantize_w1(e, 0)
            quantize_w1(e, 1)
            quantize_da(e, 1)
            if first:
                quantize_g(2, 0, C, ring_at("last_tokens", 0))
            for k in (1, 0, 2):
                input_gradient(e, k)
            if e + 2 < E:
                load_a(e + 2, 0)
                load_w1(e + 2, 0)
                if first:
                    load_a(e + 2, 1)
                    load_w1(e + 2, 1)
                else:
                    load_w1(e + 2, 1)
                    load_a(e + 2, 1, 0, PIECE)
                    load_a(e + 2, 1, PIECE, C)

        e = E - 1
        form_da(e, 1, 0, PIECE)
        quantize_da(e, 0)
        quantize_w1(e, 0)
        quantize_w1(e, 1)
        quantize_da(e, 1, 0, PIECE)
        for k in (1, 0, 2):
            input_gradient(e, k, 0, PIECE)
        form_da(e, 1, PIECE, C)
        copy_out(e, 2, False, 0, PIECE)
        quantize_da(e, 1, PIECE, C)
        for k in (1, 0, 2):
            input_gradient(e, k, PIECE, C)
        copy_out(e, 1, True, 0, PIECE)
        copy_out(e, 0, True, 0, PIECE)
        scatter(e, 1, 0, PIECE, True)
        scatter(e, 0, 0, PIECE, True)
        copy_out(e, 1, False, PIECE, C)
        scatter(e, 1, PIECE, C, False)
        store(1, nc.sync)
        copy_out(e, 0, True, PIECE, C)
        copy_out(e, 2, False, PIECE, C)
        scatter(e, 0, PIECE, C, True)
        store(0, nc.scalar)
        scatter(E - 2, 2, PIECE, 2 * C, False)
        store(2, nc.sync)
